import numpy as np
import ml_dtypes


def mxq(x, axis, fmt="e4m3"):
    dtype, down = {"e4m3": (ml_dtypes.float8_e4m3fn, 7), "e5m2": (ml_dtypes.float8_e5m2, 14)}[fmt]
    v = np.moveaxis(np.asarray(x, np.float32).astype(ml_dtypes.bfloat16).astype(np.float64), axis, -1)
    blocks = v.reshape(v.shape[:-1] + (-1, 32))
    amax = np.abs(blocks).max(-1, keepdims=True)
    byte = np.maximum(np.where(amax > 0, np.frexp(amax)[1] - 1 + 127, 0) - down, 1)
    scale = np.exp2(byte - 127.0)
    codes = (blocks / scale).astype(np.float32).astype(dtype).astype(np.float64)
    return np.moveaxis((codes * scale).reshape(v.shape), -1, axis)


WIDE = False


def mx_kscale(k):
    if not WIDE:
        return np.ones(k)
    levels = np.array([30, -30])
    if k % 512:
        return np.exp2(np.random.permutation(np.resize(levels, k // 32))).repeat(32)
    a = np.empty((k // 512, 16))
    for p in range(k // 512):
        a[p, :8] = np.random.permutation(np.resize(levels, 8))
        for g in range(8):
            far = levels[np.abs(levels - a[p, g]) >= 10]
            a[p, g + 8] = far[np.random.randint(len(far))]
    return np.exp2(a.ravel()).repeat(32)


def f64(x):
    return np.asarray(x).astype(np.float64)


def striped(idx):
    return np.tile(idx.reshape(-1, 16).T, (8, 1)).astype(np.uint16)


def unstriped(offs):
    return offs[:16].T.reshape(-1).astype(np.int64)


E2M1 = np.array([0.0, 0.5, 1.0, 1.5, 2.0, 3.0, 4.0, 6.0, -0.0, -0.5, -1.0, -1.5, -2.0, -3.0, -4.0, -6.0])


def pack_weight(w, fmt):
    k, n = w.shape
    w = f64(np.asarray(w, np.float32).astype(ml_dtypes.bfloat16)).reshape(k // 32, 32, n)
    amax = np.abs(w).max(1)
    if fmt == "e4m3":
        byte = np.frexp(amax)[1] - 1 + 127 - 7
    else:
        mant, ex = np.frexp(amax / 6.0)
        byte = np.where(mant > 0.5, ex, ex - 1) + 127
    byte = np.clip(np.where(amax > 0, byte, 1), 1, 254)
    scaled = (w * np.exp2(127.0 - byte)[:, None, :]).reshape(k, n).astype(np.float32)
    by_word = np.ascontiguousarray(scaled.reshape(k // 512, 128, 4, n).transpose(0, 1, 3, 2))
    if fmt == "e4m3":
        words = by_word.astype(ml_dtypes.float8_e4m3fn).view(np.uint8)
    else:
        c = by_word.astype(ml_dtypes.float4_e2m1fn).view(np.uint8) & 0xF
        words = (c[..., 0::2] | (c[..., 1::2] << 4)).reshape(k // 512, 128, 2 * n)
    return np.ascontiguousarray(words), np.ascontiguousarray(byte.astype(np.uint8).reshape(k // 512, 16, n))


def unpack_weight(words, scales, fmt):
    g, _, n = scales.shape
    words = np.ascontiguousarray(words).reshape(g, 128, n, -1)
    if fmt == "e4m3":
        vals = words.view(ml_dtypes.float8_e4m3fn).astype(np.float64)
    else:
        nib = np.empty((g, 128, n, 4), np.uint8)
        nib[..., 0::2] = words & 0xF
        nib[..., 1::2] = words >> 4
        vals = E2M1[nib]
    vals = vals * np.repeat(np.exp2(scales.astype(np.float64) - 127.0), 8, axis=1)[..., None]
    return vals.transpose(0, 1, 3, 2).reshape(g * 512, n)


def d_silu(v):
    s = 1.0 / (1.0 + np.exp(-np.maximum(v, -700.0)))
    return s * (1.0 + v * (1.0 - s))


K, T, E, C, H, N = 768, 2048, 4, 512, 512, 512


def by_expert(wq, xq):
    return np.concatenate([wq[e].T @ xq[:, e * C:(e + 1) * C] for e in range(E)], axis=1)


def setup_inputs():
    n = np.random.standard_normal
    s = mx_kscale(N)[:, None]
    u = mx_kscale(H)
    w2 = [pack_weight(m, "e2m1") for m in n((E, N, H)) / np.sqrt(N) / s[None] * u[None, None, :]]
    w1 = [pack_weight(m, "e2m1") for m in n((E, H, K)) / np.sqrt(H) / u[None, :, None]]
    return {
        "dyT": (n((N, T)) * s).astype(np.float32),
        "a": n((H, E * C)).astype(np.float32),
        "w2_words": np.stack([m[0] for m in w2]),
        "w2_scales": np.stack([m[1] for m in w2]),
        "w1_words": np.stack([m[0] for m in w1]),
        "w1_scales": np.stack([m[1] for m in w1]),
        "gate": np.tile(np.random.uniform(0.2, 1.0, E * C), (N, 1)).astype(np.float32),
        "offs": striped(np.random.permutation(T)[:E * C]),
    }


def reference(dyT, a, w2_words, w2_scales, w1_words, w1_scales, gate, offs):
    idx = unstriped(offs)
    w2 = np.stack([unpack_weight(w2_words[e], w2_scales[e], "e2m1") for e in range(E)])
    w1 = np.stack([unpack_weight(w1_words[e], w1_scales[e], "e2m1") for e in range(E)])
    gq = mxq(f64(gate) * f64(dyT)[:, idx], 0, "e5m2")
    dh = by_expert(w2, gq)
    da = dh * d_silu(f64(a))
    dx = by_expert(w1, mxq(da, 0, "e5m2"))
    out = np.zeros((K, T))
    out[:, idx] = dx
    return out

@@ -1,0 +1,232 @@
+from contextlib import ExitStack
+
+import concourse.mybir as mybir
+
+K, T, E, C, H, N = 768, 2048, 4, 512, 512, 512
+P = 128
+PACK = 4
+K_TILES = K // P
+
+F32 = mybir.dt.float32
+BF16 = mybir.dt.bfloat16
+I32 = mybir.dt.int32
+U32 = mybir.dt.uint32
+U16 = mybir.dt.uint16
+U8 = mybir.dt.uint8
+FP4X4 = mybir.dt.float4_e2m1fn_x4
+FP8X4 = mybir.dt.float8_e5m2_x4
+ACT = mybir.ActivationFunctionType
+ALU = mybir.AluOpType
+
+FLOPS = 2 * E * C * (N * H + H * K)
+BYTES = 4 * (N * T + H * E * C + E * C + K * T) + 2 * E * C + E * (N * H + H * K) * 17 // 32
+
+
+def tile_moe_bdx_mlp_silu_kernel(tc, dyT, a, w2_words, w2_scales, w1_words, w1_scales, gate, offs, out):
+    nc = tc.nc
+    with ExitStack() as ctx:
+        keep = ctx.enter_context(tc.tile_pool(name="keep", bufs=1))
+        ring = ctx.enter_context(tc.tile_pool(name="ring", bufs=2))
+        psum_h = ctx.enter_context(tc.psum_pool(name="psum_h", bufs=4))
+        psum_x = ctx.enter_context(tc.psum_pool(name="psum_x", bufs=4))
+
+        offsets = keep.tile([P, E * C // 16], U16, name="offsets")
+        dy = [keep.tile([P, T], F32, name=f"dy{t}", tag=f"columns{t}") for t in range(PACK)]
+        pre = [keep.tile([P, PACK, C], F32, name=f"pre{e}") for e in range(E)]
+        w2_raw = keep.tile([P, E, 2 * H], U8, name="w2_raw", align_bytes=64)
+        w2 = keep.tile([P, E, 2 * H], U8, name="w2", align_bytes=64)
+        w2_sraw = keep.tile([P, E, H], U8, name="w2_sraw", align_bytes=64)
+        w2_s = keep.tile([P, E, H], U8, name="w2_s", align_bytes=64)
+        w1 = keep.tile([P, E, 2 * K], U8, name="w1", align_bytes=64)
+        w1_s = keep.tile([P, E, K], U8, name="w1_s", align_bytes=64)
+
+        def in_turn(i, shape, dtype, name):
+            return ring.tile(shape, dtype, name=name, tag=f"turn{i % 2}", align_bytes=64, bufs=1)
+
+        gates = [keep.tile([P, C], F32, name=f"gates{e}") for e in range(E - 1)]
+        gates.append(in_turn(0, [P, C], F32, "gates_last"))
+
+        nc.vector.memset(w2_sraw[:].bitcast(I32), 0)
+        nc.vector.memset(w1_s[:].bitcast(I32), 0)
+        warm = keep.tile([P, 8], F32, name="warm")
+        nc.vector.memset(warm[:], 0.0)
+        nc.scalar.activation(warm[:], warm[:], ACT.Sigmoid)
+
+        dy_rows = dyT.rearrange("(p t) j -> p t j", t=PACK)
+        a_rows = a.rearrange("(p t) j -> p t j", t=PACK)
+
+        def load_scales(planes, scales):
+            for q in range(4):
+                nc.sync.dma_start(
+                    out=planes[32 * q : 32 * q + 4].bitcast(I32),
+                    in_=scales[:, 0, 4 * q : 4 * q + 4, :].rearrange("e f n -> f e n").bitcast(I32),
+                )
+
+        def load_w2(e):
+            nc.sync.dma_start(
+                out=w2_raw[:, e : e + 2].bitcast(I32), in_=w2_words[e : e + 2].rearrange("e o p n -> p (e o) n").bitcast(I32)
+            )
+
+        def load_gates(e):
+            nc.sync.dma_start(out=gates[e][:], in_=gate[0:P, e * C : (e + 1) * C])
+
+        def load_dy(t):
+            nc.sync.dma_start(out=dy[t][:], in_=dy_rows[:, t, :])
+
+        def load_pre(e):
+            nc.sync.dma_start(out=pre[e][:], in_=a_rows[:, :, e * C : (e + 1) * C])
+
+        nc.sync.dma_start(out=offsets[:], in_=offs)
+        load_scales(w2_sraw, w2_scales)
+        load_w2(0)
+        for i in range(3):
+            load_gates(i)
+            load_dy(i)
+        load_pre(0)
+        load_dy(3)
+        load_w2(2)
+        load_gates(3)
+        load_pre(1)
+        load_scales(w1_s, w1_scales)
+        nc.sync.dma_start(out=w1[:].bitcast(I32), in_=w1_words.rearrange("e o p n -> p (e o) n").bitcast(I32))
+        load_pre(2)
+        load_pre(3)
+
+        nc.vector.tensor_copy(
+            out=w2_s[:].rearrange("p e (t m) -> p e t m", t=PACK),
+            in_=w2_sraw[:].rearrange("p e (m t) -> p e t m", t=PACK),
+        )
+        for e in (0, 2):
+            nc.vector.tensor_copy(
+                out=w2[:, e : e + 2].bitcast(U16).rearrange("p e (t m) -> p e t m", t=PACK),
+                in_=w2_raw[:, e : e + 2].bitcast(U16).rearrange("p e (m t) -> p e t m", t=PACK),
+            )
+
+        def interleave(grouped, planes):
+            nc.scalar.copy(
+                out=grouped[:].rearrange("p (c i) t -> p c t i", i=4),
+                in_=planes[:].rearrange("p t (c i) -> p c t i", i=4),
+            )
+
+        def slots(e):
+            return offsets[:, e * C // 16 : (e + 1) * C // 16]
+
+        def derivative(e):
+            other = ring.tile([P, PACK, C], F32, name="other")
+            if e % 2 == 0:
+                for t in range(0, PACK, 2):
+                    nc.scalar.activation(other[:, t : t + 2, :], pre[e][:, t : t + 2, :], ACT.Sigmoid)
+                for t in range(0, PACK, 2):
+                    nc.scalar.activation(pre[e][:, t : t + 2, :], pre[e][:, t : t + 2, :], ACT.Silu, scale=-1.0)
+                z, s = pre[e], other
+            else:
+                nc.scalar.activation(other[:], pre[e][:], ACT.Silu, scale=-1.0)
+                nc.scalar.activation(pre[e][:], pre[e][:], ACT.Sigmoid)
+                z, s = other, pre[e]
+            if e == 0:
+                nc.vector.scalar_tensor_tensor(out=other[:], in0=z[:], scalar=1.0, in1=s[:], op0=ALU.subtract, op1=ALU.mult)
+                return other[:]
+            nc.scalar.activation(z[:], z[:], ACT.Identity, bias=-1.0)
+            return z, s
+
+        def staging(e):
+            return in_turn(e, [P, PACK + 1, C], F32, "staging")
+
+        def product(stage, z, s):
+            d = stage[:, 0:PACK, :]
+            for t in range(PACK):
+                nc.gpsimd.tensor_tensor(d[:, t, :], z[:, t, :], s[:, t, :], ALU.mult)
+            return d
+
+        def quantize(grouped, kind, depth):
+            codes = ring.tile([P, C], U32, name=f"codes_{kind}", align_bytes=64, bufs=depth)
+            scales = ring.tile([P, C], U8, name=f"scales_{kind}", align_bytes=64, bufs=depth)
+            nc.vector.quantize_mx(out=codes[:].bitcast(FP8X4), scales=scales[:], in_=grouped[:].rearrange("p c t -> p (c t)"))
+            return codes, scales
+
+        def gather(e):
+            g = ring.tile([P, PACK, C], F32, name="g", bufs=3)
+            for t in range(PACK):
+                nc.vector.tensor_tensor(g[:, t, :], dy[t][:].indirect(slots(e)), gates[e][:], ALU.mult)
+            g_grouped = ring.tile([P, C, PACK], BF16, name="g_grouped", align_bytes=64)
+            interleave(g_grouped, g)
+            return quantize(g_grouped, "g", E)
+
+        def multiply(e, minus_d, g_codes, g_scales):
+            da = ring.tile([P, PACK, C], BF16, name="da", align_bytes=64, bufs=1)
+            if e > 0:
+                dh_copy = ring.tile([P, PACK, C], F32, name="dh_copy", bufs=1)
+            for t in range(PACK):
+                dh = psum_h.tile([P, C], F32, name="dh")
+                nc.tensor.matmul_mx(
+                    out=dh[:],
+                    lhsT=w2[:, e, 2 * P * t : 2 * P * (t + 1)].bitcast(FP4X4),
+                    lhsT_scale=w2_s[:, e, P * t : P * (t + 1)],
+                    rhs=g_codes[:].bitcast(FP8X4),
+                    rhs_scale=g_scales[:],
+                    start=True,
+                    stop=True,
+                )
+                if e == 0:
+                    nc.vector.scalar_tensor_tensor(
+                        out=da[:, t, :], in0=dh[:], scalar=-1.0, in1=minus_d[:, t, :], op0=ALU.mult, op1=ALU.mult
+                    )
+                else:
+                    nc.scalar.activation(dh_copy[:, t, :], dh[:], ACT.Copy, scale=-1.0)
+            if e > 0:
+                for t in range(0, PACK, 2):
+                    nc.gpsimd.tensor_tensor(da[:, t : t + 2, :], dh_copy[:, t : t + 2, :], minus_d[:, t : t + 2, :], ALU.mult)
+            da_grouped = in_turn(max(e, 1), [P, C, PACK], BF16, "da_grouped")
+            interleave(da_grouped, da)
+            da_codes, da_scales = quantize(da_grouped, "da", 2)
+            return da_codes, da_scales
+
+        def project(e, m, da_codes, da_scales, result):
+            dx = psum_x.tile([P, C], F32, name="dx")
+            nc.tensor.matmul_mx(
+                out=dx[:],
+                lhsT=w1[:, e, 2 * P * m : 2 * P * (m + 1)].bitcast(FP4X4),
+                lhsT_scale=w1_s[:, e, P * m : P * (m + 1)],
+                rhs=da_codes[:].bitcast(FP8X4),
+                rhs_scale=da_scales[:],
+                start=True,
+                stop=True,
+            )
+            nc.scalar.copy(out=result, in_=dx[:])
+
+        def project_first(e, operand):
+            results = []
+            for m in range(K_TILES - 1):
+                result = ring.tile([P, C], F32, name="result", bufs=6)
+                project(e, m, *operand, result[:])
+                results.append(result[:])
+            return results
+
+        def project_last(e, operand, stage):
+            project(e, K_TILES - 1, *operand, stage[:, PACK, :])
+            return [stage[:, PACK, :]]
+
+        def put_back(e, results):
+            for m in range(K_TILES):
+                nc.vector.tensor_copy(window[m][:].indirect(slots(e)), results[m])
+                if e == E - 1:
+                    nc.sync.dma_start(out=out[m * P : (m + 1) * P, :], in_=window[m][:])
+
+        codes = [gather(0)]
+        operand = multiply(0, derivative(0), *codes[0])
+        first = project_first(0, operand)
+        factors = derivative(1)
+        codes += [gather(e) for e in range(1, E)]
+        window = [keep.tile([P, T], F32, name=f"window{m}", tag=f"columns{m}") for m in range(K_TILES)]
+        d = product(staging(0), *factors)
+        for e in range(1, E):
+            following = multiply(e, d, *codes[e])
+            stage = staging(e)
+            results = first + project_last(e - 1, operand, stage)
+            if e + 1 < E:
+                d = product(stage, *derivative(e + 1))
+            put_back(e - 1, results)
+            operand = following
+            first = project_first(e, operand)
+        stage = staging(E)
+        put_back(E - 1, first + project_last(E - 1, operand, stage))

@@ -39,18 +39,17 @@ def tile_moe_bdx_mlp_silu_kernel(tc, dyT, a, w2_words, w2_scales, w1_words, w1_s
         w2_s = keep.tile([P, E, H], U8, name="w2_s", align_bytes=64)
         w1 = keep.tile([P, E, 2 * K], U8, name="w1", align_bytes=64)
         w1_s = keep.tile([P, E, K], U8, name="w1_s", align_bytes=64)
-
-        def in_turn(i, shape, dtype, name):
-            return ring.tile(shape, dtype, name=name, tag=f"turn{i % 2}", align_bytes=64, bufs=1)
-
-        gates = [keep.tile([P, C], F32, name=f"gates{e}") for e in range(E - 1)]
-        gates.append(in_turn(0, [P, C], F32, "gates_last"))
+        shared = keep.tile([P, PACK * 2 * C], F32, name="shared", align_bytes=64)
+        gates_first = keep.tile([P, C], F32, name="gates_first")
+        gates_middle = keep.tile([P, 2 * C], F32, name="gates_middle")
+        gates_last = keep.tile([P, C], F32, name="gates_last", tag="held")
+        gates = [gates_first[:], gates_middle[:, 0:C], gates_middle[:, C : 2 * C], gates_last[:]]
 
         nc.vector.memset(w2_sraw[:].bitcast(I32), 0)
         nc.vector.memset(w1_s[:].bitcast(I32), 0)
         warm = keep.tile([P, 8], F32, name="warm")
         nc.vector.memset(warm[:], 0.0)
-        nc.scalar.activation(warm[:], warm[:], ACT.Sigmoid)
+        nc.scalar.activation(warm[:], warm[:], ACT.Silu)
 
         dy_rows = dyT.rearrange("(p t) j -> p t j", t=PACK)
         a_rows = a.rearrange("(p t) j -> p t j", t=PACK)
@@ -62,13 +61,8 @@ def tile_moe_bdx_mlp_silu_kernel(tc, dyT, a, w2_words, w2_scales, w1_words, w1_s
                     in_=scales[:, 0, 4 * q : 4 * q + 4, :].rearrange("e f n -> f e n").bitcast(I32),
                 )
 
-        def load_w2(e):
-            nc.sync.dma_start(
-                out=w2_raw[:, e : e + 2].bitcast(I32), in_=w2_words[e : e + 2].rearrange("e o p n -> p (e o) n").bitcast(I32)
-            )
-
-        def load_gates(e):
-            nc.sync.dma_start(out=gates[e][:], in_=gate[0:P, e * C : (e + 1) * C])
+        def load_words(tile, words):
+            nc.sync.dma_start(out=tile[:].bitcast(I32), in_=words.rearrange("e o p n -> p (e o) n").bitcast(I32))
 
         def load_dy(t):
             nc.sync.dma_start(out=dy[t][:], in_=dy_rows[:, t, :])
@@ -77,156 +71,182 @@ def tile_moe_bdx_mlp_silu_kernel(tc, dyT, a, w2_words, w2_scales, w1_words, w1_s
             nc.sync.dma_start(out=pre[e][:], in_=a_rows[:, :, e * C : (e + 1) * C])
 
         nc.sync.dma_start(out=offsets[:], in_=offs)
-        load_scales(w2_sraw, w2_scales)
-        load_w2(0)
-        for i in range(3):
-            load_gates(i)
-            load_dy(i)
+        nc.sync.dma_start(out=gates_first[:], in_=gate[0:P, 0:C])
+        load_dy(0)
+        nc.sync.dma_start(out=gates_middle[:], in_=gate[0:P, C : 3 * C])
+        load_dy(1)
+        load_dy(2)
         load_pre(0)
         load_dy(3)
-        load_w2(2)
-        load_gates(3)
+        load_scales(w2_sraw, w2_scales)
+        load_words(w2_raw, w2_words)
         load_pre(1)
+        nc.sync.dma_start(out=gates_last[:], in_=gate[0:P, 3 * C : 4 * C])
         load_scales(w1_s, w1_scales)
-        nc.sync.dma_start(out=w1[:].bitcast(I32), in_=w1_words.rearrange("e o p n -> p (e o) n").bitcast(I32))
+        load_words(w1, w1_words)
         load_pre(2)
         load_pre(3)
 
-        nc.vector.tensor_copy(
-            out=w2_s[:].rearrange("p e (t m) -> p e t m", t=PACK),
-            in_=w2_sraw[:].rearrange("p e (m t) -> p e t m", t=PACK),
-        )
-        for e in (0, 2):
+        def permute(experts):
             nc.vector.tensor_copy(
-                out=w2[:, e : e + 2].bitcast(U16).rearrange("p e (t m) -> p e t m", t=PACK),
-                in_=w2_raw[:, e : e + 2].bitcast(U16).rearrange("p e (m t) -> p e t m", t=PACK),
+                out=w2_s[:, experts].rearrange("p e (t m) -> p e t m", t=PACK),
+                in_=w2_sraw[:, experts].rearrange("p e (m t) -> p e t m", t=PACK),
+            )
+            nc.vector.tensor_copy(
+                out=w2[:, experts].bitcast(U16).rearrange("p e (t m) -> p e t m", t=PACK),
+                in_=w2_raw[:, experts].bitcast(U16).rearrange("p e (m t) -> p e t m", t=PACK),
             )
 
         def interleave(grouped, planes):
             nc.scalar.copy(
-                out=grouped[:].rearrange("p (c i) t -> p c t i", i=4),
-                in_=planes[:].rearrange("p t (c i) -> p c t i", i=4),
+                out=grouped.rearrange("p (c i t) -> p c t i", i=4, t=PACK),
+                in_=planes.rearrange("p t (c i) -> p c t i", i=4),
             )
 
         def slots(e):
             return offsets[:, e * C // 16 : (e + 1) * C // 16]
 
-        def derivative(e):
-            other = ring.tile([P, PACK, C], F32, name="other")
-            if e % 2 == 0:
-                for t in range(0, PACK, 2):
-                    nc.scalar.activation(other[:, t : t + 2, :], pre[e][:, t : t + 2, :], ACT.Sigmoid)
-                for t in range(0, PACK, 2):
-                    nc.scalar.activation(pre[e][:, t : t + 2, :], pre[e][:, t : t + 2, :], ACT.Silu, scale=-1.0)
-                z, s = pre[e], other
-            else:
-                nc.scalar.activation(other[:], pre[e][:], ACT.Silu, scale=-1.0)
-                nc.scalar.activation(pre[e][:], pre[e][:], ACT.Sigmoid)
-                z, s = other, pre[e]
-            if e == 0:
-                nc.vector.scalar_tensor_tensor(out=other[:], in0=z[:], scalar=1.0, in1=s[:], op0=ALU.subtract, op1=ALU.mult)
-                return other[:]
-            nc.scalar.activation(z[:], z[:], ACT.Identity, bias=-1.0)
-            return z, s
-
-        def staging(e):
-            return in_turn(e, [P, PACK + 1, C], F32, "staging")
-
-        def product(stage, z, s):
-            d = stage[:, 0:PACK, :]
-            for t in range(PACK):
-                nc.gpsimd.tensor_tensor(d[:, t, :], z[:, t, :], s[:, t, :], ALU.mult)
-            return d
-
-        def quantize(grouped, kind, depth):
-            codes = ring.tile([P, C], U32, name=f"codes_{kind}", align_bytes=64, bufs=depth)
-            scales = ring.tile([P, C], U8, name=f"scales_{kind}", align_bytes=64, bufs=depth)
-            nc.vector.quantize_mx(out=codes[:].bitcast(FP8X4), scales=scales[:], in_=grouped[:].rearrange("p c t -> p (c t)"))
+        def quantize(grouped, kind):
+            codes = ring.tile([P, C], U32, name=f"codes_{kind}", align_bytes=64)
+            scales = ring.tile([P, C], U8, name=f"scales_{kind}", align_bytes=64)
+            nc.vector.quantize_mx(out=codes[:].bitcast(FP8X4), scales=scales[:], in_=grouped)
             return codes, scales
 
-        def gather(e):
-            g = ring.tile([P, PACK, C], F32, name="g", bufs=3)
-            for t in range(PACK):
-                nc.vector.tensor_tensor(g[:, t, :], dy[t][:].indirect(slots(e)), gates[e][:], ALU.mult)
-            g_grouped = ring.tile([P, C, PACK], BF16, name="g_grouped", align_bytes=64)
-            interleave(g_grouped, g)
-            return quantize(g_grouped, "g", E)
+        def gather(e, t, plane):
+            nc.vector.tensor_tensor(plane, dy[t][:].indirect(slots(e)), gates[e], ALU.mult)
 
-        def multiply(e, minus_d, g_codes, g_scales):
-            da = ring.tile([P, PACK, C], BF16, name="da", align_bytes=64, bufs=1)
-            if e > 0:
-                dh_copy = ring.tile([P, PACK, C], F32, name="dh_copy", bufs=1)
-            for t in range(PACK):
-                dh = psum_h.tile([P, C], F32, name="dh")
-                nc.tensor.matmul_mx(
-                    out=dh[:],
-                    lhsT=w2[:, e, 2 * P * t : 2 * P * (t + 1)].bitcast(FP4X4),
-                    lhsT_scale=w2_s[:, e, P * t : P * (t + 1)],
-                    rhs=g_codes[:].bitcast(FP8X4),
-                    rhs_scale=g_scales[:],
-                    start=True,
-                    stop=True,
-                )
-                if e == 0:
-                    nc.vector.scalar_tensor_tensor(
-                        out=da[:, t, :], in0=dh[:], scalar=-1.0, in1=minus_d[:, t, :], op0=ALU.mult, op1=ALU.mult
-                    )
+        def group(planes, kind):
+            grouped = ring.tile([P, C * PACK], BF16, name=f"grouped_{kind}", align_bytes=64, bufs=1)
+            interleave(grouped[:], planes)
+            return quantize(grouped[:], kind)
+
+        second = {}
+
+        def function(e, nth):
+            if nth == 0:
+                second[e] = ring.tile([P, PACK, C], F32, name="second")
+            target = second[e] if nth == 0 else pre[e]
+            for t in range(0, PACK, 2):
+                if (e + nth) % 2 == 0:
+                    nc.scalar.activation(target[:, t : t + 2, :], pre[e][:, t : t + 2, :], ACT.Silu, scale=-1.0)
                 else:
-                    nc.scalar.activation(dh_copy[:, t, :], dh[:], ACT.Copy, scale=-1.0)
-            if e > 0:
-                for t in range(0, PACK, 2):
-                    nc.gpsimd.tensor_tensor(da[:, t : t + 2, :], dh_copy[:, t : t + 2, :], minus_d[:, t : t + 2, :], ALU.mult)
-            da_grouped = in_turn(max(e, 1), [P, C, PACK], BF16, "da_grouped")
-            interleave(da_grouped, da)
-            da_codes, da_scales = quantize(da_grouped, "da", 2)
-            return da_codes, da_scales
+                    nc.scalar.activation(target[:, t : t + 2, :], pre[e][:, t : t + 2, :], ACT.Sigmoid)
 
-        def project(e, m, da_codes, da_scales, result):
+        def silu_and_sigmoid(e):
+            return (second[e], pre[e]) if e % 2 == 0 else (pre[e], second[e])
+
+        def first_product(e, t, operand):
+            dh = psum_h.tile([P, C], F32, name="dh")
+            nc.tensor.matmul_mx(
+                out=dh[:],
+                lhsT=w2[:, e, 2 * P * t : 2 * P * (t + 1)].bitcast(FP4X4),
+                lhsT_scale=w2_s[:, e, P * t : P * (t + 1)],
+                rhs=operand[0][:].bitcast(FP8X4),
+                rhs_scale=operand[1][:],
+                start=True,
+                stop=True,
+            )
+            return dh
+
+        def hidden_gradient(e, operand):
+            dh_copy = keep.tile([P, PACK, C], F32, name=f"dh_copy{e}", tag="held" if e > 1 else "g0")
+            for t in range(PACK):
+                nc.scalar.copy(out=dh_copy[:, t, :], in_=first_product(e, t, operand)[:])
+            return dh_copy
+
+        def through_silu(e, dh_copy):
+            z, s = silu_and_sigmoid(e)
+            u = keep.tile([P, PACK, C], F32, name="u", tag="held") if e == 1 else dh_copy
+            da = ring.tile([P, PACK, C], BF16, name="da", tag="da", align_bytes=64, bufs=1)
+            for t in range(PACK):
+                nc.gpsimd.tensor_tensor(u[:, t, :], dh_copy[:, t, :], s[:, t, :], ALU.mult)
+            for t in range(PACK):
+                nc.gpsimd.tensor_scalar(s[:, t, :], z[:, t, :], -1.0, 1.0, ALU.mult, ALU.add)
+            for t in range(PACK):
+                nc.gpsimd.tensor_tensor(da[:, t, :], u[:, t, :], s[:, t, :], ALU.mult)
+            return da
+
+        def project(e, m, operand):
             dx = psum_x.tile([P, C], F32, name="dx")
             nc.tensor.matmul_mx(
                 out=dx[:],
                 lhsT=w1[:, e, 2 * P * m : 2 * P * (m + 1)].bitcast(FP4X4),
                 lhsT_scale=w1_s[:, e, P * m : P * (m + 1)],
-                rhs=da_codes[:].bitcast(FP8X4),
-                rhs_scale=da_scales[:],
+                rhs=operand[0][:].bitcast(FP8X4),
+                rhs_scale=operand[1][:],
                 start=True,
                 stop=True,
             )
-            nc.scalar.copy(out=result, in_=dx[:])
+            if m + 1 < K_TILES:
+                result = ring.tile([P, C], F32, name="result", bufs=K_TILES - 1)
+            else:
+                result = ring.tile([P, C], F32, name="result_last", tag="da", align_bytes=64, bufs=1)
+            nc.scalar.copy(out=result[:], in_=dx[:])
+            nc.vector.tensor_copy(window[m][:].indirect(slots(e)), result[:])
+            if e == E - 1:
+                nc.sync.dma_start(out=out[m * P : (m + 1) * P, :], in_=window[m][:])
 
-        def project_first(e, operand):
-            results = []
-            for m in range(K_TILES - 1):
-                result = ring.tile([P, C], F32, name="result", bufs=6)
-                project(e, m, *operand, result[:])
-                results.append(result[:])
-            return results
+        function(0, 0)
+        function(0, 1)
+        g = [keep.tile([P, PACK, C], F32, name=f"g{e}", tag=f"g{e}") for e in range(E - 1)]
+        for t in range(PACK):
+            for e in range(E - 1):
+                gather(e, t, g[e][:, t, :])
+        g_planes = [tile[:] for tile in g] + [shared[:].rearrange("p (t x) -> p t x", t=PACK)[:, :, 0:C]]
+        permute(slice(0, E))
 
-        def project_last(e, operand, stage):
-            project(e, K_TILES - 1, *operand, stage[:, PACK, :])
-            return [stage[:, PACK, :]]
+        def quarter(t):
+            return shared[:, 2 * C * t : 2 * C * (t + 1)]
 
-        def put_back(e, results):
-            for m in range(K_TILES):
-                nc.vector.tensor_copy(window[m][:].indirect(slots(e)), results[m])
-                if e == E - 1:
-                    nc.sync.dma_start(out=out[m * P : (m + 1) * P, :], in_=window[m][:])
+        minus_d = shared[:, 2 * C : 6 * C]
+        z, s = silu_and_sigmoid(0)
+        nc.vector.scalar_tensor_tensor(
+            out=minus_d,
+            in0=z[:].rearrange("p t c -> p (t c)"),
+            scalar=1.0,
+            in1=s[:].rearrange("p t c -> p (t c)"),
+            op0=ALU.subtract,
+            op1=ALU.mult,
+        )
+        interleave(quarter(0).bitcast(BF16), g_planes[0])
+        g_operand = quantize(quarter(0).bitcast(BF16), "g")
+        gather(E - 1, 0, quarter(0)[:, 0:C])
+        da = ring.tile([P, PACK, C], BF16, name="da", tag="da", align_bytes=64, bufs=1)
+        for t in range(PACK):
+            nc.vector.scalar_tensor_tensor(
+                out=da[:, t, :],
+                in0=first_product(0, t, g_operand)[:],
+                scalar=-1.0,
+                in1=minus_d[:, t * C : (t + 1) * C],
+                op0=ALU.mult,
+                op1=ALU.mult,
+            )
+        function(1, 0)
+        g_operand = group(g_planes[1], "g")
+        gather(E - 1, 1, quarter(1)[:, 0:C])
+        gather(E - 1, 2, quarter(2)[:, 0:C])
+        interleave(quarter(3).bitcast(BF16), da[:])
+        da_operand = quantize(quarter(3).bitcast(BF16), "da")
+        gather(E - 1, 3, quarter(3)[:, 0:C])
 
-        codes = [gather(0)]
-        operand = multiply(0, derivative(0), *codes[0])
-        first = project_first(0, operand)
-        factors = derivative(1)
-        codes += [gather(e) for e in range(1, E)]
         window = [keep.tile([P, T], F32, name=f"window{m}", tag=f"columns{m}") for m in range(K_TILES)]
-        d = product(staging(0), *factors)
-        for e in range(1, E):
-            following = multiply(e, d, *codes[e])
-            stage = staging(e)
-            results = first + project_last(e - 1, operand, stage)
+        for e in range(E):
+            project(e, 0, da_operand)
             if e + 1 < E:
-                d = product(stage, *derivative(e + 1))
-            put_back(e - 1, results)
-            operand = following
-            first = project_first(e, operand)
-        stage = staging(E)
-        put_back(E - 1, first + project_last(E - 1, operand, stage))
+                dh_copy = hidden_gradient(e + 1, g_operand)
+            project(e, 1, da_operand)
+            if e == 0:
+                function(1, 1)
+            for m in range(2, K_TILES - 1):
+                project(e, m, da_operand)
+            if e + 1 < E:
+                da = through_silu(e + 1, dh_copy)
+            if e + 2 < E:
+                function(e + 2, 0)
+                g_operand = group(g_planes[e + 2], "g")
+            if e + 1 < E:
+                following = group(da[:], "da")
+            project(e, K_TILES - 1, da_operand)
+            if e + 2 < E:
+                function(e + 2, 1)
+            da_operand = following

@@ -43,6 +43,7 @@ def tile_moe_bdx_mlp_silu_kernel(tc, dyT, a, w2_words, w2_scales, w1_words, w1_s
         gates_first = keep.tile([P, C], F32, name="gates_first")
         gates_middle = keep.tile([P, 2 * C], F32, name="gates_middle")
         gates_last = keep.tile([P, C], F32, name="gates_last", tag="held")
+        gates_kept = keep.tile([P, C], F32, name="gates_kept")
         gates = [gates_first[:], gates_middle[:, 0:C], gates_middle[:, C : 2 * C], gates_last[:]]
 
         nc.vector.memset(w2_sraw[:].bitcast(I32), 0)
@@ -71,12 +72,12 @@ def tile_moe_bdx_mlp_silu_kernel(tc, dyT, a, w2_words, w2_scales, w1_words, w1_s
             nc.sync.dma_start(out=pre[e][:], in_=a_rows[:, :, e * C : (e + 1) * C])
 
         nc.sync.dma_start(out=offsets[:], in_=offs)
-        nc.sync.dma_start(out=gates_first[:], in_=gate[0:P, 0:C])
         load_dy(0)
+        nc.sync.dma_start(out=gates_first[:], in_=gate[0:P, 0:C])
         nc.sync.dma_start(out=gates_middle[:], in_=gate[0:P, C : 3 * C])
         load_dy(1)
-        load_dy(2)
         load_pre(0)
+        load_dy(2)
         load_dy(3)
         load_scales(w2_sraw, w2_scales)
         load_words(w2_raw, w2_words)
@@ -85,6 +86,7 @@ def tile_moe_bdx_mlp_silu_kernel(tc, dyT, a, w2_words, w2_scales, w1_words, w1_s
         load_scales(w1_s, w1_scales)
         load_words(w1, w1_words)
         load_pre(2)
+        nc.sync.dma_start(out=gates_kept[:], in_=gate[P : 2 * P, 3 * C : 4 * C])
         load_pre(3)
 
         def permute(experts):
@@ -122,15 +124,20 @@ def tile_moe_bdx_mlp_silu_kernel(tc, dyT, a, w2_words, w2_scales, w1_words, w1_s
 
         second = {}
 
-        def function(e, nth):
-            if nth == 0:
+        def function(e, nth, halves=(0, 2)):
+            if e not in second:
                 second[e] = ring.tile([P, PACK, C], F32, name="second")
             target = second[e] if nth == 0 else pre[e]
-            for t in range(0, PACK, 2):
+            for t in halves:
                 if (e + nth) % 2 == 0:
                     nc.scalar.activation(target[:, t : t + 2, :], pre[e][:, t : t + 2, :], ACT.Silu, scale=-1.0)
                 else:
                     nc.scalar.activation(target[:, t : t + 2, :], pre[e][:, t : t + 2, :], ACT.Sigmoid)
+
+        def one_minus(e):
+            z = silu_and_sigmoid(e)[0]
+            for t in range(0, PACK, 2):
+                nc.scalar.activation(z[:, t : t + 2, :], z[:, t : t + 2, :], ACT.Identity, bias=1.0, scale=-1.0)
 
         def silu_and_sigmoid(e):
             return (second[e], pre[e]) if e % 2 == 0 else (pre[e], second[e])
@@ -155,15 +162,18 @@ def tile_moe_bdx_mlp_silu_kernel(tc, dyT, a, w2_words, w2_scales, w1_words, w1_s
             return dh_copy
 
         def through_silu(e, dh_copy):
-            z, s = silu_and_sigmoid(e)
-            u = keep.tile([P, PACK, C], F32, name="u", tag="held") if e == 1 else dh_copy
             da = ring.tile([P, PACK, C], BF16, name="da", tag="da", align_bytes=64, bufs=1)
-            for t in range(PACK):
-                nc.gpsimd.tensor_tensor(u[:, t, :], dh_copy[:, t, :], s[:, t, :], ALU.mult)
-            for t in range(PACK):
-                nc.gpsimd.tensor_scalar(s[:, t, :], z[:, t, :], -1.0, 1.0, ALU.mult, ALU.add)
-            for t in range(PACK):
-                nc.gpsimd.tensor_tensor(da[:, t, :], u[:, t, :], s[:, t, :], ALU.mult)
+            early, late = second[e], pre[e]
+            parts = [(slice(0, 2), dh_copy[:, 0:2, :]), (slice(2, 4), dh_copy[:, 2:4, :])]
+            if e == 1:
+                u = keep.tile([P, PACK - 1, C], F32, name="u", tag="held")
+                parts = [(slice(0, 2), u[:, 0:2, :]), (slice(2, 3), g_planes[E - 1][:, 0:1, :]), (slice(3, 4), u[:, 2:3, :])]
+            for planes, u_part in parts:
+                nc.gpsimd.tensor_tensor(u_part, dh_copy[:, planes, :], early[:, planes, :], ALU.mult)
+            for planes, u_part in parts:
+                nc.gpsimd.tensor_tensor(da[:, planes, :], u_part, late[:, planes, :], ALU.mult)
+            if e == 1:
+                nc.gpsimd.tensor_tensor(quarter(0)[:, 0:C], ungated[:], gates_kept[:], ALU.mult)
             return da
 
         def project(e, m, operand):
@@ -188,29 +198,36 @@ def tile_moe_bdx_mlp_silu_kernel(tc, dyT, a, w2_words, w2_scales, w1_words, w1_s
 
         function(0, 0)
         function(0, 1)
-        g = [keep.tile([P, PACK, C], F32, name=f"g{e}", tag=f"g{e}") for e in range(E - 1)]
+        g = [keep.tile([P, PACK, C], F32, name=f"g{e}", tag=f"g{e}") for e in range(2)]
+        g_third = keep.tile([P, (PACK + 1) * C], F32, name="g_third", align_bytes=64)
+        g_planes = [g[0][:], g[1][:], g_third[:, 0 : PACK * C].rearrange("p (t c) -> p t c", t=PACK)]
+        g_planes.append(shared[:].rearrange("p (t x) -> p t x", t=PACK)[:, :, 0:C])
+        ungated = keep.tile([P, C], F32, name="ungated")
+        nc.vector.tensor_copy(ungated[:], dy[0][:].indirect(slots(E - 1)))
         for t in range(PACK):
-            for e in range(E - 1):
-                gather(e, t, g[e][:, t, :])
-        g_planes = [tile[:] for tile in g] + [shared[:].rearrange("p (t x) -> p t x", t=PACK)[:, :, 0:C]]
+            gather(0, t, g[0][:, t, :])
+            gather(1, t, g[1][:, t, :])
+            if t + 1 < PACK:
+                gather(2, t, g_third[:, t * C : (t + 1) * C])
         permute(slice(0, E))
 
         def quarter(t):
             return shared[:, 2 * C * t : 2 * C * (t + 1)]
 
-        minus_d = shared[:, 2 * C : 6 * C]
         z, s = silu_and_sigmoid(0)
+        minus_d = z[:].rearrange("p t c -> p (t c)")
         nc.vector.scalar_tensor_tensor(
             out=minus_d,
-            in0=z[:].rearrange("p t c -> p (t c)"),
+            in0=minus_d,
             scalar=1.0,
             in1=s[:].rearrange("p t c -> p (t c)"),
             op0=ALU.subtract,
             op1=ALU.mult,
         )
-        interleave(quarter(0).bitcast(BF16), g_planes[0])
-        g_operand = quantize(quarter(0).bitcast(BF16), "g")
-        gather(E - 1, 0, quarter(0)[:, 0:C])
+        grouped_first = g_third[:, 3 * C : 5 * C].bitcast(BF16)
+        interleave(grouped_first, g_planes[0])
+        g_operand = quantize(grouped_first, "g")
+        gather(2, 3, g_third[:, 3 * C : 4 * C])
         da = ring.tile([P, PACK, C], BF16, name="da", tag="da", align_bytes=64, bufs=1)
         for t in range(PACK):
             nc.vector.scalar_tensor_tensor(
@@ -222,7 +239,10 @@ def tile_moe_bdx_mlp_silu_kernel(tc, dyT, a, w2_words, w2_scales, w1_words, w1_s
                 op1=ALU.mult,
             )
         function(1, 0)
-        g_operand = group(g_planes[1], "g")
+        grouped_second = shared[:, 5 * C // 2 : 9 * C // 2].bitcast(BF16)
+        interleave(grouped_second, g_planes[1])
+        g_operand = quantize(grouped_second, "g")
+        function(1, 1, halves=(0,))
         gather(E - 1, 1, quarter(1)[:, 0:C])
         gather(E - 1, 2, quarter(2)[:, 0:C])
         interleave(quarter(3).bitcast(BF16), da[:])
@@ -235,8 +255,10 @@ def tile_moe_bdx_mlp_silu_kernel(tc, dyT, a, w2_words, w2_scales, w1_words, w1_s
             if e + 1 < E:
                 dh_copy = hidden_gradient(e + 1, g_operand)
             project(e, 1, da_operand)
-            if e == 0:
-                function(1, 1)
+            if e + 1 < E:
+                function(e + 1, 1, halves=(2,))
+            if e % 2 == 0:
+                one_minus(e + 1)
             for m in range(2, K_TILES - 1):
                 project(e, m, da_operand)
             if e + 1 < E:
@@ -247,6 +269,8 @@ def tile_moe_bdx_mlp_silu_kernel(tc, dyT, a, w2_words, w2_scales, w1_words, w1_s
             if e + 1 < E:
                 following = group(da[:], "da")
             project(e, K_TILES - 1, da_operand)
+            if e == 0:
+                one_minus(e + 2)
             if e + 2 < E:
-                function(e + 2, 1)
+                function(e + 2, 1, halves=(0,))
             da_operand = following

@@ -32,9 +32,10 @@ def tile_moe_bdx_mlp_silu_kernel(tc, dyT, a, w2_words, w2_scales, w1_words, w1_s
 
         offsets = keep.tile([P, E * C // 16], U16, name="offsets")
         dy = [keep.tile([P, T], F32, name=f"dy{t}", tag=f"columns{t}") for t in range(PACK)]
-        pre = [keep.tile([P, PACK, C], F32, name=f"pre{e}") for e in range(E)]
+        pre = [keep.tile([P, PACK, C], F32, name=f"pre{e}", tag=f"pre{e}", align_bytes=64) for e in range(E)]
         w2_raw = keep.tile([P, E, 2 * H], U8, name="w2_raw", align_bytes=64)
-        w2 = keep.tile([P, E, 2 * H], U8, name="w2", align_bytes=64)
+        w2 = keep.tile([P, 2, 2 * H], U8, name="w2", align_bytes=64)
+        w2_words_of = [w2[:, 0], w2[:, 1]]
         w2_sraw = keep.tile([P, E, H], U8, name="w2_sraw", align_bytes=64)
         w2_s = keep.tile([P, E, H], U8, name="w2_s", align_bytes=64)
         w1 = keep.tile([P, E, 2 * K], U8, name="w1", align_bytes=64)
@@ -50,7 +51,7 @@ def tile_moe_bdx_mlp_silu_kernel(tc, dyT, a, w2_words, w2_scales, w1_words, w1_s
         nc.vector.memset(w1_s[:].bitcast(I32), 0)
         warm = keep.tile([P, 8], F32, name="warm")
         nc.vector.memset(warm[:], 0.0)
-        nc.scalar.activation(warm[:], warm[:], ACT.Silu)
+        nc.scalar.activation(warm[:], warm[:], ACT.Sigmoid)
 
         dy_rows = dyT.rearrange("(p t) j -> p t j", t=PACK)
         a_rows = a.rearrange("(p t) j -> p t j", t=PACK)
@@ -71,8 +72,8 @@ def tile_moe_bdx_mlp_silu_kernel(tc, dyT, a, w2_words, w2_scales, w1_words, w1_s
         def load_pre(e):
             nc.sync.dma_start(out=pre[e][:], in_=a_rows[:, :, e * C : (e + 1) * C])
 
-        nc.sync.dma_start(out=offsets[:], in_=offs)
         load_dy(0)
+        nc.sync.dma_start(out=offsets[:], in_=offs)
         nc.sync.dma_start(out=gates_first[:], in_=gate[0:P, 0:C])
         nc.sync.dma_start(out=gates_middle[:], in_=gate[0:P, C : 3 * C])
         load_dy(1)
@@ -95,9 +96,17 @@ def tile_moe_bdx_mlp_silu_kernel(tc, dyT, a, w2_words, w2_scales, w1_words, w1_s
                 in_=w2_sraw[:, experts].rearrange("p e (m t) -> p e t m", t=PACK),
             )
             nc.vector.tensor_copy(
-                out=w2[:, experts].bitcast(U16).rearrange("p e (t m) -> p e t m", t=PACK),
-                in_=w2_raw[:, experts].bitcast(U16).rearrange("p e (m t) -> p e t m", t=PACK),
+                out=w2[:].bitcast(U16).rearrange("p e (t m) -> p e t m", t=PACK),
+                in_=w2_raw[:, 0:2].bitcast(U16).rearrange("p e (m t) -> p e t m", t=PACK),
             )
+
+        def permute_late(e):
+            words = keep.tile([P, 2 * H], U8, name=f"w2_late{e}", tag=f"pre{e - 1}", align_bytes=64)
+            nc.gpsimd.tensor_copy(
+                out=words[:].rearrange("p (t m b) -> p t m b", t=PACK, b=2),
+                in_=w2_raw[:, e].rearrange("p (m t b) -> p t m b", t=PACK, b=2),
+            )
+            w2_words_of.append(words[:])
 
         def interleave(grouped, planes):
             nc.scalar.copy(
@@ -112,7 +121,7 @@ def tile_moe_bdx_mlp_silu_kernel(tc, dyT, a, w2_words, w2_scales, w1_words, w1_s
             codes = ring.tile([P, C], U32, name=f"codes_{kind}", align_bytes=64)
             scales = ring.tile([P, C], U8, name=f"scales_{kind}", align_bytes=64)
             nc.vector.quantize_mx(out=codes[:].bitcast(FP8X4), scales=scales[:], in_=grouped)
-            return codes, scales
+            return codes[:], scales[:]
 
         def gather(e, t, plane):
             nc.vector.tensor_tensor(plane, dy[t][:].indirect(slots(e)), gates[e], ALU.mult)
@@ -122,34 +131,43 @@ def tile_moe_bdx_mlp_silu_kernel(tc, dyT, a, w2_words, w2_scales, w1_words, w1_s
             interleave(grouped[:], planes)
             return quantize(grouped[:], kind)
 
+        def group_both(g_part, da_part):
+            grouped = ring.tile([P, 2, C * PACK], BF16, name="grouped_both", align_bytes=64, bufs=1)
+            interleave(grouped[:, 0], g_part)
+            interleave(grouped[:, 1], da_part)
+            codes = ring.tile([P, 2 * C], U32, name="codes_both", align_bytes=64)
+            scales = ring.tile([P, 2 * C], U8, name="scales_both", align_bytes=64)
+            nc.vector.quantize_mx(out=codes[:].bitcast(FP8X4), scales=scales[:], in_=grouped[:].rearrange("p a n -> p (a n)"))
+            return (codes[:, 0:C], scales[:, 0:C]), (codes[:, C : 2 * C], scales[:, C : 2 * C])
+
         second = {}
 
-        def function(e, nth, halves=(0, 2)):
+        def function(e, nth, parts=((0, 2), (2, 4))):
             if e not in second:
                 second[e] = ring.tile([P, PACK, C], F32, name="second")
             target = second[e] if nth == 0 else pre[e]
-            for t in halves:
-                if (e + nth) % 2 == 0:
-                    nc.scalar.activation(target[:, t : t + 2, :], pre[e][:, t : t + 2, :], ACT.Silu, scale=-1.0)
+            for first, last in parts:
+                if (e + nth) % 2 == 1:
+                    nc.scalar.activation(target[:, first:last, :], pre[e][:, first:last, :], ACT.Silu, scale=-1.0)
                 else:
-                    nc.scalar.activation(target[:, t : t + 2, :], pre[e][:, t : t + 2, :], ACT.Sigmoid)
+                    nc.scalar.activation(target[:, first:last, :], pre[e][:, first:last, :], ACT.Sigmoid)
 
-        def one_minus(e):
+        def one_minus(e, halves=(0, 2)):
             z = silu_and_sigmoid(e)[0]
-            for t in range(0, PACK, 2):
+            for t in halves:
                 nc.scalar.activation(z[:, t : t + 2, :], z[:, t : t + 2, :], ACT.Identity, bias=1.0, scale=-1.0)
 
         def silu_and_sigmoid(e):
-            return (second[e], pre[e]) if e % 2 == 0 else (pre[e], second[e])
+            return (second[e], pre[e]) if e % 2 == 1 else (pre[e], second[e])
 
         def first_product(e, t, operand):
             dh = psum_h.tile([P, C], F32, name="dh")
             nc.tensor.matmul_mx(
                 out=dh[:],
-                lhsT=w2[:, e, 2 * P * t : 2 * P * (t + 1)].bitcast(FP4X4),
+                lhsT=w2_words_of[e][:, 2 * P * t : 2 * P * (t + 1)].bitcast(FP4X4),
                 lhsT_scale=w2_s[:, e, P * t : P * (t + 1)],
-                rhs=operand[0][:].bitcast(FP8X4),
-                rhs_scale=operand[1][:],
+                rhs=operand[0].bitcast(FP8X4),
+                rhs_scale=operand[1],
                 start=True,
                 stop=True,
             )
@@ -182,8 +200,8 @@ def tile_moe_bdx_mlp_silu_kernel(tc, dyT, a, w2_words, w2_scales, w1_words, w1_s
                 out=dx[:],
                 lhsT=w1[:, e, 2 * P * m : 2 * P * (m + 1)].bitcast(FP4X4),
                 lhsT_scale=w1_s[:, e, P * m : P * (m + 1)],
-                rhs=operand[0][:].bitcast(FP8X4),
-                rhs_scale=operand[1][:],
+                rhs=operand[0].bitcast(FP8X4),
+                rhs_scale=operand[1],
                 start=True,
                 stop=True,
             )
@@ -198,17 +216,22 @@ def tile_moe_bdx_mlp_silu_kernel(tc, dyT, a, w2_words, w2_scales, w1_words, w1_s
 
         function(0, 0)
         function(0, 1)
-        g = [keep.tile([P, PACK, C], F32, name=f"g{e}", tag=f"g{e}") for e in range(2)]
-        g_third = keep.tile([P, (PACK + 1) * C], F32, name="g_third", align_bytes=64)
-        g_planes = [g[0][:], g[1][:], g_third[:, 0 : PACK * C].rearrange("p (t c) -> p t c", t=PACK)]
+        g_first = keep.tile([P, PACK, C], F32, name="g_first", tag="g0")
+        g_middle = keep.tile([P, (2 * PACK + 1) * C], F32, name="g_middle", align_bytes=64)
+        by_plane = g_middle[:, 0 : 2 * PACK * C].rearrange("p (t e c) -> p t e c", t=PACK, e=2)
+        g_planes = [g_first[:], by_plane[:, :, 0, :], by_plane[:, :, 1, :]]
         g_planes.append(shared[:].rearrange("p (t x) -> p t x", t=PACK)[:, :, 0:C])
         ungated = keep.tile([P, C], F32, name="ungated")
         nc.vector.tensor_copy(ungated[:], dy[0][:].indirect(slots(E - 1)))
         for t in range(PACK):
-            gather(0, t, g[0][:, t, :])
-            gather(1, t, g[1][:, t, :])
+            gather(0, t, g_first[:, t, :])
             if t + 1 < PACK:
-                gather(2, t, g_third[:, t * C : (t + 1) * C])
+                both = offsets[:, C // 16 : 3 * C // 16]
+                nc.vector.tensor_tensor(
+                    g_middle[:, 2 * t * C : 2 * (t + 1) * C], dy[t][:].indirect(both), gates_middle[:], ALU.mult
+                )
+            else:
+                gather(1, t, g_middle[:, 2 * t * C : (2 * t + 1) * C])
         permute(slice(0, E))
 
         def quarter(t):
@@ -224,10 +247,10 @@ def tile_moe_bdx_mlp_silu_kernel(tc, dyT, a, w2_words, w2_scales, w1_words, w1_s
             op0=ALU.subtract,
             op1=ALU.mult,
         )
-        grouped_first = g_third[:, 3 * C : 5 * C].bitcast(BF16)
+        grouped_first = g_middle[:, 7 * C : 9 * C].bitcast(BF16)
         interleave(grouped_first, g_planes[0])
         g_operand = quantize(grouped_first, "g")
-        gather(2, 3, g_third[:, 3 * C : 4 * C])
+        gather(2, 3, g_middle[:, 7 * C : 8 * C])
         da = ring.tile([P, PACK, C], BF16, name="da", tag="da", align_bytes=64, bufs=1)
         for t in range(PACK):
             nc.vector.scalar_tensor_tensor(
@@ -242,7 +265,7 @@ def tile_moe_bdx_mlp_silu_kernel(tc, dyT, a, w2_words, w2_scales, w1_words, w1_s
         grouped_second = shared[:, 5 * C // 2 : 9 * C // 2].bitcast(BF16)
         interleave(grouped_second, g_planes[1])
         g_operand = quantize(grouped_second, "g")
-        function(1, 1, halves=(0,))
+        one_minus(1, halves=(0,))
         gather(E - 1, 1, quarter(1)[:, 0:C])
         gather(E - 1, 2, quarter(2)[:, 0:C])
         interleave(quarter(3).bitcast(BF16), da[:])
@@ -255,22 +278,28 @@ def tile_moe_bdx_mlp_silu_kernel(tc, dyT, a, w2_words, w2_scales, w1_words, w1_s
             if e + 1 < E:
                 dh_copy = hidden_gradient(e + 1, g_operand)
             project(e, 1, da_operand)
-            if e + 1 < E:
-                function(e + 1, 1, halves=(2,))
-            if e % 2 == 0:
+            if e == 0:
+                one_minus(1, halves=(2,))
+            elif e + 1 < E:
+                function(e + 1, 1, parts=((2, 4),))
+            if e == 1:
                 one_minus(e + 1)
-            for m in range(2, K_TILES - 1):
+            project(e, 2, da_operand)
+            if e == 0:
+                function(1, 1)
+            for m in range(3, K_TILES - 1):
                 project(e, m, da_operand)
             if e + 1 < E:
                 da = through_silu(e + 1, dh_copy)
             if e + 2 < E:
+                permute_late(e + 2)
                 function(e + 2, 0)
-                g_operand = group(g_planes[e + 2], "g")
-            if e + 1 < E:
+                g_operand, following = group_both(g_planes[e + 2], da[:])
+            elif e + 1 < E:
                 following = group(da[:], "da")
             project(e, K_TILES - 1, da_operand)
-            if e == 0:
+            if e == 1:
                 one_minus(e + 2)
             if e + 2 < E:
-                function(e + 2, 1, halves=(0,))
+                function(e + 2, 1, parts=((0, 2),))
             da_operand = following

@@ -33,7 +33,7 @@ def tile_moe_bdx_mlp_silu_kernel(tc, dyT, a, w2_words, w2_scales, w1_words, w1_s
         offsets = keep.tile([P, E * C // 16], U16, name="offsets")
         dy = [keep.tile([P, T], F32, name=f"dy{t}", tag=f"columns{t}") for t in range(PACK)]
         pre = [keep.tile([P, PACK, C], F32, name=f"pre{e}", tag=f"pre{e}", align_bytes=64) for e in range(E)]
-        w2_raw = keep.tile([P, E, 2 * H], U8, name="w2_raw", align_bytes=64)
+        w2_raw = [keep.tile([P, 2, 2 * H], U8, name=f"w2_raw{pair}", align_bytes=64) for pair in range(2)]
         w2 = keep.tile([P, 2, 2 * H], U8, name="w2", align_bytes=64)
         w2_words_of = [w2[:, 0], w2[:, 1]]
         w2_sraw = keep.tile([P, E, H], U8, name="w2_sraw", align_bytes=64)
@@ -72,6 +72,8 @@ def tile_moe_bdx_mlp_silu_kernel(tc, dyT, a, w2_words, w2_scales, w1_words, w1_s
         def load_pre(e):
             nc.sync.dma_start(out=pre[e][:], in_=a_rows[:, :, e * C : (e + 1) * C])
 
+        load_scales(w2_sraw, w2_scales)
+        load_words(w2_raw[0], w2_words[0:2])
         load_dy(0)
         nc.sync.dma_start(out=offsets[:], in_=offs)
         nc.sync.dma_start(out=gates_first[:], in_=gate[0:P, 0:C])
@@ -80,12 +82,11 @@ def tile_moe_bdx_mlp_silu_kernel(tc, dyT, a, w2_words, w2_scales, w1_words, w1_s
         load_pre(0)
         load_dy(2)
         load_dy(3)
-        load_scales(w2_sraw, w2_scales)
-        load_words(w2_raw, w2_words)
         load_pre(1)
         nc.sync.dma_start(out=gates_last[:], in_=gate[0:P, 3 * C : 4 * C])
         load_scales(w1_s, w1_scales)
         load_words(w1, w1_words)
+        load_words(w2_raw[1], w2_words[2:4])
         load_pre(2)
         nc.sync.dma_start(out=gates_kept[:], in_=gate[P : 2 * P, 3 * C : 4 * C])
         load_pre(3)
@@ -97,14 +98,14 @@ def tile_moe_bdx_mlp_silu_kernel(tc, dyT, a, w2_words, w2_scales, w1_words, w1_s
             )
             nc.vector.tensor_copy(
                 out=w2[:].bitcast(U16).rearrange("p e (t m) -> p e t m", t=PACK),
-                in_=w2_raw[:, 0:2].bitcast(U16).rearrange("p e (m t) -> p e t m", t=PACK),
+                in_=w2_raw[0][:].bitcast(U16).rearrange("p e (m t) -> p e t m", t=PACK),
             )
 
         def permute_late(e):
             words = keep.tile([P, 2 * H], U8, name=f"w2_late{e}", tag=f"pre{e - 1}", align_bytes=64)
             nc.gpsimd.tensor_copy(
                 out=words[:].rearrange("p (t m b) -> p t m b", t=PACK, b=2),
-                in_=w2_raw[:, e].rearrange("p (m t b) -> p t m b", t=PACK, b=2),
+                in_=w2_raw[1][:, e - 2].rearrange("p (m t b) -> p t m b", t=PACK, b=2),
             )
             w2_words_of.append(words[:])
 
@@ -217,21 +218,17 @@ def tile_moe_bdx_mlp_silu_kernel(tc, dyT, a, w2_words, w2_scales, w1_words, w1_s
         function(0, 0)
         function(0, 1)
         g_first = keep.tile([P, PACK, C], F32, name="g_first", tag="g0")
-        g_middle = keep.tile([P, (2 * PACK + 1) * C], F32, name="g_middle", align_bytes=64)
-        by_plane = g_middle[:, 0 : 2 * PACK * C].rearrange("p (t e c) -> p t e c", t=PACK, e=2)
-        g_planes = [g_first[:], by_plane[:, :, 0, :], by_plane[:, :, 1, :]]
+        g_second = keep.tile([P, PACK, C], F32, name="g_second")
+        g_third = keep.tile([P, PACK * C], F32, name="g_third", align_bytes=64)
+        g_planes = [g_first[:], g_second[:], g_third[:].rearrange("p (t c) -> p t c", t=PACK)]
         g_planes.append(shared[:].rearrange("p (t x) -> p t x", t=PACK)[:, :, 0:C])
         ungated = keep.tile([P, C], F32, name="ungated")
         nc.vector.tensor_copy(ungated[:], dy[0][:].indirect(slots(E - 1)))
         for t in range(PACK):
             gather(0, t, g_first[:, t, :])
-            if t + 1 < PACK:
-                both = offsets[:, C // 16 : 3 * C // 16]
-                nc.vector.tensor_tensor(
-                    g_middle[:, 2 * t * C : 2 * (t + 1) * C], dy[t][:].indirect(both), gates_middle[:], ALU.mult
-                )
-            else:
-                gather(1, t, g_middle[:, 2 * t * C : (2 * t + 1) * C])
+            gather(1, t, g_second[:, t, :])
+            if t < 2:
+                gather(2, t, g_third[:, t * C : (t + 1) * C])
         permute(slice(0, E))
 
         def quarter(t):
@@ -247,10 +244,11 @@ def tile_moe_bdx_mlp_silu_kernel(tc, dyT, a, w2_words, w2_scales, w1_words, w1_s
             op0=ALU.subtract,
             op1=ALU.mult,
         )
-        grouped_first = g_middle[:, 7 * C : 9 * C].bitcast(BF16)
+        grouped_first = g_third[:, 2 * C : 4 * C].bitcast(BF16)
         interleave(grouped_first, g_planes[0])
         g_operand = quantize(grouped_first, "g")
-        gather(2, 3, g_middle[:, 7 * C : 8 * C])
+        gather(2, 2, g_third[:, 2 * C : 3 * C])
+        gather(2, 3, g_third[:, 3 * C : 4 * C])
         da = ring.tile([P, PACK, C], BF16, name="da", tag="da", align_bytes=64, bufs=1)
         for t in range(PACK):
             nc.vector.scalar_tensor_tensor(

@@ -33,9 +33,8 @@ def tile_moe_bdx_mlp_silu_kernel(tc, dyT, a, w2_words, w2_scales, w1_words, w1_s
         offsets = keep.tile([P, E * C // 16], U16, name="offsets")
         dy = [keep.tile([P, T], F32, name=f"dy{t}", tag=f"columns{t}") for t in range(PACK)]
         pre = [keep.tile([P, PACK, C], F32, name=f"pre{e}", tag=f"pre{e}", align_bytes=64) for e in range(E)]
-        w2_raw = [keep.tile([P, 2, 2 * H], U8, name=f"w2_raw{pair}", align_bytes=64) for pair in range(2)]
-        w2 = keep.tile([P, 2, 2 * H], U8, name="w2", align_bytes=64)
-        w2_words_of = [w2[:, 0], w2[:, 1]]
+        w2_raw = keep.tile([P, E, 2 * H], U8, name="w2_raw", align_bytes=64)
+        w2 = keep.tile([P, E, 2 * H], U8, name="w2", align_bytes=64)
         w2_sraw = keep.tile([P, E, H], U8, name="w2_sraw", align_bytes=64)
         w2_s = keep.tile([P, E, H], U8, name="w2_s", align_bytes=64)
         w1 = keep.tile([P, E, 2 * K], U8, name="w1", align_bytes=64)
@@ -73,7 +72,7 @@ def tile_moe_bdx_mlp_silu_kernel(tc, dyT, a, w2_words, w2_scales, w1_words, w1_s
             nc.sync.dma_start(out=pre[e][:], in_=a_rows[:, :, e * C : (e + 1) * C])
 
         load_scales(w2_sraw, w2_scales)
-        load_words(w2_raw[0], w2_words[0:2])
+        load_words(w2_raw, w2_words)
         load_dy(0)
         nc.sync.dma_start(out=offsets[:], in_=offs)
         nc.sync.dma_start(out=gates_first[:], in_=gate[0:P, 0:C])
@@ -86,7 +85,6 @@ def tile_moe_bdx_mlp_silu_kernel(tc, dyT, a, w2_words, w2_scales, w1_words, w1_s
         nc.sync.dma_start(out=gates_last[:], in_=gate[0:P, 3 * C : 4 * C])
         load_scales(w1_s, w1_scales)
         load_words(w1, w1_words)
-        load_words(w2_raw[1], w2_words[2:4])
         load_pre(2)
         nc.sync.dma_start(out=gates_kept[:], in_=gate[P : 2 * P, 3 * C : 4 * C])
         load_pre(3)
@@ -98,16 +96,8 @@ def tile_moe_bdx_mlp_silu_kernel(tc, dyT, a, w2_words, w2_scales, w1_words, w1_s
             )
             nc.vector.tensor_copy(
                 out=w2[:].bitcast(U16).rearrange("p e (t m) -> p e t m", t=PACK),
-                in_=w2_raw[0][:].bitcast(U16).rearrange("p e (m t) -> p e t m", t=PACK),
+                in_=w2_raw[:].bitcast(U16).rearrange("p e (m t) -> p e t m", t=PACK),
             )
-
-        def permute_late(e):
-            words = keep.tile([P, 2 * H], U8, name=f"w2_late{e}", tag=f"pre{e - 1}", align_bytes=64)
-            nc.gpsimd.tensor_copy(
-                out=words[:].rearrange("p (t m b) -> p t m b", t=PACK, b=2),
-                in_=w2_raw[1][:, e - 2].rearrange("p (m t b) -> p t m b", t=PACK, b=2),
-            )
-            w2_words_of.append(words[:])
 
         def interleave(grouped, planes):
             nc.scalar.copy(
@@ -165,7 +155,7 @@ def tile_moe_bdx_mlp_silu_kernel(tc, dyT, a, w2_words, w2_scales, w1_words, w1_s
             dh = psum_h.tile([P, C], F32, name="dh")
             nc.tensor.matmul_mx(
                 out=dh[:],
-                lhsT=w2_words_of[e][:, 2 * P * t : 2 * P * (t + 1)].bitcast(FP4X4),
+                lhsT=w2[:, e, 2 * P * t : 2 * P * (t + 1)].bitcast(FP4X4),
                 lhsT_scale=w2_s[:, e, P * t : P * (t + 1)],
                 rhs=operand[0].bitcast(FP8X4),
                 rhs_scale=operand[1],
@@ -290,7 +280,6 @@ def tile_moe_bdx_mlp_silu_kernel(tc, dyT, a, w2_words, w2_scales, w1_words, w1_s
             if e + 1 < E:
                 da = through_silu(e + 1, dh_copy)
             if e + 2 < E:
-                permute_late(e + 2)
                 function(e + 2, 0)
                 g_operand, following = group_both(g_planes[e + 2], da[:])
             elif e + 1 < E:

@@ -6,6 +6,10 @@ K, T, E, C, H, N = 768, 2048, 4, 512, 512, 512
 P = 128
 PACK = 4
 K_TILES = K // P
+LIST_ROWS = 16
+QUADRANTS, QUADRANT_ROWS, SCALE_ROWS = 4, 32, 4
+RUN = 4
+LOWER, UPPER = slice(0, 2), slice(2, 4)
 
 F32 = mybir.dt.float32
 BF16 = mybir.dt.bfloat16
@@ -30,7 +34,7 @@ def tile_moe_bdx_mlp_silu_kernel(tc, dyT, a, w2_words, w2_scales, w1_words, w1_s
         psum_h = ctx.enter_context(tc.psum_pool(name="psum_h", bufs=4))
         psum_x = ctx.enter_context(tc.psum_pool(name="psum_x", bufs=4))
 
-        offsets = keep.tile([P, E * C // 16], U16, name="offsets")
+        offsets = keep.tile([P, E * C // LIST_ROWS], U16, name="offsets")
         dy = [keep.tile([P, T], F32, name=f"dy{t}", tag=f"columns{t}") for t in range(PACK)]
         pre = [keep.tile([P, PACK, C], F32, name=f"pre{e}", tag=f"pre{e}", align_bytes=64) for e in range(E)]
         w2_raw = keep.tile([P, E, 2 * H], U8, name="w2_raw", align_bytes=64)
@@ -48,22 +52,19 @@ def tile_moe_bdx_mlp_silu_kernel(tc, dyT, a, w2_words, w2_scales, w1_words, w1_s
 
         nc.vector.memset(w2_sraw[:].bitcast(I32), 0)
         nc.vector.memset(w1_s[:].bitcast(I32), 0)
-        warm = keep.tile([P, 8], F32, name="warm")
-        nc.vector.memset(warm[:], 0.0)
-        nc.scalar.activation(warm[:], warm[:], ACT.Sigmoid)
 
         dy_rows = dyT.rearrange("(p t) j -> p t j", t=PACK)
         a_rows = a.rearrange("(p t) j -> p t j", t=PACK)
 
-        def load_scales(planes, scales):
-            for q in range(4):
+        def load_scales(rows, scales):
+            for q in range(QUADRANTS):
                 nc.sync.dma_start(
-                    out=planes[32 * q : 32 * q + 4].bitcast(I32),
-                    in_=scales[:, 0, 4 * q : 4 * q + 4, :].rearrange("e f n -> f e n").bitcast(I32),
+                    out=rows[QUADRANT_ROWS * q : QUADRANT_ROWS * q + SCALE_ROWS].bitcast(I32),
+                    in_=scales[:, 0, SCALE_ROWS * q : SCALE_ROWS * (q + 1), :].rearrange("e f n -> f e n").bitcast(I32),
                 )
 
-        def load_words(tile, words):
-            nc.sync.dma_start(out=tile[:].bitcast(I32), in_=words.rearrange("e o p n -> p (e o) n").bitcast(I32))
+        def load_words(words, source):
+            nc.sync.dma_start(out=words[:].bitcast(I32), in_=source.rearrange("e o p n -> p (e o) n").bitcast(I32))
 
         def load_dy(t):
             nc.sync.dma_start(out=dy[t][:], in_=dy_rows[:, t, :])
@@ -71,8 +72,8 @@ def tile_moe_bdx_mlp_silu_kernel(tc, dyT, a, w2_words, w2_scales, w1_words, w1_s
         def load_pre(e):
             nc.sync.dma_start(out=pre[e][:], in_=a_rows[:, :, e * C : (e + 1) * C])
 
-        load_scales(w2_sraw, w2_scales)
         load_words(w2_raw, w2_words)
+        load_scales(w2_sraw, w2_scales)
         load_dy(0)
         nc.sync.dma_start(out=offsets[:], in_=offs)
         nc.sync.dma_start(out=gates_first[:], in_=gate[0:P, 0:C])
@@ -89,113 +90,79 @@ def tile_moe_bdx_mlp_silu_kernel(tc, dyT, a, w2_words, w2_scales, w1_words, w1_s
         nc.sync.dma_start(out=gates_kept[:], in_=gate[P : 2 * P, 3 * C : 4 * C])
         load_pre(3)
 
-        def permute(experts):
-            nc.vector.tensor_copy(
-                out=w2_s[:, experts].rearrange("p e (t m) -> p e t m", t=PACK),
-                in_=w2_sraw[:, experts].rearrange("p e (m t) -> p e t m", t=PACK),
-            )
-            nc.vector.tensor_copy(
-                out=w2[:].bitcast(U16).rearrange("p e (t m) -> p e t m", t=PACK),
-                in_=w2_raw[:].bitcast(U16).rearrange("p e (m t) -> p e t m", t=PACK),
-            )
-
-        def interleave(grouped, planes):
-            nc.scalar.copy(
-                out=grouped.rearrange("p (c i t) -> p c t i", i=4, t=PACK),
-                in_=planes.rearrange("p t (c i) -> p c t i", i=4),
-            )
+        def quarter(t):
+            return shared[:, 2 * C * t : 2 * C * (t + 1)]
 
         def slots(e):
-            return offsets[:, e * C // 16 : (e + 1) * C // 16]
-
-        def quantize(grouped, kind):
-            codes = ring.tile([P, C], U32, name=f"codes_{kind}", align_bytes=64)
-            scales = ring.tile([P, C], U8, name=f"scales_{kind}", align_bytes=64)
-            nc.vector.quantize_mx(out=codes[:].bitcast(FP8X4), scales=scales[:], in_=grouped)
-            return codes[:], scales[:]
+            return offsets[:, e * C // LIST_ROWS : (e + 1) * C // LIST_ROWS]
 
         def gather(e, t, plane):
             nc.vector.tensor_tensor(plane, dy[t][:].indirect(slots(e)), gates[e], ALU.mult)
 
-        def group(planes, kind):
-            grouped = ring.tile([P, C * PACK], BF16, name=f"grouped_{kind}", align_bytes=64, bufs=1)
-            interleave(grouped[:], planes)
-            return quantize(grouped[:], kind)
+        def interleave(grouped, planes):
+            nc.scalar.copy(
+                out=grouped.rearrange("p (c i t) -> p c t i", i=RUN, t=PACK),
+                in_=planes.rearrange("p t (c i) -> p c t i", i=RUN),
+            )
 
-        def group_both(g_part, da_part):
-            grouped = ring.tile([P, 2, C * PACK], BF16, name="grouped_both", align_bytes=64, bufs=1)
-            interleave(grouped[:, 0], g_part)
-            interleave(grouped[:, 1], da_part)
-            codes = ring.tile([P, 2 * C], U32, name="codes_both", align_bytes=64)
-            scales = ring.tile([P, 2 * C], U8, name="scales_both", align_bytes=64)
-            nc.vector.quantize_mx(out=codes[:].bitcast(FP8X4), scales=scales[:], in_=grouped[:].rearrange("p a n -> p (a n)"))
-            return (codes[:, 0:C], scales[:, 0:C]), (codes[:, C : 2 * C], scales[:, C : 2 * C])
+        def quantize(grouped, kind, operands=1):
+            codes = ring.tile([P, operands * C], U32, name=f"codes_{kind}", align_bytes=64)
+            scales = ring.tile([P, operands * C], U8, name=f"scales_{kind}", align_bytes=64)
+            nc.vector.quantize_mx(out=codes[:].bitcast(FP8X4), scales=scales[:], in_=grouped)
+            return [(codes[:, j * C : (j + 1) * C], scales[:, j * C : (j + 1) * C]) for j in range(operands)]
 
-        second = {}
+        early = {}
 
-        def function(e, nth, parts=((0, 2), (2, 4))):
-            if e not in second:
-                second[e] = ring.tile([P, PACK, C], F32, name="second")
-            target = second[e] if nth == 0 else pre[e]
-            for first, last in parts:
+        def function(e, nth, halves=(LOWER, UPPER)):
+            if nth == 0:
+                early[e] = ring.tile([P, PACK, C], F32, name="second")
+            target = early[e] if nth == 0 else pre[e]
+            for planes in halves:
                 if (e + nth) % 2 == 1:
-                    nc.scalar.activation(target[:, first:last, :], pre[e][:, first:last, :], ACT.Silu, scale=-1.0)
+                    nc.scalar.activation(target[:, planes, :], pre[e][:, planes, :], ACT.Silu, scale=-1.0)
                 else:
-                    nc.scalar.activation(target[:, first:last, :], pre[e][:, first:last, :], ACT.Sigmoid)
+                    nc.scalar.activation(target[:, planes, :], pre[e][:, planes, :], ACT.Sigmoid)
 
-        def one_minus(e, halves=(0, 2)):
-            z = silu_and_sigmoid(e)[0]
-            for t in halves:
-                nc.scalar.activation(z[:, t : t + 2, :], z[:, t : t + 2, :], ACT.Identity, bias=1.0, scale=-1.0)
+        def one_minus_silu(e, halves=(LOWER, UPPER)):
+            silu = early[e] if e % 2 == 1 else pre[e]
+            for planes in halves:
+                nc.scalar.activation(silu[:, planes, :], silu[:, planes, :], ACT.Identity, bias=1.0, scale=-1.0)
 
-        def silu_and_sigmoid(e):
-            return (second[e], pre[e]) if e % 2 == 1 else (pre[e], second[e])
-
-        def first_product(e, t, operand):
-            dh = psum_h.tile([P, C], F32, name="dh")
+        def product(psum, name, words, scales, e, tile, operand):
+            bank = psum.tile([P, C], F32, name=name)
             nc.tensor.matmul_mx(
-                out=dh[:],
-                lhsT=w2[:, e, 2 * P * t : 2 * P * (t + 1)].bitcast(FP4X4),
-                lhsT_scale=w2_s[:, e, P * t : P * (t + 1)],
+                out=bank[:],
+                lhsT=words[:, e, 2 * P * tile : 2 * P * (tile + 1)].bitcast(FP4X4),
+                lhsT_scale=scales[:, e, P * tile : P * (tile + 1)],
                 rhs=operand[0].bitcast(FP8X4),
                 rhs_scale=operand[1],
                 start=True,
                 stop=True,
             )
+            return bank
+
+        def hidden_gradient(e, g_operand):
+            dh = keep.tile([P, PACK, C], F32, name=f"dh_copy{e}", tag="held" if e > 1 else "g0")
+            for t in range(PACK):
+                nc.scalar.copy(out=dh[:, t, :], in_=product(psum_h, "dh", w2, w2_s, e, t, g_operand)[:])
             return dh
 
-        def hidden_gradient(e, operand):
-            dh_copy = keep.tile([P, PACK, C], F32, name=f"dh_copy{e}", tag="held" if e > 1 else "g0")
-            for t in range(PACK):
-                nc.scalar.copy(out=dh_copy[:, t, :], in_=first_product(e, t, operand)[:])
-            return dh_copy
-
-        def through_silu(e, dh_copy):
+        def through_silu(e, dh):
             da = ring.tile([P, PACK, C], BF16, name="da", tag="da", align_bytes=64, bufs=1)
-            early, late = second[e], pre[e]
-            parts = [(slice(0, 2), dh_copy[:, 0:2, :]), (slice(2, 4), dh_copy[:, 2:4, :])]
+            parts = [(planes, dh[:, planes, :]) for planes in (LOWER, UPPER)]
             if e == 1:
-                u = keep.tile([P, PACK - 1, C], F32, name="u", tag="held")
-                parts = [(slice(0, 2), u[:, 0:2, :]), (slice(2, 3), g_planes[E - 1][:, 0:1, :]), (slice(3, 4), u[:, 2:3, :])]
-            for planes, u_part in parts:
-                nc.gpsimd.tensor_tensor(u_part, dh_copy[:, planes, :], early[:, planes, :], ALU.mult)
-            for planes, u_part in parts:
-                nc.gpsimd.tensor_tensor(da[:, planes, :], u_part, late[:, planes, :], ALU.mult)
+                held = keep.tile([P, PACK - 1, C], F32, name="u", tag="held")
+                parts = [(LOWER, held[:, 0:2, :]), (slice(2, 3), g_planes[3][:, 0:1, :]), (slice(3, 4), held[:, 2:3, :])]
+            for planes, partial in parts:
+                nc.gpsimd.tensor_tensor(partial, dh[:, planes, :], early[e][:, planes, :], ALU.mult)
+            for planes, partial in parts:
+                nc.gpsimd.tensor_tensor(da[:, planes, :], partial, pre[e][:, planes, :], ALU.mult)
             if e == 1:
                 nc.gpsimd.tensor_tensor(quarter(0)[:, 0:C], ungated[:], gates_kept[:], ALU.mult)
             return da
 
-        def project(e, m, operand):
-            dx = psum_x.tile([P, C], F32, name="dx")
-            nc.tensor.matmul_mx(
-                out=dx[:],
-                lhsT=w1[:, e, 2 * P * m : 2 * P * (m + 1)].bitcast(FP4X4),
-                lhsT_scale=w1_s[:, e, P * m : P * (m + 1)],
-                rhs=operand[0].bitcast(FP8X4),
-                rhs_scale=operand[1],
-                start=True,
-                stop=True,
-            )
+        def project(e, m, da_operand):
+            dx = product(psum_x, "dx", w1, w1_s, e, m, da_operand)
             if m + 1 < K_TILES:
                 result = ring.tile([P, C], F32, name="result", bufs=K_TILES - 1)
             else:
@@ -213,37 +180,41 @@ def tile_moe_bdx_mlp_silu_kernel(tc, dyT, a, w2_words, w2_scales, w1_words, w1_s
         g_planes = [g_first[:], g_second[:], g_third[:].rearrange("p (t c) -> p t c", t=PACK)]
         g_planes.append(shared[:].rearrange("p (t x) -> p t x", t=PACK)[:, :, 0:C])
         ungated = keep.tile([P, C], F32, name="ungated")
-        nc.vector.tensor_copy(ungated[:], dy[0][:].indirect(slots(E - 1)))
+        nc.vector.tensor_copy(ungated[:], dy[0][:].indirect(slots(3)))
         for t in range(PACK):
             gather(0, t, g_first[:, t, :])
             gather(1, t, g_second[:, t, :])
             if t < 2:
                 gather(2, t, g_third[:, t * C : (t + 1) * C])
-        permute(slice(0, E))
 
-        def quarter(t):
-            return shared[:, 2 * C * t : 2 * C * (t + 1)]
+        nc.vector.tensor_copy(
+            out=w2_s[:].rearrange("p e (t m) -> p e t m", t=PACK),
+            in_=w2_sraw[:].rearrange("p e (m t) -> p e t m", t=PACK),
+        )
+        nc.vector.tensor_copy(
+            out=w2[:].bitcast(U16).rearrange("p e (t m) -> p e t m", t=PACK),
+            in_=w2_raw[:].bitcast(U16).rearrange("p e (m t) -> p e t m", t=PACK),
+        )
 
-        z, s = silu_and_sigmoid(0)
-        minus_d = z[:].rearrange("p t c -> p (t c)")
+        minus_d = pre[0][:].rearrange("p t c -> p (t c)")
         nc.vector.scalar_tensor_tensor(
             out=minus_d,
             in0=minus_d,
             scalar=1.0,
-            in1=s[:].rearrange("p t c -> p (t c)"),
+            in1=early[0][:].rearrange("p t c -> p (t c)"),
             op0=ALU.subtract,
             op1=ALU.mult,
         )
         grouped_first = g_third[:, 2 * C : 4 * C].bitcast(BF16)
         interleave(grouped_first, g_planes[0])
-        g_operand = quantize(grouped_first, "g")
+        [g_operand] = quantize(grouped_first, "g")
         gather(2, 2, g_third[:, 2 * C : 3 * C])
         gather(2, 3, g_third[:, 3 * C : 4 * C])
         da = ring.tile([P, PACK, C], BF16, name="da", tag="da", align_bytes=64, bufs=1)
         for t in range(PACK):
             nc.vector.scalar_tensor_tensor(
                 out=da[:, t, :],
-                in0=first_product(0, t, g_operand)[:],
+                in0=product(psum_h, "dh", w2, w2_s, 0, t, g_operand)[:],
                 scalar=-1.0,
                 in1=minus_d[:, t * C : (t + 1) * C],
                 op0=ALU.mult,
@@ -252,41 +223,46 @@ def tile_moe_bdx_mlp_silu_kernel(tc, dyT, a, w2_words, w2_scales, w1_words, w1_s
         function(1, 0)
         grouped_second = shared[:, 5 * C // 2 : 9 * C // 2].bitcast(BF16)
         interleave(grouped_second, g_planes[1])
-        g_operand = quantize(grouped_second, "g")
-        one_minus(1, halves=(0,))
-        gather(E - 1, 1, quarter(1)[:, 0:C])
-        gather(E - 1, 2, quarter(2)[:, 0:C])
+        [g_operand] = quantize(grouped_second, "g")
+        one_minus_silu(1, halves=(LOWER,))
+        gather(3, 1, quarter(1)[:, 0:C])
+        gather(3, 2, quarter(2)[:, 0:C])
         interleave(quarter(3).bitcast(BF16), da[:])
-        da_operand = quantize(quarter(3).bitcast(BF16), "da")
-        gather(E - 1, 3, quarter(3)[:, 0:C])
+        [da_operand] = quantize(quarter(3).bitcast(BF16), "da")
+        gather(3, 3, quarter(3)[:, 0:C])
 
         window = [keep.tile([P, T], F32, name=f"window{m}", tag=f"columns{m}") for m in range(K_TILES)]
         for e in range(E):
             project(e, 0, da_operand)
             if e + 1 < E:
-                dh_copy = hidden_gradient(e + 1, g_operand)
+                dh = hidden_gradient(e + 1, g_operand)
             project(e, 1, da_operand)
             if e == 0:
-                one_minus(1, halves=(2,))
+                one_minus_silu(1, halves=(UPPER,))
             elif e + 1 < E:
-                function(e + 1, 1, parts=((2, 4),))
+                function(e + 1, 1, halves=(UPPER,))
             if e == 1:
-                one_minus(e + 1)
+                one_minus_silu(2)
             project(e, 2, da_operand)
             if e == 0:
                 function(1, 1)
             for m in range(3, K_TILES - 1):
                 project(e, m, da_operand)
             if e + 1 < E:
-                da = through_silu(e + 1, dh_copy)
+                da = through_silu(e + 1, dh)
             if e + 2 < E:
                 function(e + 2, 0)
-                g_operand, following = group_both(g_planes[e + 2], da[:])
+                grouped = ring.tile([P, 2, C * PACK], BF16, name="grouped_both", align_bytes=64, bufs=1)
+                interleave(grouped[:, 0], g_planes[e + 2])
+                interleave(grouped[:, 1], da[:])
+                g_operand, next_operand = quantize(grouped[:].rearrange("p a n -> p (a n)"), "both", operands=2)
             elif e + 1 < E:
-                following = group(da[:], "da")
+                grouped = ring.tile([P, C * PACK], BF16, name="grouped_da", align_bytes=64, bufs=1)
+                interleave(grouped[:], da[:])
+                [next_operand] = quantize(grouped[:], "da")
             project(e, K_TILES - 1, da_operand)
             if e == 1:
-                one_minus(e + 2)
+                one_minus_silu(3)
             if e + 2 < E:
-                function(e + 2, 1, parts=((0, 2),))
-            da_operand = following
+                function(e + 2, 1, halves=(LOWER,))
+            da_operand = next_operand

@@ -1,6 +1,7 @@
 from contextlib import ExitStack
 
 import concourse.mybir as mybir
+from concourse.masks import make_identity
 
 K, T, E, C, H, N = 768, 2048, 4, 512, 512, 512
 P = 128
@@ -36,19 +37,16 @@ def tile_moe_bdx_mlp_silu_kernel(tc, dyT, a, w2_words, w2_scales, w1_words, w1_s
 
         offsets = keep.tile([P, E * C // LIST_ROWS], U16, name="offsets")
         dy = [keep.tile([P, T], F32, name=f"dy{t}", tag=f"columns{t}") for t in range(PACK)]
-        pre = [keep.tile([P, PACK, C], F32, name=f"pre{e}", tag=f"pre{e}", align_bytes=64) for e in range(E)]
-        w2_raw = keep.tile([P, E, 2 * H], U8, name="w2_raw", align_bytes=64)
-        w2 = keep.tile([P, E, 2 * H], U8, name="w2", align_bytes=64)
+        pre = {e: keep.tile([P, PACK, C], F32, name=f"pre{e}") for e in range(1, E)}
+        w2_raw = [keep.tile([P, 2, 2 * H], U8, name=f"w2_raw{j}", align_bytes=64) for j in range(2)]
         w2_sraw = keep.tile([P, E, H], U8, name="w2_sraw", align_bytes=64)
-        w2_s = keep.tile([P, E, H], U8, name="w2_s", align_bytes=64)
         w1 = keep.tile([P, E, 2 * K], U8, name="w1", align_bytes=64)
         w1_s = keep.tile([P, E, K], U8, name="w1_s", align_bytes=64)
         shared = keep.tile([P, PACK * 2 * C], F32, name="shared", align_bytes=64)
-        gates_first = keep.tile([P, C], F32, name="gates_first")
-        gates_middle = keep.tile([P, 2 * C], F32, name="gates_middle")
-        gates_last = keep.tile([P, C], F32, name="gates_last", tag="held")
-        gates_kept = keep.tile([P, C], F32, name="gates_kept")
-        gates = [gates_first[:], gates_middle[:, 0:C], gates_middle[:, C : 2 * C], gates_last[:]]
+        gates = [keep.tile([P, C], F32, name=f"gates{e}", tag="held" if e == 2 else f"gates{e}", align_bytes=64) for e in range(E)]
+
+        pre_upper = keep.tile([P, 2, C], F32, name="pre_upper", tag="upper")
+        pre_first = [shared[:, 4 * C : 6 * C].rearrange("p (t c) -> p t c", t=2), pre_upper[:]]
 
         nc.vector.memset(w2_sraw[:].bitcast(I32), 0)
         nc.vector.memset(w1_s[:].bitcast(I32), 0)
@@ -72,23 +70,53 @@ def tile_moe_bdx_mlp_silu_kernel(tc, dyT, a, w2_words, w2_scales, w1_words, w1_s
         def load_pre(e):
             nc.sync.dma_start(out=pre[e][:], in_=a_rows[:, :, e * C : (e + 1) * C])
 
-        load_words(w2_raw, w2_words)
-        load_scales(w2_sraw, w2_scales)
-        load_dy(0)
+        blocks = E * C // P
+        gate_rows = keep.tile([P, P], F32, name="gate_rows")
+        gate_columns = keep.tile([P, blocks], F32, name="gate_columns", tag="factor", align_bytes=64)
+        identity = keep.tile([P, P], F32, name="identity")
+        nc.gpsimd.memset(gate_rows[:], 0.0)
         nc.sync.dma_start(out=offsets[:], in_=offs)
-        nc.sync.dma_start(out=gates_first[:], in_=gate[0:P, 0:C])
-        nc.sync.dma_start(out=gates_middle[:], in_=gate[0:P, C : 3 * C])
+        nc.sync.dma_start(out=gate_rows[0:blocks, :], in_=gate[0, :].rearrange("(b c) -> b c", c=P))
+        make_identity(nc, identity[:])
+        turned = psum_h.tile([P, C], F32, name="dh")
+        nc.tensor.transpose(turned[:, 0:P], gate_rows[:], identity[:])
+        nc.scalar.copy(out=gate_columns[:], in_=turned[:, 0:blocks])
+        for e in range(E):
+            spread = psum_x.tile([P, C], F32, name="dx")
+            for j in range(C // P):
+                b = e * C // P + j
+                nc.tensor.transpose(spread[:, j * P : (j + 1) * P], gate_columns[:, b : b + 1].to_broadcast([P, P]), identity[:])
+            nc.scalar.copy(out=gates[e][:], in_=spread[:])
+
+        load_dy(0)
         load_dy(1)
-        load_pre(0)
+        for planes in (LOWER, UPPER):
+            nc.sync.dma_start(out=pre_first[planes == UPPER], in_=a_rows[:, planes, 0:C])
         load_dy(2)
         load_dy(3)
+        load_words(w2_raw[0], w2_words[0:2])
+        load_scales(w2_sraw, w2_scales)
         load_pre(1)
-        nc.sync.dma_start(out=gates_last[:], in_=gate[0:P, 3 * C : 4 * C])
+        load_words(w2_raw[1], w2_words[2:4])
         load_scales(w1_s, w1_scales)
         load_words(w1, w1_words)
         load_pre(2)
-        nc.sync.dma_start(out=gates_kept[:], in_=gate[P : 2 * P, 3 * C : 4 * C])
         load_pre(3)
+
+        w1_of = [w1[:, e, :] for e in range(E)]
+        w1_s_of = [w1_s[:, e, :] for e in range(E)]
+        w2, w2_s = {}, {}
+
+        def permute(engine, target, source):
+            engine.tensor_copy(
+                out=target.rearrange("p e (t m) -> p e t m", t=PACK),
+                in_=source.rearrange("p e (m t) -> p e t m", t=PACK),
+            )
+
+        def permute_late(e, words, scales):
+            permute(nc.gpsimd, scales[:], w2_sraw[:, e : e + 1, :])
+            permute(nc.gpsimd, words[:].bitcast(U16), w2_raw[1][:, e - 2 : e - 1, :].bitcast(U16))
+            w2[e], w2_s[e] = words[:, 0, :], scales[:, 0, :]
 
         def quarter(t):
             return shared[:, 2 * C * t : 2 * C * (t + 1)]
@@ -97,7 +125,7 @@ def tile_moe_bdx_mlp_silu_kernel(tc, dyT, a, w2_words, w2_scales, w1_words, w1_s
             return offsets[:, e * C // LIST_ROWS : (e + 1) * C // LIST_ROWS]
 
         def gather(e, t, plane):
-            nc.vector.tensor_tensor(plane, dy[t][:].indirect(slots(e)), gates[e], ALU.mult)
+            nc.vector.tensor_tensor(plane, dy[t][:].indirect(slots(e)), gates[e][:], ALU.mult)
 
         def interleave(grouped, planes):
             nc.scalar.copy(
@@ -112,28 +140,39 @@ def tile_moe_bdx_mlp_silu_kernel(tc, dyT, a, w2_words, w2_scales, w1_words, w1_s
             return [(codes[:, j * C : (j + 1) * C], scales[:, j * C : (j + 1) * C]) for j in range(operands)]
 
         early = {}
+        halves_of_a = {e: [pre[e][:, LOWER, :], pre[e][:, UPPER, :]] for e in range(1, E)}
+        halves_of_a[0] = pre_first
+        late = dict(halves_of_a)
 
         def function(e, nth, halves=(LOWER, UPPER)):
-            if nth == 0:
-                early[e] = ring.tile([P, PACK, C], F32, name="second")
-            target = early[e] if nth == 0 else pre[e]
+            if nth == 0 and e == 0:
+                early[e] = keep.tile([P, PACK, C], F32, name="early0", tag="factor", align_bytes=64)
+            elif nth == 0:
+                early[e] = ring.tile([P, PACK, C], F32, name="second", bufs=1)
+            elif e == 1:
+                late_second = keep.tile([P, PACK, C], F32, name="late_second", tag="factor", align_bytes=64)
+                late[e] = [late_second[:, LOWER, :], late_second[:, UPPER, :]]
             for planes in halves:
+                target = early[e][:, planes, :] if nth == 0 else late[e][planes == UPPER]
                 if (e + nth) % 2 == 1:
-                    nc.scalar.activation(target[:, planes, :], pre[e][:, planes, :], ACT.Silu, scale=-1.0)
+                    nc.scalar.activation(target, halves_of_a[e][planes == UPPER], ACT.Silu, scale=-1.0)
                 else:
-                    nc.scalar.activation(target[:, planes, :], pre[e][:, planes, :], ACT.Sigmoid)
+                    nc.scalar.activation(target, halves_of_a[e][planes == UPPER], ACT.Sigmoid)
+
+        def one_minus(target, silu):
+            nc.scalar.activation(target, silu, ACT.Identity, bias=1.0, scale=-1.0)
 
         def one_minus_silu(e, halves=(LOWER, UPPER)):
-            silu = early[e] if e % 2 == 1 else pre[e]
             for planes in halves:
-                nc.scalar.activation(silu[:, planes, :], silu[:, planes, :], ACT.Identity, bias=1.0, scale=-1.0)
+                silu = early[e][:, planes, :] if e % 2 == 1 else late[e][planes == UPPER]
+                one_minus(silu, silu)
 
         def product(psum, name, words, scales, e, tile, operand):
             bank = psum.tile([P, C], F32, name=name)
             nc.tensor.matmul_mx(
                 out=bank[:],
-                lhsT=words[:, e, 2 * P * tile : 2 * P * (tile + 1)].bitcast(FP4X4),
-                lhsT_scale=scales[:, e, P * tile : P * (tile + 1)],
+                lhsT=words[e][:, 2 * P * tile : 2 * P * (tile + 1)].bitcast(FP4X4),
+                lhsT_scale=scales[e][:, P * tile : P * (tile + 1)],
                 rhs=operand[0].bitcast(FP8X4),
                 rhs_scale=operand[1],
                 start=True,
@@ -142,94 +181,111 @@ def tile_moe_bdx_mlp_silu_kernel(tc, dyT, a, w2_words, w2_scales, w1_words, w1_s
             return bank
 
         def hidden_gradient(e, g_operand):
-            dh = keep.tile([P, PACK, C], F32, name=f"dh_copy{e}", tag="held" if e > 1 else "g0")
+            dh = keep.tile([P, PACK, C], F32, name=f"dh_copy{e}", tag="held" if e > 1 else "partial", align_bytes=64)
             for t in range(PACK):
                 nc.scalar.copy(out=dh[:, t, :], in_=product(psum_h, "dh", w2, w2_s, e, t, g_operand)[:])
             return dh
 
+        def gate_last(planes):
+            for t in planes:
+                nc.gpsimd.tensor_tensor(g_planes[3][:, t, :], ungated[t], gates[E - 1][:], ALU.mult)
+
+        def da_slot(e):
+            return "da_other" if e == 2 else "da"
+
         def through_silu(e, dh):
-            da = ring.tile([P, PACK, C], BF16, name="da", tag="da", align_bytes=64, bufs=1)
+            da = ring.tile([P, PACK, C], BF16, name="da", tag=da_slot(e), align_bytes=64, bufs=1)
             parts = [(planes, dh[:, planes, :]) for planes in (LOWER, UPPER)]
             if e == 1:
-                held = keep.tile([P, PACK - 1, C], F32, name="u", tag="held")
-                parts = [(LOWER, held[:, 0:2, :]), (slice(2, 3), g_planes[3][:, 0:1, :]), (slice(3, 4), held[:, 2:3, :])]
+                held = keep.tile([P, 2, C], F32, name="u", tag="held", align_bytes=64)
+                parts = [(LOWER, held[:]), (UPPER, g_planes[3][:, LOWER, :])]
             for planes, partial in parts:
-                nc.gpsimd.tensor_tensor(partial, dh[:, planes, :], early[e][:, planes, :], ALU.mult)
+                factor = upper_factor[:] if e == 1 and planes == UPPER else early[e][:, planes, :]
+                nc.gpsimd.tensor_tensor(partial, dh[:, planes, :], factor, ALU.mult)
             for planes, partial in parts:
-                nc.gpsimd.tensor_tensor(da[:, planes, :], partial, pre[e][:, planes, :], ALU.mult)
+                nc.gpsimd.tensor_tensor(da[:, planes, :], partial, late[e][planes == UPPER], ALU.mult)
             if e == 1:
-                nc.gpsimd.tensor_tensor(quarter(0)[:, 0:C], ungated[:], gates_kept[:], ALU.mult)
+                gate_last(range(0, 2))
+                permute_late(
+                    2,
+                    keep.tile([P, 1, 2 * H], U8, name="w2_third", tag="factor", align_bytes=64),
+                    keep.tile([P, 1, H], U8, name="w2_s_third", tag="partial", align_bytes=64),
+                )
             return da
 
         def project(e, m, da_operand):
-            dx = product(psum_x, "dx", w1, w1_s, e, m, da_operand)
+            dx = product(psum_x, "dx", w1_of, w1_s_of, e, m, da_operand)
             if m + 1 < K_TILES:
                 result = ring.tile([P, C], F32, name="result", bufs=K_TILES - 1)
             else:
-                result = ring.tile([P, C], F32, name="result_last", tag="da", align_bytes=64, bufs=1)
-            nc.scalar.copy(out=result[:], in_=dx[:])
-            nc.vector.tensor_copy(window[m][:].indirect(slots(e)), result[:])
+                result = ring.tile([P, (5 if e == 0 else 1) * C], F32, name="result_last", tag=da_slot(e + 1), align_bytes=64, bufs=1)
+                if e == 0:
+                    late[2] = [result[:, j * C : (j + 2) * C].rearrange("p (t c) -> p t c", t=2) for j in (1, 3)]
+            nc.scalar.copy(out=result[:, 0:C], in_=dx[:])
+            nc.vector.tensor_copy(window[m][:].indirect(slots(e)), result[:, 0:C])
             if e == E - 1:
                 nc.sync.dma_start(out=out[m * P : (m + 1) * P, :], in_=window[m][:])
 
         function(0, 0)
         function(0, 1)
-        g_first = keep.tile([P, PACK, C], F32, name="g_first", tag="g0")
+        g_first = keep.tile([P, PACK, C], F32, name="g_first", tag="first", align_bytes=64)
         g_second = keep.tile([P, PACK, C], F32, name="g_second")
-        g_third = keep.tile([P, PACK * C], F32, name="g_third", align_bytes=64)
-        g_planes = [g_first[:], g_second[:], g_third[:].rearrange("p (t c) -> p t c", t=PACK)]
+        g_planes = [g_first[:], g_second[:]]
         g_planes.append(shared[:].rearrange("p (t x) -> p t x", t=PACK)[:, :, 0:C])
-        ungated = keep.tile([P, C], F32, name="ungated")
-        nc.vector.tensor_copy(ungated[:], dy[0][:].indirect(slots(3)))
+        last = keep.tile([P, PACK * 2 * C], F32, name="last", tag="last", align_bytes=64)
+        g_planes.append(last[:].rearrange("p (t x) -> p t x", t=PACK)[:, :, 0:C])
+        ungated_first = keep.tile([P, C], F32, name="ungated_first")
+        nc.vector.tensor_copy(ungated_first[:], dy[0][:].indirect(slots(3)))
         for t in range(PACK):
             gather(0, t, g_first[:, t, :])
             gather(1, t, g_second[:, t, :])
-            if t < 2:
-                gather(2, t, g_third[:, t * C : (t + 1) * C])
+            if t == 0:
+                gather(2, t, quarter(t)[:, 0:C])
 
-        nc.vector.tensor_copy(
-            out=w2_s[:].rearrange("p e (t m) -> p e t m", t=PACK),
-            in_=w2_sraw[:].rearrange("p e (m t) -> p e t m", t=PACK),
-        )
-        nc.vector.tensor_copy(
-            out=w2[:].bitcast(U16).rearrange("p e (t m) -> p e t m", t=PACK),
-            in_=w2_raw[:].bitcast(U16).rearrange("p e (m t) -> p e t m", t=PACK),
-        )
+        w2_early = keep.tile([P, 2, 2 * H], U8, name="w2_early", tag="gates0", align_bytes=64)
+        w2_s_early = keep.tile([P, 2, H], U8, name="w2_s_early", tag="gates1", align_bytes=64)
+        permute(nc.vector, w2_early[:].bitcast(U16), w2_raw[0][:].bitcast(U16))
+        permute(nc.vector, w2_s_early[:], w2_sraw[:, 0:2, :])
+        for e in range(2):
+            w2[e], w2_s[e] = w2_early[:, e, :], w2_s_early[:, e, :]
 
-        minus_d = pre[0][:].rearrange("p t c -> p (t c)")
-        nc.vector.scalar_tensor_tensor(
-            out=minus_d,
-            in0=minus_d,
-            scalar=1.0,
-            in1=early[0][:].rearrange("p t c -> p (t c)"),
-            op0=ALU.subtract,
-            op1=ALU.mult,
-        )
-        grouped_first = g_third[:, 2 * C : 4 * C].bitcast(BF16)
-        interleave(grouped_first, g_planes[0])
-        [g_operand] = quantize(grouped_first, "g")
-        gather(2, 2, g_third[:, 2 * C : 3 * C])
-        gather(2, 3, g_third[:, 3 * C : 4 * C])
+        interleave(quarter(1).bitcast(BF16), g_planes[0])
+        [g_operand] = quantize(quarter(1).bitcast(BF16), "g")
+        gather(2, 1, quarter(1)[:, 0:C])
+        partial_first = keep.tile([P, PACK, C], F32, name="partial_first", tag="partial", align_bytes=64)
         da = ring.tile([P, PACK, C], BF16, name="da", tag="da", align_bytes=64, bufs=1)
         for t in range(PACK):
             nc.vector.scalar_tensor_tensor(
-                out=da[:, t, :],
-                in0=product(psum_h, "dh", w2, w2_s, 0, t, g_operand)[:],
-                scalar=-1.0,
-                in1=minus_d[:, t * C : (t + 1) * C],
-                op0=ALU.mult,
+                out=partial_first[:, t, :],
+                in0=late[0][t // 2][:, t % 2, :],
+                scalar=1.0,
+                in1=product(psum_h, "dh", w2, w2_s, 0, t, g_operand)[:],
+                op0=ALU.subtract,
                 op1=ALU.mult,
             )
+            if t < 2:
+                nc.gpsimd.tensor_tensor(da[:, t, :], partial_first[:, t, :], early[0][:, t, :], ALU.mult)
+        slot_halves = (slice(0, C // 2), slice(C // 2, C))
+        for half in slot_halves:
+            nc.gpsimd.tensor_tensor(da[:, UPPER, half], partial_first[:, UPPER, half], early[0][:, UPPER, half], ALU.mult)
+        ungated_rest = keep.tile([P, PACK - 1, C], F32, name="ungated_rest", tag="upper")
+        ungated = [ungated_first[:]] + [ungated_rest[:, t - 1, :] for t in range(1, PACK)]
+        for t in range(1, PACK):
+            nc.vector.tensor_copy(ungated[t], dy[t][:].indirect(slots(3)))
         function(1, 0)
-        grouped_second = shared[:, 5 * C // 2 : 9 * C // 2].bitcast(BF16)
-        interleave(grouped_second, g_planes[1])
-        [g_operand] = quantize(grouped_second, "g")
+        interleave(quarter(2).bitcast(BF16), g_planes[1])
+        [g_operand] = quantize(quarter(2).bitcast(BF16), "g")
+        gather(2, 2, quarter(2)[:, 0:C])
+        for half in slot_halves:
+            nc.scalar.activation(
+                quarter(3).bitcast(BF16)[:, PACK * half.start : PACK * half.stop].rearrange("p (c i t) -> p c t i", i=RUN, t=PACK),
+                da[:, :, half].rearrange("p t (c i) -> p c t i", i=RUN),
+                ACT.Copy,
+                scale=-1.0,
+            )
         one_minus_silu(1, halves=(LOWER,))
-        gather(3, 1, quarter(1)[:, 0:C])
-        gather(3, 2, quarter(2)[:, 0:C])
-        interleave(quarter(3).bitcast(BF16), da[:])
         [da_operand] = quantize(quarter(3).bitcast(BF16), "da")
-        gather(3, 3, quarter(3)[:, 0:C])
+        gather(2, 3, quarter(3)[:, 0:C])
 
         window = [keep.tile([P, T], F32, name=f"window{m}", tag=f"columns{m}") for m in range(K_TILES)]
         for e in range(E):
@@ -238,7 +294,8 @@ def tile_moe_bdx_mlp_silu_kernel(tc, dyT, a, w2_words, w2_scales, w1_words, w1_s
                 dh = hidden_gradient(e + 1, g_operand)
             project(e, 1, da_operand)
             if e == 0:
-                one_minus_silu(1, halves=(UPPER,))
+                upper_factor = ring.tile([P, 2, C], F32, name="upper_factor", tag="da", align_bytes=64, bufs=1)
+                one_minus(upper_factor[:], early[1][:, UPPER, :])
             elif e + 1 < E:
                 function(e + 1, 1, halves=(UPPER,))
             if e == 1:
@@ -252,12 +309,23 @@ def tile_moe_bdx_mlp_silu_kernel(tc, dyT, a, w2_words, w2_scales, w1_words, w1_s
                 da = through_silu(e + 1, dh)
             if e + 2 < E:
                 function(e + 2, 0)
-                grouped = ring.tile([P, 2, C * PACK], BF16, name="grouped_both", align_bytes=64, bufs=1)
-                interleave(grouped[:, 0], g_planes[e + 2])
-                interleave(grouped[:, 1], da[:])
-                g_operand, next_operand = quantize(grouped[:].rearrange("p a n -> p (a n)"), "both", operands=2)
+                if e == 0:
+                    grouped = last[:, 4 * C : 8 * C].bitcast(BF16)
+                else:
+                    grouped = keep.tile([P, 2 * C * PACK], BF16, name="grouped_both", tag="first", align_bytes=64)[:]
+                interleave(grouped[:, 0 : C * PACK], g_planes[e + 2])
+                interleave(grouped[:, C * PACK : 2 * C * PACK], da[:])
+                g_operand, next_operand = quantize(grouped, "both", operands=2)
+                if e == 0:
+                    gate_last(range(2, PACK))
+                else:
+                    permute_late(
+                        3,
+                        ring.tile([P, 1, 2 * H], U8, name="w2_last", tag="da", align_bytes=64, bufs=1),
+                        keep.tile([P, 1, H], U8, name="w2_s_last", tag="last", align_bytes=64),
+                    )
             elif e + 1 < E:
-                grouped = ring.tile([P, C * PACK], BF16, name="grouped_da", align_bytes=64, bufs=1)
+                grouped = keep.tile([P, C * PACK], BF16, name="grouped_da", tag="first", align_bytes=64)
                 interleave(grouped[:], da[:])
                 [next_operand] = quantize(grouped[:], "da")
             project(e, K_TILES - 1, da_operand)

@@ -113,9 +113,11 @@ def tile_moe_bdx_mlp_silu_kernel(tc, dyT, a, w2_words, w2_scales, w1_words, w1_s
                 in_=source.rearrange("p e (m t) -> p e t m", t=PACK),
             )
 
-        def permute_late(e, words, scales):
-            permute(nc.gpsimd, scales[:], w2_sraw[:, e : e + 1, :])
-            permute(nc.gpsimd, words[:].bitcast(U16), w2_raw[1][:, e - 2 : e - 1, :].bitcast(U16))
+        def permute_late(e, slot):
+            both = keep.tile([P, 1, 3 * H], U8, name=f"w2_late{e}", tag=slot, align_bytes=64)
+            words, scales = both[:, :, 0 : 2 * H], both[:, :, 2 * H : 3 * H]
+            permute(nc.gpsimd, scales, w2_sraw[:, e : e + 1, :])
+            permute(nc.gpsimd, words.bitcast(U16), w2_raw[1][:, e - 2 : e - 1, :].bitcast(U16))
             w2[e], w2_s[e] = words[:, 0, :], scales[:, 0, :]
 
         def quarter(t):
@@ -139,7 +141,7 @@ def tile_moe_bdx_mlp_silu_kernel(tc, dyT, a, w2_words, w2_scales, w1_words, w1_s
             nc.vector.quantize_mx(out=codes[:].bitcast(FP8X4), scales=scales[:], in_=grouped)
             return [(codes[:, j * C : (j + 1) * C], scales[:, j * C : (j + 1) * C]) for j in range(operands)]
 
-        early = {}
+        early, upper_factor = {}, {}
         halves_of_a = {e: [pre[e][:, LOWER, :], pre[e][:, UPPER, :]] for e in range(1, E)}
         halves_of_a[0] = pre_first
         late = dict(halves_of_a)
@@ -148,7 +150,7 @@ def tile_moe_bdx_mlp_silu_kernel(tc, dyT, a, w2_words, w2_scales, w1_words, w1_s
             if nth == 0 and e == 0:
                 early[e] = keep.tile([P, PACK, C], F32, name="early0", tag="factor", align_bytes=64)
             elif nth == 0:
-                early[e] = ring.tile([P, PACK, C], F32, name="second", bufs=1)
+                early[e] = keep.tile([P, PACK, C], F32, name=f"early{e}", tag="upper" if e == 3 else "early")
             elif e == 1:
                 late_second = keep.tile([P, PACK, C], F32, name="late_second", tag="factor", align_bytes=64)
                 late[e] = [late_second[:, LOWER, :], late_second[:, UPPER, :]]
@@ -186,10 +188,6 @@ def tile_moe_bdx_mlp_silu_kernel(tc, dyT, a, w2_words, w2_scales, w1_words, w1_s
                 nc.scalar.copy(out=dh[:, t, :], in_=product(psum_h, "dh", w2, w2_s, e, t, g_operand)[:])
             return dh
 
-        def gate_last(planes):
-            for t in planes:
-                nc.gpsimd.tensor_tensor(g_planes[3][:, t, :], ungated[t], gates[E - 1][:], ALU.mult)
-
         def da_slot(e):
             return "da_other" if e == 2 else "da"
 
@@ -197,20 +195,15 @@ def tile_moe_bdx_mlp_silu_kernel(tc, dyT, a, w2_words, w2_scales, w1_words, w1_s
             da = ring.tile([P, PACK, C], BF16, name="da", tag=da_slot(e), align_bytes=64, bufs=1)
             parts = [(planes, dh[:, planes, :]) for planes in (LOWER, UPPER)]
             if e == 1:
-                held = keep.tile([P, 2, C], F32, name="u", tag="held", align_bytes=64)
-                parts = [(LOWER, held[:]), (UPPER, g_planes[3][:, LOWER, :])]
+                held = keep.tile([P, PACK, C], F32, name="u", tag="held", align_bytes=64)
+                parts = [(planes, held[:, planes, :]) for planes in (LOWER, UPPER)]
             for planes, partial in parts:
-                factor = upper_factor[:] if e == 1 and planes == UPPER else early[e][:, planes, :]
+                factor = upper_factor[e] if e % 2 == 1 and planes == UPPER else early[e][:, planes, :]
                 nc.gpsimd.tensor_tensor(partial, dh[:, planes, :], factor, ALU.mult)
             for planes, partial in parts:
                 nc.gpsimd.tensor_tensor(da[:, planes, :], partial, late[e][planes == UPPER], ALU.mult)
             if e == 1:
-                gate_last(range(0, 2))
-                permute_late(
-                    2,
-                    keep.tile([P, 1, 2 * H], U8, name="w2_third", tag="factor", align_bytes=64),
-                    keep.tile([P, 1, H], U8, name="w2_s_third", tag="partial", align_bytes=64),
-                )
+                permute_late(2, "factor")
             return da
 
         def project(e, m, da_operand):
@@ -218,9 +211,11 @@ def tile_moe_bdx_mlp_silu_kernel(tc, dyT, a, w2_words, w2_scales, w1_words, w1_s
             if m + 1 < K_TILES:
                 result = ring.tile([P, C], F32, name="result", bufs=K_TILES - 1)
             else:
-                result = ring.tile([P, (5 if e == 0 else 1) * C], F32, name="result_last", tag=da_slot(e + 1), align_bytes=64, bufs=1)
-                if e == 0:
-                    late[2] = [result[:, j * C : (j + 2) * C].rearrange("p (t c) -> p t c", t=2) for j in (1, 3)]
+                result = ring.tile([P, (1 + 2 * (2, 3, 0, 0)[e]) * C], F32, name="result_last", tag=da_slot(e + 1), align_bytes=64, bufs=1)
+                if e < 2:
+                    late[e + 2] = [result[:, j * C : (j + 2) * C].rearrange("p (t c) -> p t c", t=2) for j in (1, 3)]
+                if e == 1:
+                    upper_factor[3] = result[:, 5 * C : 7 * C].rearrange("p (t c) -> p t c", t=2)
             nc.scalar.copy(out=result[:, 0:C], in_=dx[:])
             nc.vector.tensor_copy(window[m][:].indirect(slots(e)), result[:, 0:C])
             if e == E - 1:
@@ -232,8 +227,6 @@ def tile_moe_bdx_mlp_silu_kernel(tc, dyT, a, w2_words, w2_scales, w1_words, w1_s
         g_second = keep.tile([P, PACK, C], F32, name="g_second")
         g_planes = [g_first[:], g_second[:]]
         g_planes.append(shared[:].rearrange("p (t x) -> p t x", t=PACK)[:, :, 0:C])
-        last = keep.tile([P, PACK * 2 * C], F32, name="last", tag="last", align_bytes=64)
-        g_planes.append(last[:].rearrange("p (t x) -> p t x", t=PACK)[:, :, 0:C])
         ungated_first = keep.tile([P, C], F32, name="ungated_first")
         nc.vector.tensor_copy(ungated_first[:], dy[0][:].indirect(slots(3)))
         for t in range(PACK):
@@ -294,8 +287,8 @@ def tile_moe_bdx_mlp_silu_kernel(tc, dyT, a, w2_words, w2_scales, w1_words, w1_s
                 dh = hidden_gradient(e + 1, g_operand)
             project(e, 1, da_operand)
             if e == 0:
-                upper_factor = ring.tile([P, 2, C], F32, name="upper_factor", tag="da", align_bytes=64, bufs=1)
-                one_minus(upper_factor[:], early[1][:, UPPER, :])
+                upper_factor[1] = ring.tile([P, 2, C], F32, name="upper_factor", tag="da", align_bytes=64, bufs=1)[:]
+                one_minus(upper_factor[1], early[1][:, UPPER, :])
             elif e + 1 < E:
                 function(e + 1, 1, halves=(UPPER,))
             if e == 1:
@@ -309,28 +302,25 @@ def tile_moe_bdx_mlp_silu_kernel(tc, dyT, a, w2_words, w2_scales, w1_words, w1_s
                 da = through_silu(e + 1, dh)
             if e + 2 < E:
                 function(e + 2, 0)
-                if e == 0:
-                    grouped = last[:, 4 * C : 8 * C].bitcast(BF16)
-                else:
-                    grouped = keep.tile([P, 2 * C * PACK], BF16, name="grouped_both", tag="first", align_bytes=64)[:]
+                grouped = keep.tile([P, 2 * C * PACK], BF16, name="grouped_both", tag="last" if e == 0 else "first", align_bytes=64)[:]
                 interleave(grouped[:, 0 : C * PACK], g_planes[e + 2])
                 interleave(grouped[:, C * PACK : 2 * C * PACK], da[:])
                 g_operand, next_operand = quantize(grouped, "both", operands=2)
                 if e == 0:
-                    gate_last(range(2, PACK))
+                    g_last = keep.tile([P, PACK, C], F32, name="g_last", tag="last", align_bytes=64)
+                    for t in range(PACK):
+                        nc.gpsimd.tensor_tensor(g_last[:, t, :], ungated[t], gates[E - 1][:], ALU.mult)
+                    g_planes.append(g_last[:])
                 else:
-                    permute_late(
-                        3,
-                        ring.tile([P, 1, 2 * H], U8, name="w2_last", tag="da", align_bytes=64, bufs=1),
-                        keep.tile([P, 1, H], U8, name="w2_s_last", tag="last", align_bytes=64),
-                    )
+                    permute_late(3, "first")
             elif e + 1 < E:
                 grouped = keep.tile([P, C * PACK], BF16, name="grouped_da", tag="first", align_bytes=64)
                 interleave(grouped[:], da[:])
                 [next_operand] = quantize(grouped[:], "da")
             project(e, K_TILES - 1, da_operand)
             if e == 1:
-                one_minus_silu(3)
+                one_minus_silu(3, halves=(LOWER,))
+                one_minus(upper_factor[3], early[3][:, UPPER, :])
             if e + 2 < E:
                 function(e + 2, 1, halves=(LOWER,))
             da_operand = next_operand

@@ -42,11 +42,11 @@ def tile_moe_bdx_mlp_silu_kernel(tc, dyT, a, w2_words, w2_scales, w1_words, w1_s
         w2_sraw = keep.tile([P, E, H], U8, name="w2_sraw", align_bytes=64)
         w1 = keep.tile([P, E, 2 * K], U8, name="w1", align_bytes=64)
         w1_s = keep.tile([P, E, K], U8, name="w1_s", align_bytes=64)
-        shared = keep.tile([P, PACK * 2 * C], F32, name="shared", align_bytes=64)
+        shared = keep.tile([P, PACK * PACK * C], F32, name="shared", align_bytes=64)
         gates = [keep.tile([P, C], F32, name=f"gates{e}", tag="held" if e == 2 else f"gates{e}", align_bytes=64) for e in range(E)]
 
-        pre_upper = keep.tile([P, 2, C], F32, name="pre_upper", tag="upper")
-        pre_first = [shared[:, 4 * C : 6 * C].rearrange("p (t c) -> p t c", t=2), pre_upper[:]]
+        pre_lower = keep.tile([P, 2, C], F32, name="pre_lower", tag="first", align_bytes=64)
+        pre_first = [pre_lower[:], shared[:, 14 * C : 16 * C].rearrange("p (t c) -> p t c", t=2)]
 
         nc.vector.memset(w2_sraw[:].bitcast(I32), 0)
         nc.vector.memset(w1_s[:].bitcast(I32), 0)
@@ -67,8 +67,8 @@ def tile_moe_bdx_mlp_silu_kernel(tc, dyT, a, w2_words, w2_scales, w1_words, w1_s
         def load_dy(t):
             nc.sync.dma_start(out=dy[t][:], in_=dy_rows[:, t, :])
 
-        def load_pre(e):
-            nc.sync.dma_start(out=pre[e][:], in_=a_rows[:, :, e * C : (e + 1) * C])
+        def load_pre(e, planes=slice(0, PACK)):
+            nc.sync.dma_start(out=pre[e][:, planes, :], in_=a_rows[:, planes, e * C : (e + 1) * C])
 
         blocks = E * C // P
         gate_rows = keep.tile([P, P], F32, name="gate_rows")
@@ -95,8 +95,9 @@ def tile_moe_bdx_mlp_silu_kernel(tc, dyT, a, w2_words, w2_scales, w1_words, w1_s
         load_dy(2)
         load_dy(3)
         load_words(w2_raw[0], w2_words[0:2])
+        load_pre(1, LOWER)
         load_scales(w2_sraw, w2_scales)
-        load_pre(1)
+        load_pre(1, UPPER)
         load_words(w2_raw[1], w2_words[2:4])
         load_scales(w1_s, w1_scales)
         load_words(w1, w1_words)
@@ -113,21 +114,21 @@ def tile_moe_bdx_mlp_silu_kernel(tc, dyT, a, w2_words, w2_scales, w1_words, w1_s
                 in_=source.rearrange("p e (m t) -> p e t m", t=PACK),
             )
 
-        def permute_late(e, slot):
-            both = keep.tile([P, 1, 3 * H], U8, name=f"w2_late{e}", tag=slot, align_bytes=64)
+        def permute_late(e, pool, slot):
+            both = pool.tile([P, 1, 3 * H], U8, name=f"w2_late{e}", tag=slot, align_bytes=64, bufs=1)
             words, scales = both[:, :, 0 : 2 * H], both[:, :, 2 * H : 3 * H]
             permute(nc.gpsimd, scales, w2_sraw[:, e : e + 1, :])
             permute(nc.gpsimd, words.bitcast(U16), w2_raw[1][:, e - 2 : e - 1, :].bitcast(U16))
             w2[e], w2_s[e] = words[:, 0, :], scales[:, 0, :]
 
         def quarter(t):
-            return shared[:, 2 * C * t : 2 * C * (t + 1)]
+            return shared[:, PACK * C * t : PACK * C * (t + 1)]
 
-        def slots(e):
-            return offsets[:, e * C // LIST_ROWS : (e + 1) * C // LIST_ROWS]
+        def slots(e, part=slice(0, C)):
+            return offsets[:, (e * C + part.start) // LIST_ROWS : (e * C + part.stop) // LIST_ROWS]
 
-        def gather(e, t, plane):
-            nc.vector.tensor_tensor(plane, dy[t][:].indirect(slots(e)), gates[e][:], ALU.mult)
+        def gather(e, t, plane, part=slice(0, C)):
+            nc.vector.tensor_tensor(plane[:, part], dy[t][:].indirect(slots(e, part)), gates[e][:, part], ALU.mult)
 
         def interleave(grouped, planes):
             nc.scalar.copy(
@@ -135,8 +136,9 @@ def tile_moe_bdx_mlp_silu_kernel(tc, dyT, a, w2_words, w2_scales, w1_words, w1_s
                 in_=planes.rearrange("p t (c i) -> p c t i", i=RUN),
             )
 
-        def quantize(grouped, kind, operands=1):
-            codes = ring.tile([P, operands * C], U32, name=f"codes_{kind}", align_bytes=64)
+        def quantize(grouped, kind, operands=1, slot=None):
+            pool = ring if slot is None else keep
+            codes = pool.tile([P, operands * C], U32, name=f"codes_{kind}", tag=slot or f"codes_{kind}", align_bytes=64)
             scales = ring.tile([P, operands * C], U8, name=f"scales_{kind}", align_bytes=64)
             nc.vector.quantize_mx(out=codes[:].bitcast(FP8X4), scales=scales[:], in_=grouped)
             return [(codes[:, j * C : (j + 1) * C], scales[:, j * C : (j + 1) * C]) for j in range(operands)]
@@ -150,7 +152,7 @@ def tile_moe_bdx_mlp_silu_kernel(tc, dyT, a, w2_words, w2_scales, w1_words, w1_s
             if nth == 0 and e == 0:
                 early[e] = keep.tile([P, PACK, C], F32, name="early0", tag="factor", align_bytes=64)
             elif nth == 0:
-                early[e] = keep.tile([P, PACK, C], F32, name=f"early{e}", tag="upper" if e == 3 else "early")
+                early[e] = keep.tile([P, PACK, C], F32, name=f"early{e}", tag="upper" if e == 3 else "early", align_bytes=64)
             elif e == 1:
                 late_second = keep.tile([P, PACK, C], F32, name="late_second", tag="factor", align_bytes=64)
                 late[e] = [late_second[:, LOWER, :], late_second[:, UPPER, :]]
@@ -188,6 +190,9 @@ def tile_moe_bdx_mlp_silu_kernel(tc, dyT, a, w2_words, w2_scales, w1_words, w1_s
                 nc.scalar.copy(out=dh[:, t, :], in_=product(psum_h, "dh", w2, w2_s, e, t, g_operand)[:])
             return dh
 
+        def gate_last(t):
+            nc.gpsimd.tensor_tensor(g_planes[3][:, t, :], ungated[t], gates[E - 1][:], ALU.mult)
+
         def da_slot(e):
             return "da_other" if e == 2 else "da"
 
@@ -195,15 +200,16 @@ def tile_moe_bdx_mlp_silu_kernel(tc, dyT, a, w2_words, w2_scales, w1_words, w1_s
             da = ring.tile([P, PACK, C], BF16, name="da", tag=da_slot(e), align_bytes=64, bufs=1)
             parts = [(planes, dh[:, planes, :]) for planes in (LOWER, UPPER)]
             if e == 1:
-                held = keep.tile([P, PACK, C], F32, name="u", tag="held", align_bytes=64)
-                parts = [(planes, held[:, planes, :]) for planes in (LOWER, UPPER)]
+                held = keep.tile([P, 2, C], F32, name="u", tag="held", align_bytes=64)
+                parts = [(LOWER, held[:]), (UPPER, g_planes[3][:, LOWER, :])]
             for planes, partial in parts:
-                factor = upper_factor[e] if e % 2 == 1 and planes == UPPER else early[e][:, planes, :]
+                factor = upper_factor[e] if e == 3 and planes == UPPER else early[e][:, planes, :]
                 nc.gpsimd.tensor_tensor(partial, dh[:, planes, :], factor, ALU.mult)
             for planes, partial in parts:
                 nc.gpsimd.tensor_tensor(da[:, planes, :], partial, late[e][planes == UPPER], ALU.mult)
             if e == 1:
-                permute_late(2, "factor")
+                gate_last(0)
+                permute_late(2, keep, "factor")
             return da
 
         def project(e, m, da_operand):
@@ -221,16 +227,19 @@ def tile_moe_bdx_mlp_silu_kernel(tc, dyT, a, w2_words, w2_scales, w1_words, w1_s
             if e == E - 1:
                 nc.sync.dma_start(out=out[m * P : (m + 1) * P, :], in_=window[m][:])
 
+        slot_halves = (slice(0, C // 2), slice(C // 2, C))
         function(0, 0)
         function(0, 1)
-        g_first = keep.tile([P, PACK, C], F32, name="g_first", tag="first", align_bytes=64)
-        g_second = keep.tile([P, PACK, C], F32, name="g_second")
-        g_planes = [g_first[:], g_second[:]]
+        g_first, g_second = [quarter(j).rearrange("p (t c) -> p t c", t=PACK) for j in (1, 2)]
+        g_planes = [g_first, g_second]
         g_planes.append(shared[:].rearrange("p (t x) -> p t x", t=PACK)[:, :, 0:C])
-        ungated_first = keep.tile([P, C], F32, name="ungated_first")
-        nc.vector.tensor_copy(ungated_first[:], dy[0][:].indirect(slots(3)))
+        last = keep.tile([P, (PACK + 1) * C], F32, name="last", align_bytes=64)
+        g_planes.append(last[:, 0 : PACK * C].rearrange("p (t c) -> p t c", t=PACK))
+        ungated_first = quarter(0)[:, C : 2 * C]
+        nc.vector.tensor_copy(ungated_first, dy[0][:].indirect(slots(3)))
         for t in range(PACK):
-            gather(0, t, g_first[:, t, :])
+            for part in slot_halves if t == PACK - 1 else (slice(0, C),):
+                gather(0, t, g_first[:, t, :], part)
             gather(1, t, g_second[:, t, :])
             if t == 0:
                 gather(2, t, quarter(t)[:, 0:C])
@@ -242,11 +251,14 @@ def tile_moe_bdx_mlp_silu_kernel(tc, dyT, a, w2_words, w2_scales, w1_words, w1_s
         for e in range(2):
             w2[e], w2_s[e] = w2_early[:, e, :], w2_s_early[:, e, :]
 
-        interleave(quarter(1).bitcast(BF16), g_planes[0])
-        [g_operand] = quantize(quarter(1).bitcast(BF16), "g")
+        grouped_first = quarter(0)[:, 2 * C : 4 * C].bitcast(BF16)
+        for half in slot_halves:
+            interleave(grouped_first[:, PACK * half.start : PACK * half.stop], g_first[:, :, half])
+        [g_operand] = quantize(grouped_first, "g", slot="upper")
         gather(2, 1, quarter(1)[:, 0:C])
         partial_first = keep.tile([P, PACK, C], F32, name="partial_first", tag="partial", align_bytes=64)
-        da = ring.tile([P, PACK, C], BF16, name="da", tag="da", align_bytes=64, bufs=1)
+        da = quarter(3)[:, 0 : 2 * C].bitcast(BF16).rearrange("p (t c) -> p t c", t=PACK)
+        grouped_da = quarter(3)[:, 2 * C : 4 * C].bitcast(BF16)
         for t in range(PACK):
             nc.vector.scalar_tensor_tensor(
                 out=partial_first[:, t, :],
@@ -258,26 +270,26 @@ def tile_moe_bdx_mlp_silu_kernel(tc, dyT, a, w2_words, w2_scales, w1_words, w1_s
             )
             if t < 2:
                 nc.gpsimd.tensor_tensor(da[:, t, :], partial_first[:, t, :], early[0][:, t, :], ALU.mult)
-        slot_halves = (slice(0, C // 2), slice(C // 2, C))
         for half in slot_halves:
             nc.gpsimd.tensor_tensor(da[:, UPPER, half], partial_first[:, UPPER, half], early[0][:, UPPER, half], ALU.mult)
-        ungated_rest = keep.tile([P, PACK - 1, C], F32, name="ungated_rest", tag="upper")
-        ungated = [ungated_first[:]] + [ungated_rest[:, t - 1, :] for t in range(1, PACK)]
+        ungated_rest = keep.tile([P, PACK - 1, C], F32, name="ungated_rest", tag="upper", align_bytes=64)
+        ungated = [ungated_first] + [ungated_rest[:, t - 1, :] for t in range(1, PACK)]
         for t in range(1, PACK):
             nc.vector.tensor_copy(ungated[t], dy[t][:].indirect(slots(3)))
         function(1, 0)
-        interleave(quarter(2).bitcast(BF16), g_planes[1])
-        [g_operand] = quantize(quarter(2).bitcast(BF16), "g")
+        one_minus_silu(1)
+        grouped_second = keep.tile([P, C * PACK], BF16, name="grouped_second", tag="first", align_bytes=64)
+        interleave(grouped_second[:], g_planes[1])
+        [g_operand] = quantize(grouped_second[:], "g")
         gather(2, 2, quarter(2)[:, 0:C])
         for half in slot_halves:
             nc.scalar.activation(
-                quarter(3).bitcast(BF16)[:, PACK * half.start : PACK * half.stop].rearrange("p (c i t) -> p c t i", i=RUN, t=PACK),
+                grouped_da[:, PACK * half.start : PACK * half.stop].rearrange("p (c i t) -> p c t i", i=RUN, t=PACK),
                 da[:, :, half].rearrange("p t (c i) -> p c t i", i=RUN),
                 ACT.Copy,
                 scale=-1.0,
             )
-        one_minus_silu(1, halves=(LOWER,))
-        [da_operand] = quantize(quarter(3).bitcast(BF16), "da")
+        [da_operand] = quantize(grouped_da, "da")
         gather(2, 3, quarter(3)[:, 0:C])
 
         window = [keep.tile([P, T], F32, name=f"window{m}", tag=f"columns{m}") for m in range(K_TILES)]
@@ -286,11 +298,8 @@ def tile_moe_bdx_mlp_silu_kernel(tc, dyT, a, w2_words, w2_scales, w1_words, w1_s
             if e + 1 < E:
                 dh = hidden_gradient(e + 1, g_operand)
             project(e, 1, da_operand)
-            if e == 0:
-                upper_factor[1] = ring.tile([P, 2, C], F32, name="upper_factor", tag="da", align_bytes=64, bufs=1)[:]
-                one_minus(upper_factor[1], early[1][:, UPPER, :])
-            elif e + 1 < E:
-                function(e + 1, 1, halves=(UPPER,))
+            if e == 2:
+                function(3, 1, halves=(UPPER,))
             if e == 1:
                 one_minus_silu(2)
             project(e, 2, da_operand)
@@ -302,25 +311,28 @@ def tile_moe_bdx_mlp_silu_kernel(tc, dyT, a, w2_words, w2_scales, w1_words, w1_s
                 da = through_silu(e + 1, dh)
             if e + 2 < E:
                 function(e + 2, 0)
-                grouped = keep.tile([P, 2 * C * PACK], BF16, name="grouped_both", tag="last" if e == 0 else "first", align_bytes=64)[:]
-                interleave(grouped[:, 0 : C * PACK], g_planes[e + 2])
-                interleave(grouped[:, C * PACK : 2 * C * PACK], da[:])
-                g_operand, next_operand = quantize(grouped, "both", operands=2)
                 if e == 0:
-                    g_last = keep.tile([P, PACK, C], F32, name="g_last", tag="last", align_bytes=64)
-                    for t in range(PACK):
-                        nc.gpsimd.tensor_tensor(g_last[:, t, :], ungated[t], gates[E - 1][:], ALU.mult)
-                    g_planes.append(g_last[:])
+                    grouped = last[:, C : (PACK + 1) * C].bitcast(BF16)
                 else:
-                    permute_late(3, "first")
+                    grouped = keep.tile([P, 2 * C * PACK], BF16, name="grouped_both", tag="first", align_bytes=64)[:]
+                interleave(grouped[:, C * PACK : 2 * C * PACK], g_planes[e + 2])
+                interleave(grouped[:, 0 : C * PACK], da[:])
+                next_operand, g_operand = quantize(grouped, "both", operands=2)
+                if e == 0:
+                    for t in range(1, PACK):
+                        gate_last(t)
             elif e + 1 < E:
                 grouped = keep.tile([P, C * PACK], BF16, name="grouped_da", tag="first", align_bytes=64)
                 interleave(grouped[:], da[:])
                 [next_operand] = quantize(grouped[:], "da")
+            if e == 1:
+                permute_late(3, ring, "da")
             project(e, K_TILES - 1, da_operand)
             if e == 1:
                 one_minus_silu(3, halves=(LOWER,))
                 one_minus(upper_factor[3], early[3][:, UPPER, :])
-            if e + 2 < E:
-                function(e + 2, 1, halves=(LOWER,))
+            if e == 0:
+                function(2, 1)
+            if e == 1:
+                function(3, 1, halves=(LOWER,))
             da_operand = next_operand

@@ -46,7 +46,8 @@ def tile_moe_bdx_mlp_silu_kernel(tc, dyT, a, w2_words, w2_scales, w1_words, w1_s
         gates = [keep.tile([P, C], F32, name=f"gates{e}", tag="held" if e == 2 else f"gates{e}", align_bytes=64) for e in range(E)]
 
         pre_lower = keep.tile([P, 2, C], F32, name="pre_lower", tag="first", align_bytes=64)
-        pre_first = [pre_lower[:], shared[:, 14 * C : 16 * C].rearrange("p (t c) -> p t c", t=2)]
+        pre_upper = keep.tile([P, 2, C], F32, name="pre_upper", tag="upper_a", align_bytes=64)
+        pre_first = [pre_lower[:], pre_upper[:]]
 
         nc.vector.memset(w2_sraw[:].bitcast(I32), 0)
         nc.vector.memset(w1_s[:].bitcast(I32), 0)
@@ -93,10 +94,10 @@ def tile_moe_bdx_mlp_silu_kernel(tc, dyT, a, w2_words, w2_scales, w1_words, w1_s
         for planes in (LOWER, UPPER):
             nc.sync.dma_start(out=pre_first[planes == UPPER], in_=a_rows[:, planes, 0:C])
         load_dy(2)
+        load_scales(w2_sraw, w2_scales)
         load_dy(3)
         load_words(w2_raw[0], w2_words[0:2])
         load_pre(1, LOWER)
-        load_scales(w2_sraw, w2_scales)
         load_pre(1, UPPER)
         load_words(w2_raw[1], w2_words[2:4])
         load_scales(w1_s, w1_scales)
@@ -115,11 +116,9 @@ def tile_moe_bdx_mlp_silu_kernel(tc, dyT, a, w2_words, w2_scales, w1_words, w1_s
             )
 
         def permute_late(e, pool, slot):
-            both = pool.tile([P, 1, 3 * H], U8, name=f"w2_late{e}", tag=slot, align_bytes=64, bufs=1)
-            words, scales = both[:, :, 0 : 2 * H], both[:, :, 2 * H : 3 * H]
-            permute(nc.gpsimd, scales, w2_sraw[:, e : e + 1, :])
-            permute(nc.gpsimd, words.bitcast(U16), w2_raw[1][:, e - 2 : e - 1, :].bitcast(U16))
-            w2[e], w2_s[e] = words[:, 0, :], scales[:, 0, :]
+            words = pool.tile([P, 1, 2 * H], U8, name=f"w2_late{e}", tag=slot, align_bytes=64, bufs=1)
+            permute(nc.gpsimd, words[:].bitcast(U16), w2_raw[1][:, e - 2 : e - 1, :].bitcast(U16))
+            w2[e] = words[:, 0, :]
 
         def quarter(t):
             return shared[:, PACK * C * t : PACK * C * (t + 1)]
@@ -138,7 +137,7 @@ def tile_moe_bdx_mlp_silu_kernel(tc, dyT, a, w2_words, w2_scales, w1_words, w1_s
 
         def quantize(grouped, kind, operands=1, slot=None):
             pool = ring if slot is None else keep
-            codes = pool.tile([P, operands * C], U32, name=f"codes_{kind}", tag=slot or f"codes_{kind}", align_bytes=64)
+            codes = pool.tile([P, operands * C], U32, name=f"codes_{kind}", tag=slot or f"codes_{kind}", align_bytes=64, bufs=2 if kind == "both" else 1)
             scales = ring.tile([P, operands * C], U8, name=f"scales_{kind}", align_bytes=64)
             nc.vector.quantize_mx(out=codes[:].bitcast(FP8X4), scales=scales[:], in_=grouped)
             return [(codes[:, j * C : (j + 1) * C], scales[:, j * C : (j + 1) * C]) for j in range(operands)]
@@ -258,7 +257,7 @@ def tile_moe_bdx_mlp_silu_kernel(tc, dyT, a, w2_words, w2_scales, w1_words, w1_s
         gather(2, 1, quarter(1)[:, 0:C])
         partial_first = keep.tile([P, PACK, C], F32, name="partial_first", tag="partial", align_bytes=64)
         da = quarter(3)[:, 0 : 2 * C].bitcast(BF16).rearrange("p (t c) -> p t c", t=PACK)
-        grouped_da = quarter(3)[:, 2 * C : 4 * C].bitcast(BF16)
+        grouped_da = keep.tile([P, C * PACK], BF16, name="grouped_da_first", tag="upper_a", align_bytes=64)[:]
         for t in range(PACK):
             nc.vector.scalar_tensor_tensor(
                 out=partial_first[:, t, :],
@@ -291,6 +290,10 @@ def tile_moe_bdx_mlp_silu_kernel(tc, dyT, a, w2_words, w2_scales, w1_words, w1_s
             )
         [da_operand] = quantize(grouped_da, "da")
         gather(2, 3, quarter(3)[:, 0:C])
+        w2_s_late = keep.tile([P, 2, H], U8, name="w2_s_late", tag="upper_a", align_bytes=64)
+        permute(nc.vector, w2_s_late[:], w2_sraw[:, 2:4, :])
+        for e in range(2, E):
+            w2_s[e] = w2_s_late[:, e - 2, :]
 
         window = [keep.tile([P, T], F32, name=f"window{m}", tag=f"columns{m}") for m in range(K_TILES)]
         for e in range(E):

@@ -46,7 +46,7 @@ def tile_moe_bdx_mlp_silu_kernel(tc, dyT, a, w2_words, w2_scales, w1_words, w1_s
         gates = [keep.tile([P, C], F32, name=f"gates{e}", tag="held" if e == 2 else f"gates{e}", align_bytes=64) for e in range(E)]
 
         pre_lower = keep.tile([P, 2, C], F32, name="pre_lower", tag="first", align_bytes=64)
-        pre_upper = keep.tile([P, 2, C], F32, name="pre_upper", tag="upper_a", align_bytes=64)
+        pre_upper = keep.tile([P, 2, C], F32, name="pre_upper")
         pre_first = [pre_lower[:], pre_upper[:]]
 
         nc.vector.memset(w2_sraw[:].bitcast(I32), 0)
@@ -94,9 +94,9 @@ def tile_moe_bdx_mlp_silu_kernel(tc, dyT, a, w2_words, w2_scales, w1_words, w1_s
         for planes in (LOWER, UPPER):
             nc.sync.dma_start(out=pre_first[planes == UPPER], in_=a_rows[:, planes, 0:C])
         load_dy(2)
-        load_scales(w2_sraw, w2_scales)
         load_dy(3)
         load_words(w2_raw[0], w2_words[0:2])
+        load_scales(w2_sraw, w2_scales)
         load_pre(1, LOWER)
         load_pre(1, UPPER)
         load_words(w2_raw[1], w2_words[2:4])
@@ -229,7 +229,7 @@ def tile_moe_bdx_mlp_silu_kernel(tc, dyT, a, w2_words, w2_scales, w1_words, w1_s
         slot_halves = (slice(0, C // 2), slice(C // 2, C))
         function(0, 0)
         function(0, 1)
-        g_first, g_second = [quarter(j).rearrange("p (t c) -> p t c", t=PACK) for j in (1, 2)]
+        g_second, g_first = [quarter(j).rearrange("p (t c) -> p t c", t=PACK) for j in (1, 2)]
         g_planes = [g_first, g_second]
         g_planes.append(shared[:].rearrange("p (t x) -> p t x", t=PACK)[:, :, 0:C])
         last = keep.tile([P, (PACK + 1) * C], F32, name="last", align_bytes=64)
@@ -244,33 +244,37 @@ def tile_moe_bdx_mlp_silu_kernel(tc, dyT, a, w2_words, w2_scales, w1_words, w1_s
                 gather(2, t, quarter(t)[:, 0:C])
 
         w2_early = keep.tile([P, 2, 2 * H], U8, name="w2_early", tag="gates0", align_bytes=64)
-        w2_s_early = keep.tile([P, 2, H], U8, name="w2_s_early", tag="gates1", align_bytes=64)
+        w2_s_early = keep.tile([P, E, H], U8, name="w2_s_early", tag="gates1", align_bytes=64)
         permute(nc.vector, w2_early[:].bitcast(U16), w2_raw[0][:].bitcast(U16))
-        permute(nc.vector, w2_s_early[:], w2_sraw[:, 0:2, :])
+        permute(nc.vector, w2_s_early[:], w2_sraw[:])
+        for e in range(E):
+            w2_s[e] = w2_s_early[:, e, :]
         for e in range(2):
-            w2[e], w2_s[e] = w2_early[:, e, :], w2_s_early[:, e, :]
+            w2[e] = w2_early[:, e, :]
 
         grouped_first = quarter(0)[:, 2 * C : 4 * C].bitcast(BF16)
         for half in slot_halves:
             interleave(grouped_first[:, PACK * half.start : PACK * half.stop], g_first[:, :, half])
         [g_operand] = quantize(grouped_first, "g", slot="upper")
-        gather(2, 1, quarter(1)[:, 0:C])
-        partial_first = keep.tile([P, PACK, C], F32, name="partial_first", tag="partial", align_bytes=64)
+        minus_d = quarter(2)[:, 2 * C : 4 * C].rearrange("p (t c) -> p t c", t=2)
+        nc.vector.scalar_tensor_tensor(
+            out=minus_d, in0=late[0][1], scalar=1.0, in1=early[0][:, UPPER, :], op0=ALU.subtract, op1=ALU.mult
+        )
+        partial_first = keep.tile([P, 2, C], F32, name="partial_first", tag="partial", align_bytes=64)
         da = quarter(3)[:, 0 : 2 * C].bitcast(BF16).rearrange("p (t c) -> p t c", t=PACK)
-        grouped_da = keep.tile([P, C * PACK], BF16, name="grouped_da_first", tag="upper_a", align_bytes=64)[:]
-        for t in range(PACK):
+        grouped_da = quarter(2)[:, 0 : 2 * C].bitcast(BF16)
+        for t in range(2):
             nc.vector.scalar_tensor_tensor(
                 out=partial_first[:, t, :],
-                in0=late[0][t // 2][:, t % 2, :],
+                in0=late[0][0][:, t, :],
                 scalar=1.0,
                 in1=product(psum_h, "dh", w2, w2_s, 0, t, g_operand)[:],
                 op0=ALU.subtract,
                 op1=ALU.mult,
             )
-            if t < 2:
-                nc.gpsimd.tensor_tensor(da[:, t, :], partial_first[:, t, :], early[0][:, t, :], ALU.mult)
-        for half in slot_halves:
-            nc.gpsimd.tensor_tensor(da[:, UPPER, half], partial_first[:, UPPER, half], early[0][:, UPPER, half], ALU.mult)
+            nc.gpsimd.tensor_tensor(da[:, t, :], partial_first[:, t, :], early[0][:, t, :], ALU.mult)
+        for t in range(2, PACK):
+            nc.vector.tensor_tensor(da[:, t, :], product(psum_h, "dh", w2, w2_s, 0, t, g_operand)[:], minus_d[:, t - 2, :], ALU.mult)
         ungated_rest = keep.tile([P, PACK - 1, C], F32, name="ungated_rest", tag="upper", align_bytes=64)
         ungated = [ungated_first] + [ungated_rest[:, t - 1, :] for t in range(1, PACK)]
         for t in range(1, PACK):
@@ -280,20 +284,16 @@ def tile_moe_bdx_mlp_silu_kernel(tc, dyT, a, w2_words, w2_scales, w1_words, w1_s
         grouped_second = keep.tile([P, C * PACK], BF16, name="grouped_second", tag="first", align_bytes=64)
         interleave(grouped_second[:], g_planes[1])
         [g_operand] = quantize(grouped_second[:], "g")
-        gather(2, 2, quarter(2)[:, 0:C])
-        for half in slot_halves:
-            nc.scalar.activation(
-                grouped_da[:, PACK * half.start : PACK * half.stop].rearrange("p (c i t) -> p c t i", i=RUN, t=PACK),
-                da[:, :, half].rearrange("p t (c i) -> p c t i", i=RUN),
-                ACT.Copy,
-                scale=-1.0,
-            )
+        gather(2, 1, quarter(1)[:, 0:C])
+        nc.scalar.activation(
+            grouped_da.rearrange("p (c i t) -> p c t i", i=RUN, t=PACK),
+            da.rearrange("p t (c i) -> p c t i", i=RUN),
+            ACT.Copy,
+            scale=-1.0,
+        )
         [da_operand] = quantize(grouped_da, "da")
         gather(2, 3, quarter(3)[:, 0:C])
-        w2_s_late = keep.tile([P, 2, H], U8, name="w2_s_late", tag="upper_a", align_bytes=64)
-        permute(nc.vector, w2_s_late[:], w2_sraw[:, 2:4, :])
-        for e in range(2, E):
-            w2_s[e] = w2_s_late[:, e - 2, :]
+        gather(2, 2, quarter(2)[:, 0:C])
 
         window = [keep.tile([P, T], F32, name=f"window{m}", tag=f"columns{m}") for m in range(K_TILES)]
         for e in range(E):

@@ -11,6 +11,8 @@ LIST_ROWS = 16
 QUADRANTS, QUADRANT_ROWS, SCALE_ROWS = 4, 32, 4
 RUN = 4
 LOWER, UPPER = slice(0, 2), slice(2, 4)
+ALL_SLOTS = slice(0, C)
+SLOT_HALVES = (slice(0, C // 2), slice(C // 2, C))
 
 F32 = mybir.dt.float32
 BF16 = mybir.dt.bfloat16
@@ -27,7 +29,9 @@ FLOPS = 2 * E * C * (N * H + H * K)
 BYTES = 4 * (N * T + H * E * C + E * C + K * T) + 2 * E * C + E * (N * H + H * K) * 17 // 32
 
 
-def tile_moe_bdx_mlp_silu_kernel(tc, dyT, a, w2_words, w2_scales, w1_words, w1_scales, gate, offs, out):
+def tile_moe_bdx_mlp_silu_kernel(
+    tc, dyT, a, w2_words, w2_scales, w1_words, w1_scales, gate, offs, out
+):
     nc = tc.nc
     with ExitStack() as ctx:
         keep = ctx.enter_context(tc.tile_pool(name="keep", bufs=1))
@@ -43,11 +47,13 @@ def tile_moe_bdx_mlp_silu_kernel(tc, dyT, a, w2_words, w2_scales, w1_words, w1_s
         w1 = keep.tile([P, E, 2 * K], U8, name="w1", align_bytes=64)
         w1_s = keep.tile([P, E, K], U8, name="w1_s", align_bytes=64)
         shared = keep.tile([P, PACK * PACK * C], F32, name="shared", align_bytes=64)
-        gates = [keep.tile([P, C], F32, name=f"gates{e}", tag="held" if e == 2 else f"gates{e}", align_bytes=64) for e in range(E)]
+        gates = [
+            keep.tile([P, C], F32, name=f"gates{e}", tag="held" if e == 2 else f"gates{e}", align_bytes=64)
+            for e in range(E)
+        ]
 
         pre_lower = keep.tile([P, 2, C], F32, name="pre_lower", tag="first", align_bytes=64)
-        pre_upper = keep.tile([P, 2, C], F32, name="pre_upper")
-        pre_first = [pre_lower[:], pre_upper[:]]
+        pre_first = [pre_lower[:], shared[:, 2 * C : 4 * C].rearrange("p (t c) -> p t c", t=2)]
 
         nc.vector.memset(w2_sraw[:].bitcast(I32), 0)
         nc.vector.memset(w1_s[:].bitcast(I32), 0)
@@ -86,7 +92,8 @@ def tile_moe_bdx_mlp_silu_kernel(tc, dyT, a, w2_words, w2_scales, w1_words, w1_s
             spread = psum_x.tile([P, C], F32, name="dx")
             for j in range(C // P):
                 b = e * C // P + j
-                nc.tensor.transpose(spread[:, j * P : (j + 1) * P], gate_columns[:, b : b + 1].to_broadcast([P, P]), identity[:])
+                column = gate_columns[:, b : b + 1].to_broadcast([P, P])
+                nc.tensor.transpose(spread[:, j * P : (j + 1) * P], column, identity[:])
             nc.scalar.copy(out=gates[e][:], in_=spread[:])
 
         load_dy(0)
@@ -123,10 +130,13 @@ def tile_moe_bdx_mlp_silu_kernel(tc, dyT, a, w2_words, w2_scales, w1_words, w1_s
         def quarter(t):
             return shared[:, PACK * C * t : PACK * C * (t + 1)]
 
-        def slots(e, part=slice(0, C)):
+        def two_planes(run):
+            return run.rearrange("p (t c) -> p t c", t=2)
+
+        def slots(e, part=ALL_SLOTS):
             return offsets[:, (e * C + part.start) // LIST_ROWS : (e * C + part.stop) // LIST_ROWS]
 
-        def gather(e, t, plane, part=slice(0, C)):
+        def gather(e, t, plane, part=ALL_SLOTS):
             nc.vector.tensor_tensor(plane[:, part], dy[t][:].indirect(slots(e, part)), gates[e][:, part], ALU.mult)
 
         def interleave(grouped, planes):
@@ -137,21 +147,24 @@ def tile_moe_bdx_mlp_silu_kernel(tc, dyT, a, w2_words, w2_scales, w1_words, w1_s
 
         def quantize(grouped, kind, operands=1, slot=None):
             pool = ring if slot is None else keep
-            codes = pool.tile([P, operands * C], U32, name=f"codes_{kind}", tag=slot or f"codes_{kind}", align_bytes=64, bufs=2 if kind == "both" else 1)
+            depth = 2 if operands > 1 else 1
+            codes = pool.tile(
+                [P, operands * C], U32, name=f"codes_{kind}", tag=slot or f"codes_{kind}", align_bytes=64, bufs=depth
+            )
             scales = ring.tile([P, operands * C], U8, name=f"scales_{kind}", align_bytes=64)
             nc.vector.quantize_mx(out=codes[:].bitcast(FP8X4), scales=scales[:], in_=grouped)
             return [(codes[:, j * C : (j + 1) * C], scales[:, j * C : (j + 1) * C]) for j in range(operands)]
 
-        early, upper_factor = {}, {}
+        early, early_upper = {}, {}
         halves_of_a = {e: [pre[e][:, LOWER, :], pre[e][:, UPPER, :]] for e in range(1, E)}
         halves_of_a[0] = pre_first
         late = dict(halves_of_a)
 
         def function(e, nth, halves=(LOWER, UPPER)):
-            if nth == 0 and e == 0:
-                early[e] = keep.tile([P, PACK, C], F32, name="early0", tag="factor", align_bytes=64)
-            elif nth == 0:
-                early[e] = keep.tile([P, PACK, C], F32, name=f"early{e}", tag="upper" if e == 3 else "early", align_bytes=64)
+            if nth == 0:
+                slot = ("factor", "early", "early", "upper")[e]
+                early[e] = keep.tile([P, PACK, C], F32, name=f"early{e}", tag=slot, align_bytes=64)
+                early_upper[e] = early[e][:, UPPER, :]
             elif e == 1:
                 late_second = keep.tile([P, PACK, C], F32, name="late_second", tag="factor", align_bytes=64)
                 late[e] = [late_second[:, LOWER, :], late_second[:, UPPER, :]]
@@ -202,7 +215,7 @@ def tile_moe_bdx_mlp_silu_kernel(tc, dyT, a, w2_words, w2_scales, w1_words, w1_s
                 held = keep.tile([P, 2, C], F32, name="u", tag="held", align_bytes=64)
                 parts = [(LOWER, held[:]), (UPPER, g_planes[3][:, LOWER, :])]
             for planes, partial in parts:
-                factor = upper_factor[e] if e == 3 and planes == UPPER else early[e][:, planes, :]
+                factor = early_upper[e] if planes == UPPER else early[e][:, LOWER, :]
                 nc.gpsimd.tensor_tensor(partial, dh[:, planes, :], factor, ALU.mult)
             for planes, partial in parts:
                 nc.gpsimd.tensor_tensor(da[:, planes, :], partial, late[e][planes == UPPER], ALU.mult)
@@ -216,17 +229,19 @@ def tile_moe_bdx_mlp_silu_kernel(tc, dyT, a, w2_words, w2_scales, w1_words, w1_s
             if m + 1 < K_TILES:
                 result = ring.tile([P, C], F32, name="result", bufs=K_TILES - 1)
             else:
-                result = ring.tile([P, (1 + 2 * (2, 3, 0, 0)[e]) * C], F32, name="result_last", tag=da_slot(e + 1), align_bytes=64, bufs=1)
+                guests = (2, 3, 0, 0)[e]
+                result = ring.tile(
+                    [P, (1 + 2 * guests) * C], F32, name="result_last", tag=da_slot(e + 1), align_bytes=64, bufs=1
+                )
                 if e < 2:
-                    late[e + 2] = [result[:, j * C : (j + 2) * C].rearrange("p (t c) -> p t c", t=2) for j in (1, 3)]
+                    late[e + 2] = [two_planes(result[:, j * C : (j + 2) * C]) for j in (1, 3)]
                 if e == 1:
-                    upper_factor[3] = result[:, 5 * C : 7 * C].rearrange("p (t c) -> p t c", t=2)
+                    early_upper[3] = two_planes(result[:, 5 * C : 7 * C])
             nc.scalar.copy(out=result[:, 0:C], in_=dx[:])
             nc.vector.tensor_copy(window[m][:].indirect(slots(e)), result[:, 0:C])
             if e == E - 1:
                 nc.sync.dma_start(out=out[m * P : (m + 1) * P, :], in_=window[m][:])
 
-        slot_halves = (slice(0, C // 2), slice(C // 2, C))
         function(0, 0)
         function(0, 1)
         g_second, g_first = [quarter(j).rearrange("p (t c) -> p t c", t=PACK) for j in (1, 2)]
@@ -237,29 +252,31 @@ def tile_moe_bdx_mlp_silu_kernel(tc, dyT, a, w2_words, w2_scales, w1_words, w1_s
         ungated_first = quarter(0)[:, C : 2 * C]
         nc.vector.tensor_copy(ungated_first, dy[0][:].indirect(slots(3)))
         for t in range(PACK):
-            for part in slot_halves if t == PACK - 1 else (slice(0, C),):
+            for part in SLOT_HALVES if t == PACK - 1 else (ALL_SLOTS,):
                 gather(0, t, g_first[:, t, :], part)
             gather(1, t, g_second[:, t, :])
             if t == 0:
                 gather(2, t, quarter(t)[:, 0:C])
 
         w2_early = keep.tile([P, 2, 2 * H], U8, name="w2_early", tag="gates0", align_bytes=64)
-        w2_s_early = keep.tile([P, E, H], U8, name="w2_s_early", tag="gates1", align_bytes=64)
+        w2_s_early = keep.tile([P, 2, H], U8, name="w2_s_early", tag="gates1", align_bytes=64)
         permute(nc.vector, w2_early[:].bitcast(U16), w2_raw[0][:].bitcast(U16))
-        permute(nc.vector, w2_s_early[:], w2_sraw[:])
-        for e in range(E):
-            w2_s[e] = w2_s_early[:, e, :]
+        permute(nc.vector, w2_s_early[:], w2_sraw[:, 0:2, :])
         for e in range(2):
-            w2[e] = w2_early[:, e, :]
+            w2[e], w2_s[e] = w2_early[:, e, :], w2_s_early[:, e, :]
 
-        grouped_first = quarter(0)[:, 2 * C : 4 * C].bitcast(BF16)
-        for half in slot_halves:
+        grouped_first = keep.tile([P, C * PACK], BF16, name="grouped_first", tag="grouped", align_bytes=64)[:]
+        for half in SLOT_HALVES:
             interleave(grouped_first[:, PACK * half.start : PACK * half.stop], g_first[:, :, half])
         [g_operand] = quantize(grouped_first, "g", slot="upper")
-        minus_d = quarter(2)[:, 2 * C : 4 * C].rearrange("p (t c) -> p t c", t=2)
+        minus_d = two_planes(quarter(2)[:, 2 * C : 4 * C])
         nc.vector.scalar_tensor_tensor(
             out=minus_d, in0=late[0][1], scalar=1.0, in1=early[0][:, UPPER, :], op0=ALU.subtract, op1=ALU.mult
         )
+        w2_s_late = keep.tile([P, 2, H], U8, name="w2_s_late", tag="grouped", align_bytes=64)
+        permute(nc.vector, w2_s_late[:], w2_sraw[:, 2:4, :])
+        for e in range(2, E):
+            w2_s[e] = w2_s_late[:, e - 2, :]
         partial_first = keep.tile([P, 2, C], F32, name="partial_first", tag="partial", align_bytes=64)
         da = quarter(3)[:, 0 : 2 * C].bitcast(BF16).rearrange("p (t c) -> p t c", t=PACK)
         grouped_da = quarter(2)[:, 0 : 2 * C].bitcast(BF16)
@@ -274,7 +291,8 @@ def tile_moe_bdx_mlp_silu_kernel(tc, dyT, a, w2_words, w2_scales, w1_words, w1_s
             )
             nc.gpsimd.tensor_tensor(da[:, t, :], partial_first[:, t, :], early[0][:, t, :], ALU.mult)
         for t in range(2, PACK):
-            nc.vector.tensor_tensor(da[:, t, :], product(psum_h, "dh", w2, w2_s, 0, t, g_operand)[:], minus_d[:, t - 2, :], ALU.mult)
+            dh_plane = product(psum_h, "dh", w2, w2_s, 0, t, g_operand)
+            nc.vector.tensor_tensor(da[:, t, :], dh_plane[:], minus_d[:, t - 2, :], ALU.mult)
         ungated_rest = keep.tile([P, PACK - 1, C], F32, name="ungated_rest", tag="upper", align_bytes=64)
         ungated = [ungated_first] + [ungated_rest[:, t - 1, :] for t in range(1, PACK)]
         for t in range(1, PACK):
@@ -317,7 +335,8 @@ def tile_moe_bdx_mlp_silu_kernel(tc, dyT, a, w2_words, w2_scales, w1_words, w1_s
                 if e == 0:
                     grouped = last[:, C : (PACK + 1) * C].bitcast(BF16)
                 else:
-                    grouped = keep.tile([P, 2 * C * PACK], BF16, name="grouped_both", tag="first", align_bytes=64)[:]
+                    both = keep.tile([P, 2 * C * PACK], BF16, name="grouped_both", tag="first", align_bytes=64)
+                    grouped = both[:]
                 interleave(grouped[:, C * PACK : 2 * C * PACK], g_planes[e + 2])
                 interleave(grouped[:, 0 : C * PACK], da[:])
                 next_operand, g_operand = quantize(grouped, "both", operands=2)
@@ -333,9 +352,8 @@ def tile_moe_bdx_mlp_silu_kernel(tc, dyT, a, w2_words, w2_scales, w1_words, w1_s
             project(e, K_TILES - 1, da_operand)
             if e == 1:
                 one_minus_silu(3, halves=(LOWER,))
-                one_minus(upper_factor[3], early[3][:, UPPER, :])
+                one_minus(early_upper[3], early[3][:, UPPER, :])
+                function(3, 1, halves=(LOWER,))
             if e == 0:
                 function(2, 1)
-            if e == 1:
-                function(3, 1, halves=(LOWER,))
             da_operand = next_operand

@@ -9,6 +9,7 @@ PACK = 4
 K_TILES = K // P
 LIST_ROWS = 16
 QUADRANTS, QUADRANT_ROWS, SCALE_ROWS = 4, 32, 4
+PAIR = 2
 RUN = 4
 LOWER, UPPER = slice(0, 2), slice(2, 4)
 ALL_SLOTS = slice(0, C)
@@ -37,23 +38,21 @@ def tile_moe_bdx_mlp_silu_kernel(
         keep = ctx.enter_context(tc.tile_pool(name="keep", bufs=1))
         ring = ctx.enter_context(tc.tile_pool(name="ring", bufs=2))
         psum_h = ctx.enter_context(tc.psum_pool(name="psum_h", bufs=4))
-        psum_x = ctx.enter_context(tc.psum_pool(name="psum_x", bufs=4))
+        psum_x = ctx.enter_context(tc.psum_pool(name="psum_x", bufs=2))
 
         offsets = keep.tile([P, E * C // LIST_ROWS], U16, name="offsets")
         dy = [keep.tile([P, T], F32, name=f"dy{t}", tag=f"columns{t}") for t in range(PACK)]
-        pre = {e: keep.tile([P, PACK, C], F32, name=f"pre{e}") for e in range(1, E)}
-        w2_raw = [keep.tile([P, 2, 2 * H], U8, name=f"w2_raw{j}", align_bytes=64) for j in range(2)]
+        pre = [keep.tile([P, PACK, C], F32, name=f"pre{e}") for e in range(E)]
+        w2_raw = keep.tile([P, E, 2 * H], U8, name="w2_raw", align_bytes=64)
         w2_sraw = keep.tile([P, E, H], U8, name="w2_sraw", align_bytes=64)
         w1 = keep.tile([P, E, 2 * K], U8, name="w1", align_bytes=64)
         w1_s = keep.tile([P, E, K], U8, name="w1_s", align_bytes=64)
-        shared = keep.tile([P, PACK * PACK * C], F32, name="shared", align_bytes=64)
-        gates = [
-            keep.tile([P, C], F32, name=f"gates{e}", tag="held" if e == 2 else f"gates{e}", align_bytes=64)
-            for e in range(E)
-        ]
-
-        pre_lower = keep.tile([P, 2, C], F32, name="pre_lower", tag="first", align_bytes=64)
-        pre_first = [pre_lower[:], shared[:, 2 * C : 4 * C].rearrange("p (t c) -> p t c", t=2)]
+        gates_early = keep.tile([P, (E - 1) * C], F32, name="gates_early", align_bytes=64)
+        gates_last = keep.tile([P, C], F32, name="gates_last", align_bytes=64)
+        gates = [gates_early[:, e * C : (e + 1) * C] for e in range(E - 1)] + [gates_last[:]]
+        shared = keep.tile([P, 9 * C], F32, name="shared", align_bytes=64)
+        ungated = shared[:, 0 : 4 * C].rearrange("p (t c) -> p t c", t=PACK)
+        first_part, middle_part, last_part = [shared[:, j * C : (j + 2) * C] for j in (3, 5, 7)]
 
         nc.vector.memset(w2_sraw[:].bitcast(I32), 0)
         nc.vector.memset(w1_s[:].bitcast(I32), 0)
@@ -79,7 +78,7 @@ def tile_moe_bdx_mlp_silu_kernel(
 
         blocks = E * C // P
         gate_rows = keep.tile([P, P], F32, name="gate_rows")
-        gate_columns = keep.tile([P, blocks], F32, name="gate_columns", tag="factor", align_bytes=64)
+        gate_columns = keep.tile([P, blocks], F32, name="gate_columns")
         identity = keep.tile([P, P], F32, name="identity")
         nc.gpsimd.memset(gate_rows[:], 0.0)
         nc.sync.dma_start(out=offsets[:], in_=offs)
@@ -87,273 +86,227 @@ def tile_moe_bdx_mlp_silu_kernel(
         make_identity(nc, identity[:])
         turned = psum_h.tile([P, C], F32, name="dh")
         nc.tensor.transpose(turned[:, 0:P], gate_rows[:], identity[:])
-        nc.scalar.copy(out=gate_columns[:], in_=turned[:, 0:blocks])
+        nc.vector.tensor_copy(gate_columns[:], turned[:, 0:blocks])
         for e in range(E):
-            spread = psum_x.tile([P, C], F32, name="dx")
+            spread = psum_x.tile([P, C], F32, name="spread", tag=("dx_vector", "dx_scalar")[e % 2])
             for j in range(C // P):
                 b = e * C // P + j
                 column = gate_columns[:, b : b + 1].to_broadcast([P, P])
                 nc.tensor.transpose(spread[:, j * P : (j + 1) * P], column, identity[:])
-            nc.scalar.copy(out=gates[e][:], in_=spread[:])
+            nc.vector.tensor_copy(gates[e], spread[:])
 
-        load_dy(0)
+        load_pre(0, LOWER)
+        for half in (slice(0, T // 2), slice(T // 2, T)):
+            nc.sync.dma_start(out=dy[0][:, half], in_=dy_rows[:, 0, half])
+        load_pre(0, UPPER)
         load_dy(1)
-        for planes in (LOWER, UPPER):
-            nc.sync.dma_start(out=pre_first[planes == UPPER], in_=a_rows[:, planes, 0:C])
         load_dy(2)
+        load_pre(3)
         load_dy(3)
-        load_words(w2_raw[0], w2_words[0:2])
+        load_pre(2)
+        load_words(w2_raw, w2_words)
         load_scales(w2_sraw, w2_scales)
-        load_pre(1, LOWER)
-        load_pre(1, UPPER)
-        load_words(w2_raw[1], w2_words[2:4])
+        load_pre(1)
         load_scales(w1_s, w1_scales)
         load_words(w1, w1_words)
-        load_pre(2)
-        load_pre(3)
 
         w1_of = [w1[:, e, :] for e in range(E)]
         w1_s_of = [w1_s[:, e, :] for e in range(E)]
         w2, w2_s = {}, {}
 
-        def permute(engine, target, source):
-            engine.tensor_copy(
-                out=target.rearrange("p e (t m) -> p e t m", t=PACK),
-                in_=source.rearrange("p e (m t) -> p e t m", t=PACK),
-            )
-
-        def permute_late(e, pool, slot):
-            words = pool.tile([P, 1, 2 * H], U8, name=f"w2_late{e}", tag=slot, align_bytes=64, bufs=1)
-            permute(nc.gpsimd, words[:].bitcast(U16), w2_raw[1][:, e - 2 : e - 1, :].bitcast(U16))
-            w2[e] = words[:, 0, :]
-
-        def quarter(t):
-            return shared[:, PACK * C * t : PACK * C * (t + 1)]
-
-        def two_planes(run):
-            return run.rearrange("p (t c) -> p t c", t=2)
+        def permute(first, slot):
+            both = keep.tile([P, 6 * H], U8, name=f"w2_from{first}", tag=slot, align_bytes=64)
+            words = both[:, 0 : 4 * H].rearrange("p (e n) -> p e n", e=2)
+            scales = both[:, 4 * H : 6 * H].rearrange("p (e n) -> p e n", e=2)
+            pair = slice(first, first + 2)
+            for target, source in (
+                (words.bitcast(U16), w2_raw[:, pair, :].bitcast(U16)),
+                (scales, w2_sraw[:, pair, :]),
+            ):
+                nc.vector.tensor_copy(
+                    out=target.rearrange("p e (t m) -> p e t m", t=PACK),
+                    in_=source.rearrange("p e (m t) -> p e t m", t=PACK),
+                )
+            for j in range(2):
+                w2[first + j], w2_s[first + j] = words[:, j, :], scales[:, j, :]
 
         def slots(e, part=ALL_SLOTS):
             return offsets[:, (e * C + part.start) // LIST_ROWS : (e * C + part.stop) // LIST_ROWS]
 
-        def gather(e, t, plane, part=ALL_SLOTS):
-            nc.vector.tensor_tensor(plane[:, part], dy[t][:].indirect(slots(e, part)), gates[e][:, part], ALU.mult)
+        g_early = keep.tile([P, PACK, (E - 1) * C], F32, name="g_early")
+        g_planes = [g_early[:, :, e * C : (e + 1) * C] for e in range(E - 1)]
 
-        def interleave(grouped, planes):
-            nc.scalar.copy(
+        def gather(first, count, t):
+            run = slice(first * C, (first + count) * C)
+            nc.vector.tensor_tensor(g_early[:, t, run], dy[t][:].indirect(slots(0, run)), gates_early[:, run], ALU.mult)
+
+        def gather_last(t):
+            nc.scalar.activation(ungated[:, t, :], dy[t][:].indirect(slots(E - 1)), ACT.Copy)
+
+        def interleave(copy, grouped, planes):
+            copy(
                 out=grouped.rearrange("p (c i t) -> p c t i", i=RUN, t=PACK),
                 in_=planes.rearrange("p t (c i) -> p c t i", i=RUN),
             )
 
-        def quantize(grouped, kind, operands=1, slot=None):
-            pool = ring if slot is None else keep
-            depth = 2 if operands > 1 else 1
-            codes = pool.tile(
-                [P, operands * C], U32, name=f"codes_{kind}", tag=slot or f"codes_{kind}", align_bytes=64, bufs=depth
-            )
+        def quantize(grouped, kind, operands=1):
+            codes = ring.tile([P, operands * C], U32, name=f"codes_{kind}", align_bytes=64)
             scales = ring.tile([P, operands * C], U8, name=f"scales_{kind}", align_bytes=64)
-            nc.vector.quantize_mx(out=codes[:].bitcast(FP8X4), scales=scales[:], in_=grouped)
+            nc.vector.quantize_mx(out=codes[:].bitcast(FP8X4), scales=scales[:], in_=grouped.bitcast(BF16))
             return [(codes[:, j * C : (j + 1) * C], scales[:, j * C : (j + 1) * C]) for j in range(operands)]
 
-        early, early_upper = {}, {}
-        halves_of_a = {e: [pre[e][:, LOWER, :], pre[e][:, UPPER, :]] for e in range(1, E)}
-        halves_of_a[0] = pre_first
-        late = dict(halves_of_a)
-
-        def function(e, nth, halves=(LOWER, UPPER)):
-            if nth == 0:
-                slot = ("factor", "early", "early", "upper")[e]
-                early[e] = keep.tile([P, PACK, C], F32, name=f"early{e}", tag=slot, align_bytes=64)
-                early_upper[e] = early[e][:, UPPER, :]
-            elif e == 1:
-                late_second = keep.tile([P, PACK, C], F32, name="late_second", tag="factor", align_bytes=64)
-                late[e] = [late_second[:, LOWER, :], late_second[:, UPPER, :]]
-            for planes in halves:
-                target = early[e][:, planes, :] if nth == 0 else late[e][planes == UPPER]
-                if (e + nth) % 2 == 1:
-                    nc.scalar.activation(target, halves_of_a[e][planes == UPPER], ACT.Silu, scale=-1.0)
-                else:
-                    nc.scalar.activation(target, halves_of_a[e][planes == UPPER], ACT.Sigmoid)
-
-        def one_minus(target, silu):
-            nc.scalar.activation(target, silu, ACT.Identity, bias=1.0, scale=-1.0)
-
-        def one_minus_silu(e, halves=(LOWER, UPPER)):
-            for planes in halves:
-                silu = early[e][:, planes, :] if e % 2 == 1 else late[e][planes == UPPER]
-                one_minus(silu, silu)
-
-        def product(psum, name, words, scales, e, tile, operand):
-            bank = psum.tile([P, C], F32, name=name)
+        def product(target, words, scales, tile, operand, part):
             nc.tensor.matmul_mx(
-                out=bank[:],
-                lhsT=words[e][:, 2 * P * tile : 2 * P * (tile + 1)].bitcast(FP4X4),
-                lhsT_scale=scales[e][:, P * tile : P * (tile + 1)],
-                rhs=operand[0].bitcast(FP8X4),
-                rhs_scale=operand[1],
+                out=target,
+                lhsT=words[:, 2 * P * tile : 2 * P * (tile + 1)].bitcast(FP4X4),
+                lhsT_scale=scales[:, P * tile : P * (tile + 1)],
+                rhs=operand[0][:, part].bitcast(FP8X4),
+                rhs_scale=operand[1][:, part],
                 start=True,
                 stop=True,
             )
-            return bank
 
         def hidden_gradient(e, g_operand):
-            dh = keep.tile([P, PACK, C], F32, name=f"dh_copy{e}", tag="held" if e > 1 else "partial", align_bytes=64)
-            for t in range(PACK):
-                nc.scalar.copy(out=dh[:, t, :], in_=product(psum_h, "dh", w2, w2_s, e, t, g_operand)[:])
-            return dh
+            banks = []
+            for j in range(C // P):
+                bank = psum_h.tile([P, C], F32, name="dh")
+                for t in range(PACK):
+                    product(bank[:, t * P : (t + 1) * P], w2[e], w2_s[e], t, g_operand, slice(j * P, (j + 1) * P))
+                banks.append(bank)
+            return banks
 
-        def gate_last(t):
-            nc.gpsimd.tensor_tensor(g_planes[3][:, t, :], ungated[t], gates[E - 1][:], ALU.mult)
-
-        def da_slot(e):
-            return "da_other" if e == 2 else "da"
-
-        def through_silu(e, dh):
-            da = ring.tile([P, PACK, C], BF16, name="da", tag=da_slot(e), align_bytes=64, bufs=1)
-            parts = [(planes, dh[:, planes, :]) for planes in (LOWER, UPPER)]
-            if e == 1:
-                held = keep.tile([P, 2, C], F32, name="u", tag="held", align_bytes=64)
-                parts = [(LOWER, held[:]), (UPPER, g_planes[3][:, LOWER, :])]
-            for planes, partial in parts:
-                factor = early_upper[e] if planes == UPPER else early[e][:, LOWER, :]
-                nc.gpsimd.tensor_tensor(partial, dh[:, planes, :], factor, ALU.mult)
-            for planes, partial in parts:
-                nc.gpsimd.tensor_tensor(da[:, planes, :], partial, late[e][planes == UPPER], ALU.mult)
-            if e == 1:
-                gate_last(0)
-                permute_late(2, keep, "factor")
-            return da
-
-        def project(e, m, da_operand):
-            dx = product(psum_x, "dx", w1_of, w1_s_of, e, m, da_operand)
-            if m + 1 < K_TILES:
-                result = ring.tile([P, C], F32, name="result", bufs=K_TILES - 1)
-            else:
-                guests = (2, 3, 0, 0)[e]
-                result = ring.tile(
-                    [P, (1 + 2 * guests) * C], F32, name="result_last", tag=da_slot(e + 1), align_bytes=64, bufs=1
+        def through_silu(banks, slope, grouped):
+            for j, bank in enumerate(banks):
+                nc.vector.tensor_tensor(
+                    grouped.bitcast(BF16)[:, j * C : (j + 1) * C].rearrange("p (c i t) -> p c t i", i=PAIR, t=PACK),
+                    bank[:].rearrange("p (t c i) -> p c t i", i=PAIR, t=PACK),
+                    slope[:, :, j * P : (j + 1) * P].rearrange("p t (c i) -> p c t i", i=PAIR),
+                    ALU.mult,
                 )
-                if e < 2:
-                    late[e + 2] = [two_planes(result[:, j * C : (j + 2) * C]) for j in (1, 3)]
-                if e == 1:
-                    early_upper[3] = two_planes(result[:, 5 * C : 7 * C])
-            nc.scalar.copy(out=result[:, 0:C], in_=dx[:])
-            nc.vector.tensor_copy(window[m][:].indirect(slots(e)), result[:, 0:C])
+
+        def sigmoid(target, e, halves=(LOWER, UPPER)):
+            for planes in halves:
+                nc.scalar.activation(target[:, planes, :], pre[e][:, planes, :], ACT.Sigmoid)
+
+        def silu(target, e):
+            for planes in (LOWER, UPPER):
+                nc.scalar.activation(target[:, planes, :], pre[e][:, planes, :], ACT.Silu, scale=-1.0)
+
+        def slope_on_gpsimd(e):
+            rest = middle_part.rearrange("p (t c) -> p t c", t=2)
+            for planes in (LOWER, UPPER):
+                nc.gpsimd.tensor_scalar(rest, silus[e][:, planes, :], -1.0, 1.0, ALU.mult, ALU.add)
+                nc.gpsimd.tensor_tensor(slopes[e][:, planes, :], slopes[e][:, planes, :], rest, ALU.mult)
+
+        window = {}
+
+        def emptied(engine, e, m, da_operand, held=None):
+            name = "vector" if engine is nc.vector else "scalar"
+            dx = psum_x.tile([P, C], F32, name="dx", tag=f"dx_{name}")
+            product(dx[:], w1_of[e], w1_s_of[e], m, da_operand, ALL_SLOTS)
+            result = held
+            if held is None:
+                result = ring.tile([P, C], F32, name="result", tag=f"result_{name}", bufs=3)[:]
+            if engine is nc.vector:
+                nc.vector.tensor_copy(result, dx[:])
+            else:
+                nc.scalar.copy(out=result, in_=dx[:])
+            return result
+
+        def scatter(engine, e, m, result, part=ALL_SLOTS):
+            if m not in window:
+                window[m] = keep.tile([P, T], F32, name=f"window{m}", tag=f"columns{m}")
+            if engine is nc.vector:
+                nc.vector.tensor_copy(window[m][:].indirect(slots(e, part)), result[:, part])
+            else:
+                for half in SLOT_HALVES:
+                    nc.scalar.activation(window[m][:].indirect(slots(e, half)), result[:, half], ACT.Copy)
             if e == E - 1:
-                nc.sync.dma_start(out=out[m * P : (m + 1) * P, :], in_=window[m][:])
+                queue = nc.sync if engine is nc.vector else nc.scalar
+                queue.dma_start(out=out[m * P : (m + 1) * P, :], in_=window[m][:])
 
-        function(0, 0)
-        function(0, 1)
-        g_second, g_first = [quarter(j).rearrange("p (t c) -> p t c", t=PACK) for j in (1, 2)]
-        g_planes = [g_first, g_second]
-        g_planes.append(shared[:].rearrange("p (t x) -> p t x", t=PACK)[:, :, 0:C])
-        last = keep.tile([P, (PACK + 1) * C], F32, name="last", align_bytes=64)
-        g_planes.append(last[:, 0 : PACK * C].rearrange("p (t c) -> p t c", t=PACK))
-        ungated_first = quarter(0)[:, C : 2 * C]
-        nc.vector.tensor_copy(ungated_first, dy[0][:].indirect(slots(3)))
-        for t in range(PACK):
-            for part in SLOT_HALVES if t == PACK - 1 else (ALL_SLOTS,):
-                gather(0, t, g_first[:, t, :], part)
-            gather(1, t, g_second[:, t, :])
-            if t == 0:
-                gather(2, t, quarter(t)[:, 0:C])
+        def project(engine, e, tiles, da_operand):
+            waiting = None
+            for m in tiles:
+                result = emptied(engine, e, m, da_operand)
+                if waiting is not None:
+                    scatter(engine, e, *waiting)
+                waiting = (m, result)
+            scatter(engine, e, *waiting)
 
-        w2_early = keep.tile([P, 2, 2 * H], U8, name="w2_early", tag="gates0", align_bytes=64)
-        w2_s_early = keep.tile([P, 2, H], U8, name="w2_s_early", tag="gates1", align_bytes=64)
-        permute(nc.vector, w2_early[:].bitcast(U16), w2_raw[0][:].bitcast(U16))
-        permute(nc.vector, w2_s_early[:], w2_sraw[:, 0:2, :])
-        for e in range(2):
-            w2[e], w2_s[e] = w2_early[:, e, :], w2_s_early[:, e, :]
+        slopes = {0: keep.tile([P, PACK, C], F32, name="slope0")}
+        silus = {0: pre[0]}
+        sigmoid(slopes[0], 0, halves=(LOWER,))
+        gather_last(0)
+        sigmoid(slopes[0], 0, halves=(UPPER,))
+        silu(silus[0], 0)
+        gather_last(1)
+        gather_last(2)
+        for t in range(PACK - 1):
+            gather(0, E - 1, t)
+        gather(0, 1, PACK - 1)
+        gather(1, 2, PACK - 1)
+        for e in (3, 2, 1):
+            silus[e] = keep.tile([P, PACK, C], F32, name=f"silu{e}")
+        silu(silus[3], 3)
+        grouped_first = keep.tile([P, 2 * C], F32, name="grouped_first", tag="grouped", align_bytes=64)
+        interleave(nc.scalar.copy, grouped_first[:].bitcast(BF16), g_planes[0])
+        silu(silus[2], 2)
+        silu(silus[1], 1)
+        slopes[1] = keep.tile([P, PACK, C], F32, name="slope1")
+        slopes[2], slopes[3] = pre[1], pre[2]
+        for e in (1, 2, 3):
+            sigmoid(slopes[e], e)
+        interleave(nc.vector.tensor_copy, middle_part.bitcast(BF16), g_planes[1])
+        nc.vector.tensor_scalar(silus[0][:], silus[0][:], -1.0, 1.0, ALU.mult, ALU.add)
+        nc.vector.tensor_tensor(slopes[0][:], slopes[0][:], silus[0][:], ALU.mult)
+        permute(0, "w2_first")
+        [g_operand] = quantize(grouped_first[:], "one")
+        permute(2, "grouped")
+        through_silu(hidden_gradient(0, g_operand), slopes[0], first_part)
+        da_operand, g_operand = quantize(shared[:, 3 * C : 7 * C], "both", operands=2)
+        nc.vector.tensor_copy(ungated[:, PACK - 1, :], dy[PACK - 1][:].indirect(slots(E - 1)))
 
-        grouped_first = keep.tile([P, C * PACK], BF16, name="grouped_first", tag="grouped", align_bytes=64)[:]
+        project(nc.vector, 0, (0, 1), da_operand)
+        project(nc.scalar, 0, (4, 5, 3), da_operand)
+        banks = hidden_gradient(1, g_operand)
+        slope_on_gpsimd(1)
+        nc.gpsimd.tensor_scalar(
+            middle_part.bitcast(BF16).rearrange("p (c t) -> p c t", t=PACK),
+            g_planes[2].rearrange("p t c -> p c t"),
+            1.0,
+            0.0,
+            ALU.mult,
+            ALU.add,
+        )
+        through_silu(banks, slopes[1], last_part)
+        before = da_operand
+        g_operand, da_operand = quantize(shared[:, 5 * C : 9 * C], "both", operands=2)
+        scatter(nc.vector, 0, 2, emptied(nc.vector, 0, 2, before, held=last_part[:, 0:C]))
+
+        project(nc.vector, 1, (0,), da_operand)
+        result = emptied(nc.vector, 1, 1, da_operand)
+        scatter(nc.vector, 1, 1, result)
+        project(nc.scalar, 1, (4, 5, 3, 2), da_operand)
+        banks = hidden_gradient(2, g_operand)
+        slope_on_gpsimd(2)
         for half in SLOT_HALVES:
-            interleave(grouped_first[:, PACK * half.start : PACK * half.stop], g_first[:, :, half])
-        [g_operand] = quantize(grouped_first, "g", slot="upper")
-        minus_d = two_planes(quarter(2)[:, 2 * C : 4 * C])
-        nc.vector.scalar_tensor_tensor(
-            out=minus_d, in0=late[0][1], scalar=1.0, in1=early[0][:, UPPER, :], op0=ALU.subtract, op1=ALU.mult
-        )
-        w2_s_late = keep.tile([P, 2, H], U8, name="w2_s_late", tag="grouped", align_bytes=64)
-        permute(nc.vector, w2_s_late[:], w2_sraw[:, 2:4, :])
-        for e in range(2, E):
-            w2_s[e] = w2_s_late[:, e - 2, :]
-        partial_first = keep.tile([P, 2, C], F32, name="partial_first", tag="partial", align_bytes=64)
-        da = quarter(3)[:, 0 : 2 * C].bitcast(BF16).rearrange("p (t c) -> p t c", t=PACK)
-        grouped_da = quarter(2)[:, 0 : 2 * C].bitcast(BF16)
-        for t in range(2):
-            nc.vector.scalar_tensor_tensor(
-                out=partial_first[:, t, :],
-                in0=late[0][0][:, t, :],
-                scalar=1.0,
-                in1=product(psum_h, "dh", w2, w2_s, 0, t, g_operand)[:],
-                op0=ALU.subtract,
-                op1=ALU.mult,
+            nc.gpsimd.tensor_tensor(
+                middle_part.bitcast(BF16).rearrange("p (c t) -> p c t", t=PACK)[:, half, :],
+                ungated[:, :, half].rearrange("p t c -> p c t"),
+                gates[E - 1][:, half].unsqueeze(2).to_broadcast([P, C // 2, PACK]),
+                ALU.mult,
             )
-            nc.gpsimd.tensor_tensor(da[:, t, :], partial_first[:, t, :], early[0][:, t, :], ALU.mult)
-        for t in range(2, PACK):
-            dh_plane = product(psum_h, "dh", w2, w2_s, 0, t, g_operand)
-            nc.vector.tensor_tensor(da[:, t, :], dh_plane[:], minus_d[:, t - 2, :], ALU.mult)
-        ungated_rest = keep.tile([P, PACK - 1, C], F32, name="ungated_rest", tag="upper", align_bytes=64)
-        ungated = [ungated_first] + [ungated_rest[:, t - 1, :] for t in range(1, PACK)]
-        for t in range(1, PACK):
-            nc.vector.tensor_copy(ungated[t], dy[t][:].indirect(slots(3)))
-        function(1, 0)
-        one_minus_silu(1)
-        grouped_second = keep.tile([P, C * PACK], BF16, name="grouped_second", tag="first", align_bytes=64)
-        interleave(grouped_second[:], g_planes[1])
-        [g_operand] = quantize(grouped_second[:], "g")
-        gather(2, 1, quarter(1)[:, 0:C])
-        nc.scalar.activation(
-            grouped_da.rearrange("p (c i t) -> p c t i", i=RUN, t=PACK),
-            da.rearrange("p t (c i) -> p c t i", i=RUN),
-            ACT.Copy,
-            scale=-1.0,
-        )
-        [da_operand] = quantize(grouped_da, "da")
-        gather(2, 3, quarter(3)[:, 0:C])
-        gather(2, 2, quarter(2)[:, 0:C])
+        through_silu(banks, slopes[2], last_part)
+        g_operand, da_operand = quantize(shared[:, 5 * C : 9 * C], "both", operands=2)
 
-        window = [keep.tile([P, T], F32, name=f"window{m}", tag=f"columns{m}") for m in range(K_TILES)]
-        for e in range(E):
-            project(e, 0, da_operand)
-            if e + 1 < E:
-                dh = hidden_gradient(e + 1, g_operand)
-            project(e, 1, da_operand)
-            if e == 2:
-                function(3, 1, halves=(UPPER,))
-            if e == 1:
-                one_minus_silu(2)
-            project(e, 2, da_operand)
-            if e == 0:
-                function(1, 1)
-            for m in range(3, K_TILES - 1):
-                project(e, m, da_operand)
-            if e + 1 < E:
-                da = through_silu(e + 1, dh)
-            if e + 2 < E:
-                function(e + 2, 0)
-                if e == 0:
-                    grouped = last[:, C : (PACK + 1) * C].bitcast(BF16)
-                else:
-                    both = keep.tile([P, 2 * C * PACK], BF16, name="grouped_both", tag="first", align_bytes=64)
-                    grouped = both[:]
-                interleave(grouped[:, C * PACK : 2 * C * PACK], g_planes[e + 2])
-                interleave(grouped[:, 0 : C * PACK], da[:])
-                next_operand, g_operand = quantize(grouped, "both", operands=2)
-                if e == 0:
-                    for t in range(1, PACK):
-                        gate_last(t)
-            elif e + 1 < E:
-                grouped = keep.tile([P, C * PACK], BF16, name="grouped_da", tag="first", align_bytes=64)
-                interleave(grouped[:], da[:])
-                [next_operand] = quantize(grouped[:], "da")
-            if e == 1:
-                permute_late(3, ring, "da")
-            project(e, K_TILES - 1, da_operand)
-            if e == 1:
-                one_minus_silu(3, halves=(LOWER,))
-                one_minus(early_upper[3], early[3][:, UPPER, :])
-                function(3, 1, halves=(LOWER,))
-            if e == 0:
-                function(2, 1)
-            da_operand = next_operand
+        project(nc.vector, 2, (0, 1), da_operand)
+        project(nc.scalar, 2, (4, 5, 3), da_operand)
+        banks = hidden_gradient(3, g_operand)
+        slope_on_gpsimd(3)
+        through_silu(banks, slopes[3], last_part)
+        before = da_operand
+        [da_operand] = quantize(last_part, "one")
+        scatter(nc.vector, 2, 2, emptied(nc.vector, 2, 2, before, held=last_part[:, 0:C]))
+        project(nc.vector, 3, (0, 1, 2), da_operand)
+        project(nc.scalar, 3, (4, 5, 3), da_operand)

@@ -10,6 +10,7 @@ K_TILES = K // P
 LIST_ROWS = 16
 QUADRANTS, QUADRANT_ROWS, SCALE_ROWS = 4, 32, 4
 PAIR = 2
+LAP = 8
 RUN = 4
 LOWER, UPPER = slice(0, 2), slice(2, 4)
 ALL_SLOTS = slice(0, C)
@@ -43,16 +44,18 @@ def tile_moe_bdx_mlp_silu_kernel(
         offsets = keep.tile([P, E * C // LIST_ROWS], U16, name="offsets")
         dy = [keep.tile([P, T], F32, name=f"dy{t}", tag=f"columns{t}") for t in range(PACK)]
         pre = [keep.tile([P, PACK, C], F32, name=f"pre{e}") for e in range(E)]
-        w2_raw = keep.tile([P, E, 2 * H], U8, name="w2_raw", align_bytes=64)
+        w2_raw = keep.tile([P, E, 2 * H], U8, name="w2_raw", tag="w2_raw", align_bytes=64)
         w2_sraw = keep.tile([P, E, H], U8, name="w2_sraw", align_bytes=64)
         w1 = keep.tile([P, E, 2 * K], U8, name="w1", align_bytes=64)
         w1_s = keep.tile([P, E, K], U8, name="w1_s", align_bytes=64)
         gates_early = keep.tile([P, (E - 1) * C], F32, name="gates_early", align_bytes=64)
         gates_last = keep.tile([P, C], F32, name="gates_last", align_bytes=64)
         gates = [gates_early[:, e * C : (e + 1) * C] for e in range(E - 1)] + [gates_last[:]]
-        shared = keep.tile([P, 9 * C], F32, name="shared", align_bytes=64)
+        shared = keep.tile([P, 12 * C], F32, name="shared", align_bytes=64)
         ungated = shared[:, 0 : 4 * C].rearrange("p (t c) -> p t c", t=PACK)
-        first_part, middle_part, last_part = [shared[:, j * C : (j + 2) * C] for j in (3, 5, 7)]
+        g_part, da_part = [shared[:, j * C : (j + 2) * C] for j in (4, 6)]
+        both_parts = shared[:, 4 * C : 8 * C]
+        slope = shared[:, 8 * C - LAP : 12 * C - LAP].rearrange("p (t c) -> p t c", t=PACK)
 
         nc.vector.memset(w2_sraw[:].bitcast(I32), 0)
         nc.vector.memset(w1_s[:].bitcast(I32), 0)
@@ -87,7 +90,7 @@ def tile_moe_bdx_mlp_silu_kernel(
         turned = psum_h.tile([P, C], F32, name="dh")
         nc.tensor.transpose(turned[:, 0:P], gate_rows[:], identity[:])
         nc.vector.tensor_copy(gate_columns[:], turned[:, 0:blocks])
-        for e in range(E):
+        for e in range(E - 1):
             spread = psum_x.tile([P, C], F32, name="spread", tag=("dx_vector", "dx_scalar")[e % 2])
             for j in range(C // P):
                 b = e * C // P + j
@@ -109,6 +112,7 @@ def tile_moe_bdx_mlp_silu_kernel(
         load_pre(1)
         load_scales(w1_s, w1_scales)
         load_words(w1, w1_words)
+        nc.sync.dma_start(out=gates[E - 1], in_=gate[0:P, (E - 1) * C : E * C])
 
         w1_of = [w1[:, e, :] for e in range(E)]
         w1_s_of = [w1_s[:, e, :] for e in range(E)]
@@ -120,8 +124,8 @@ def tile_moe_bdx_mlp_silu_kernel(
             scales = both[:, 4 * H : 6 * H].rearrange("p (e n) -> p e n", e=2)
             pair = slice(first, first + 2)
             for target, source in (
-                (words.bitcast(U16), w2_raw[:, pair, :].bitcast(U16)),
                 (scales, w2_sraw[:, pair, :]),
+                (words.bitcast(U16), w2_raw[:, pair, :].bitcast(U16)),
             ):
                 nc.vector.tensor_copy(
                     out=target.rearrange("p e (t m) -> p e t m", t=PACK),
@@ -193,24 +197,34 @@ def tile_moe_bdx_mlp_silu_kernel(
                 nc.scalar.activation(target[:, planes, :], pre[e][:, planes, :], ACT.Silu, scale=-1.0)
 
         def slope_on_gpsimd(e):
-            rest = middle_part.rearrange("p (t c) -> p t c", t=2)
+            rest = g_part.rearrange("p (t c) -> p t c", t=2)
             for planes in (LOWER, UPPER):
                 nc.gpsimd.tensor_scalar(rest, silus[e][:, planes, :], -1.0, 1.0, ALU.mult, ALU.add)
                 nc.gpsimd.tensor_tensor(slopes[e][:, planes, :], slopes[e][:, planes, :], rest, ALU.mult)
 
+        def one_minus(target, source):
+            nc.gpsimd.tensor_scalar(target, source, -1.0, 1.0, ALU.mult, ALU.add)
+
         window = {}
 
-        def emptied(engine, e, m, da_operand, held=None):
+        def half_tile(engine, e, m, da_operand, nth, held=None):
+            half = SLOT_HALVES[nth]
+            scatter(engine, e, m, emptied(engine, e, m, da_operand, held=held, part=half), part=half)
+
+        def emptied(engine, e, m, da_operand, held=None, part=ALL_SLOTS):
             name = "vector" if engine is nc.vector else "scalar"
-            dx = psum_x.tile([P, C], F32, name="dx", tag=f"dx_{name}")
-            product(dx[:], w1_of[e], w1_s_of[e], m, da_operand, ALL_SLOTS)
+            if e == 0 and m in (0, 1, 4, 5):
+                dx = psum_h.tile([P, C], F32, name="dh")
+            else:
+                dx = psum_x.tile([P, C], F32, name="dx", tag=f"dx_{name}")
+            product(dx[:, part], w1_of[e], w1_s_of[e], m, da_operand, part)
             result = held
             if held is None:
                 result = ring.tile([P, C], F32, name="result", tag=f"result_{name}", bufs=3)[:]
             if engine is nc.vector:
-                nc.vector.tensor_copy(result, dx[:])
+                nc.vector.tensor_copy(result[:, part], dx[:, part])
             else:
-                nc.scalar.copy(out=result, in_=dx[:])
+                nc.scalar.copy(out=result[:, part], in_=dx[:, part])
             return result
 
         def scatter(engine, e, m, result, part=ALL_SLOTS):
@@ -219,7 +233,7 @@ def tile_moe_bdx_mlp_silu_kernel(
             if engine is nc.vector:
                 nc.vector.tensor_copy(window[m][:].indirect(slots(e, part)), result[:, part])
             else:
-                for half in SLOT_HALVES:
+                for half in SLOT_HALVES if part == ALL_SLOTS else (part,):
                     nc.scalar.activation(window[m][:].indirect(slots(e, half)), result[:, half], ACT.Copy)
             if e == E - 1:
                 queue = nc.sync if engine is nc.vector else nc.scalar
@@ -249,6 +263,7 @@ def tile_moe_bdx_mlp_silu_kernel(
         for e in (3, 2, 1):
             silus[e] = keep.tile([P, PACK, C], F32, name=f"silu{e}")
         silu(silus[3], 3)
+        gather_last(3)
         grouped_first = keep.tile([P, 2 * C], F32, name="grouped_first", tag="grouped", align_bytes=64)
         interleave(nc.scalar.copy, grouped_first[:].bitcast(BF16), g_planes[0])
         silu(silus[2], 2)
@@ -257,56 +272,74 @@ def tile_moe_bdx_mlp_silu_kernel(
         slopes[2], slopes[3] = pre[1], pre[2]
         for e in (1, 2, 3):
             sigmoid(slopes[e], e)
-        interleave(nc.vector.tensor_copy, middle_part.bitcast(BF16), g_planes[1])
+        interleave(nc.vector.tensor_copy, g_part.bitcast(BF16), g_planes[1])
         nc.vector.tensor_scalar(silus[0][:], silus[0][:], -1.0, 1.0, ALU.mult, ALU.add)
         nc.vector.tensor_tensor(slopes[0][:], slopes[0][:], silus[0][:], ALU.mult)
         permute(0, "w2_first")
         [g_operand] = quantize(grouped_first[:], "one")
         permute(2, "grouped")
-        through_silu(hidden_gradient(0, g_operand), slopes[0], first_part)
-        da_operand, g_operand = quantize(shared[:, 3 * C : 7 * C], "both", operands=2)
-        nc.vector.tensor_copy(ungated[:, PACK - 1, :], dy[PACK - 1][:].indirect(slots(E - 1)))
+        through_silu(hidden_gradient(0, g_operand), slopes[0], da_part)
+        rest = keep.tile([P, PACK, C], F32, name="rest", tag="w2_raw", align_bytes=64)
+        one_minus(rest[:], silus[1][:])
+        g_operand, da_operand = quantize(both_parts, "both", operands=2)
 
         project(nc.vector, 0, (0, 1), da_operand)
         project(nc.scalar, 0, (4, 5, 3), da_operand)
         banks = hidden_gradient(1, g_operand)
-        slope_on_gpsimd(1)
+        nc.gpsimd.tensor_tensor(slope, slopes[1][:], rest[:], ALU.mult)
         nc.gpsimd.tensor_scalar(
-            middle_part.bitcast(BF16).rearrange("p (c t) -> p c t", t=PACK),
+            g_part.bitcast(BF16).rearrange("p (c t) -> p c t", t=PACK),
             g_planes[2].rearrange("p t c -> p c t"),
             1.0,
             0.0,
             ALU.mult,
             ALU.add,
         )
-        through_silu(banks, slopes[1], last_part)
+        for planes in (LOWER, UPPER):
+            one_minus(rest[:, planes, :], silus[2][:, planes, :])
+        through_silu(banks, slope, da_part)
         before = da_operand
-        g_operand, da_operand = quantize(shared[:, 5 * C : 9 * C], "both", operands=2)
-        scatter(nc.vector, 0, 2, emptied(nc.vector, 0, 2, before, held=last_part[:, 0:C]))
+        g_operand, da_operand = quantize(both_parts, "both", operands=2)
+        scatter(nc.vector, 0, 2, emptied(nc.vector, 0, 2, before, held=da_part[:, 0:C]))
 
         project(nc.vector, 1, (0,), da_operand)
-        result = emptied(nc.vector, 1, 1, da_operand)
-        scatter(nc.vector, 1, 1, result)
         project(nc.scalar, 1, (4, 5, 3, 2), da_operand)
+        half_tile(nc.vector, 1, 1, da_operand, 0)
         banks = hidden_gradient(2, g_operand)
-        slope_on_gpsimd(2)
+        nc.gpsimd.tensor_tensor(slope, slopes[2][:], rest[:], ALU.mult)
         for half in SLOT_HALVES:
             nc.gpsimd.tensor_tensor(
-                middle_part.bitcast(BF16).rearrange("p (c t) -> p c t", t=PACK)[:, half, :],
+                g_part.bitcast(BF16).rearrange("p (c t) -> p c t", t=PACK)[:, half, :],
                 ungated[:, :, half].rearrange("p t c -> p c t"),
                 gates[E - 1][:, half].unsqueeze(2).to_broadcast([P, C // 2, PACK]),
                 ALU.mult,
             )
-        through_silu(banks, slopes[2], last_part)
-        g_operand, da_operand = quantize(shared[:, 5 * C : 9 * C], "both", operands=2)
+        through_silu(banks, slope, da_part)
+        before = da_operand
+        g_operand, da_operand = quantize(both_parts, "both", operands=2)
+        half_tile(nc.vector, 1, 1, before, 1, held=da_part[:, 0:C])
 
-        project(nc.vector, 2, (0, 1), da_operand)
-        project(nc.scalar, 2, (4, 5, 3), da_operand)
+        project(nc.vector, 2, (0,), da_operand)
+        project(nc.scalar, 2, (4, 5), da_operand)
+        half_tile(nc.vector, 2, 1, da_operand, 0)
+        half_tile(nc.scalar, 2, 3, da_operand, 0)
         banks = hidden_gradient(3, g_operand)
         slope_on_gpsimd(3)
-        through_silu(banks, slopes[3], last_part)
+        through_silu(banks, slopes[3], da_part)
         before = da_operand
-        [da_operand] = quantize(last_part, "one")
-        scatter(nc.vector, 2, 2, emptied(nc.vector, 2, 2, before, held=last_part[:, 0:C]))
-        project(nc.vector, 3, (0, 1, 2), da_operand)
-        project(nc.scalar, 3, (4, 5, 3), da_operand)
+        [da_operand] = quantize(da_part, "one")
+        half_tile(nc.vector, 2, 1, before, 1, held=da_part[:, 0:C])
+        for engine, name, first, second, third, left in (
+            (nc.vector, "vector", 0, 1, 2, ALL_SLOTS),
+            (nc.scalar, "scalar", 4, 5, 3, SLOT_HALVES[1]),
+        ):
+            turn = keep.tile([P, C], F32, name="turn", tag=f"turn_{name}")
+            emptied(engine, 3, first, da_operand, held=turn[:])
+            result = emptied(engine, 3, second, da_operand)
+            scatter(engine, 3, first, turn[:])
+            turn = keep.tile([P, C], F32, name="turn", tag=f"turn_{name}")
+            emptied(engine, 2, third, before, held=turn[:], part=left)
+            scatter(engine, 3, second, result)
+            result = emptied(engine, 3, third, da_operand)
+            scatter(engine, 2, third, turn[:], part=left)
+            scatter(engine, 3, third, result)

@@ -10,7 +10,7 @@ K_TILES = K // P
 LIST_ROWS = 16
 QUADRANTS, QUADRANT_ROWS, SCALE_ROWS = 4, 32, 4
 PAIR = 2
-LAP = 8
+LAP = 32
 RUN = 4
 LOWER, UPPER = slice(0, 2), slice(2, 4)
 ALL_SLOTS = slice(0, C)
@@ -42,8 +42,8 @@ def tile_moe_bdx_mlp_silu_kernel(
         psum_x = ctx.enter_context(tc.psum_pool(name="psum_x", bufs=2))
 
         offsets = keep.tile([P, E * C // LIST_ROWS], U16, name="offsets")
-        dy = [keep.tile([P, T], F32, name=f"dy{t}", tag=f"columns{t}") for t in range(PACK)]
-        pre = [keep.tile([P, PACK, C], F32, name=f"pre{e}") for e in range(E)]
+        dy = [keep.tile([P, T], F32, name=f"dy{t}", tag=f"columns{t}", align_bytes=64) for t in range(PACK)]
+        pre = [keep.tile([P, PACK, C], F32, name=f"pre{e}", tag=f"pre{e}", align_bytes=64) for e in range(E)]
         w2_raw = keep.tile([P, E, 2 * H], U8, name="w2_raw", tag="w2_raw", align_bytes=64)
         w2_sraw = keep.tile([P, E, H], U8, name="w2_sraw", align_bytes=64)
         w1 = keep.tile([P, E, 2 * K], U8, name="w1", align_bytes=64)
@@ -104,12 +104,12 @@ def tile_moe_bdx_mlp_silu_kernel(
         load_pre(0, UPPER)
         load_dy(1)
         load_dy(2)
-        load_pre(3)
         load_dy(3)
+        load_pre(3)
         load_pre(2)
+        load_pre(1)
         load_words(w2_raw, w2_words)
         load_scales(w2_sraw, w2_scales)
-        load_pre(1)
         load_scales(w1_s, w1_scales)
         load_words(w1, w1_words)
         nc.sync.dma_start(out=gates[E - 1], in_=gate[0:P, (E - 1) * C : E * C])
@@ -153,8 +153,11 @@ def tile_moe_bdx_mlp_silu_kernel(
                 in_=planes.rearrange("p t (c i) -> p c t i", i=RUN),
             )
 
-        def quantize(grouped, kind, operands=1):
-            codes = ring.tile([P, operands * C], U32, name=f"codes_{kind}", align_bytes=64)
+        def quantize(grouped, kind, operands=1, slot=None):
+            if slot is None:
+                codes = ring.tile([P, operands * C], U32, name=f"codes_{kind}", align_bytes=64)
+            else:
+                codes = keep.tile([P, operands * C], U32, name=f"codes_{kind}", tag=slot, align_bytes=64)
             scales = ring.tile([P, operands * C], U8, name=f"scales_{kind}", align_bytes=64)
             nc.vector.quantize_mx(out=codes[:].bitcast(FP8X4), scales=scales[:], in_=grouped.bitcast(BF16))
             return [(codes[:, j * C : (j + 1) * C], scales[:, j * C : (j + 1) * C]) for j in range(operands)]
@@ -193,7 +196,7 @@ def tile_moe_bdx_mlp_silu_kernel(
                 nc.scalar.activation(target[:, planes, :], pre[e][:, planes, :], ACT.Sigmoid)
 
         def silu(target, e):
-            for planes in (LOWER, UPPER):
+            for planes in (LOWER, UPPER) if e == 0 else (slice(0, PACK),):
                 nc.scalar.activation(target[:, planes, :], pre[e][:, planes, :], ACT.Silu, scale=-1.0)
 
         def slope_on_gpsimd(e):
@@ -229,7 +232,7 @@ def tile_moe_bdx_mlp_silu_kernel(
 
         def scatter(engine, e, m, result, part=ALL_SLOTS):
             if m not in window:
-                window[m] = keep.tile([P, T], F32, name=f"window{m}", tag=f"columns{m}")
+                window[m] = keep.tile([P, T], F32, name=f"window{m}", tag=f"columns{m}", align_bytes=64)
             if engine is nc.vector:
                 nc.vector.tensor_copy(window[m][:].indirect(slots(e, part)), result[:, part])
             else:
@@ -262,26 +265,31 @@ def tile_moe_bdx_mlp_silu_kernel(
         gather(1, 2, PACK - 1)
         for e in (3, 2, 1):
             silus[e] = keep.tile([P, PACK, C], F32, name=f"silu{e}")
-        silu(silus[3], 3)
         gather_last(3)
+        silu(silus[3], 3)
         grouped_first = keep.tile([P, 2 * C], F32, name="grouped_first", tag="grouped", align_bytes=64)
-        interleave(nc.scalar.copy, grouped_first[:].bitcast(BF16), g_planes[0])
+        share = 3 * C // 4
+        interleave(nc.scalar.copy, grouped_first[:].bitcast(BF16)[:, 0 : PACK * share], g_planes[0][:, :, 0:share])
+        interleave(nc.vector.tensor_copy, grouped_first[:].bitcast(BF16)[:, PACK * share :], g_planes[0][:, :, share:])
         silu(silus[2], 2)
         silu(silus[1], 1)
         slopes[1] = keep.tile([P, PACK, C], F32, name="slope1")
         slopes[2], slopes[3] = pre[1], pre[2]
         for e in (1, 2, 3):
             sigmoid(slopes[e], e)
-        interleave(nc.vector.tensor_copy, g_part.bitcast(BF16), g_planes[1])
+        straddle = shared[:, 6 * C - LAP // 2 : 8 * C - LAP // 2]
+        interleave(nc.vector.tensor_copy, straddle.bitcast(BF16), g_planes[1])
         nc.vector.tensor_scalar(silus[0][:], silus[0][:], -1.0, 1.0, ALU.mult, ALU.add)
         nc.vector.tensor_tensor(slopes[0][:], slopes[0][:], silus[0][:], ALU.mult)
-        permute(0, "w2_first")
+        permute(0, "pre0")
         [g_operand] = quantize(grouped_first[:], "one")
         permute(2, "grouped")
-        through_silu(hidden_gradient(0, g_operand), slopes[0], da_part)
+        grouped_da = keep.tile([P, 2 * C], F32, name="grouped_da", tag="columns2", align_bytes=64)
+        through_silu(hidden_gradient(0, g_operand), slopes[0], grouped_da[:])
         rest = keep.tile([P, PACK, C], F32, name="rest", tag="w2_raw", align_bytes=64)
         one_minus(rest[:], silus[1][:])
-        g_operand, da_operand = quantize(both_parts, "both", operands=2)
+        [da_operand] = quantize(grouped_da[:], "one")
+        [g_operand] = quantize(straddle, "second", slot="columns2")
 
         project(nc.vector, 0, (0, 1), da_operand)
         project(nc.scalar, 0, (4, 5, 3), da_operand)
@@ -314,6 +322,7 @@ def tile_moe_bdx_mlp_silu_kernel(
                 gates[E - 1][:, half].unsqueeze(2).to_broadcast([P, C // 2, PACK]),
                 ALU.mult,
             )
+        one_minus(ungated[:, LOWER, :], silus[3][:, LOWER, :])
         through_silu(banks, slope, da_part)
         before = da_operand
         g_operand, da_operand = quantize(both_parts, "both", operands=2)
@@ -324,8 +333,11 @@ def tile_moe_bdx_mlp_silu_kernel(
         half_tile(nc.vector, 2, 1, da_operand, 0)
         half_tile(nc.scalar, 2, 3, da_operand, 0)
         banks = hidden_gradient(3, g_operand)
-        slope_on_gpsimd(3)
-        through_silu(banks, slopes[3], da_part)
+        rest_upper = g_part.rearrange("p (t c) -> p t c", t=2)
+        nc.gpsimd.tensor_tensor(slope[:, LOWER, :], slopes[3][:, LOWER, :], ungated[:, LOWER, :], ALU.mult)
+        one_minus(rest_upper, silus[3][:, UPPER, :])
+        nc.gpsimd.tensor_tensor(slope[:, UPPER, :], slopes[3][:, UPPER, :], rest_upper, ALU.mult)
+        through_silu(banks, slope, da_part)
         before = da_operand
         [da_operand] = quantize(da_part, "one")
         half_tile(nc.vector, 2, 1, before, 1, held=da_part[:, 0:C])

@@ -118,8 +118,7 @@ def tile_moe_bdx_mlp_silu_kernel(
         w1_s_of = [w1_s[:, e, :] for e in range(E)]
         w2, w2_s = {}, {}
 
-        def permute(first, slot):
-            both = keep.tile([P, 6 * H], U8, name=f"w2_from{first}", tag=slot, align_bytes=64)
+        def permute(first, both):
             words = both[:, 0 : 4 * H].rearrange("p (e n) -> p e n", e=2)
             scales = both[:, 4 * H : 6 * H].rearrange("p (e n) -> p e n", e=2)
             pair = slice(first, first + 2)
@@ -210,13 +209,13 @@ def tile_moe_bdx_mlp_silu_kernel(
 
         window = {}
 
-        def half_tile(engine, e, m, da_operand, nth, held=None):
+        def half_tile(engine, e, m, da_operand, nth):
             half = SLOT_HALVES[nth]
-            scatter(engine, e, m, emptied(engine, e, m, da_operand, held=held, part=half), part=half)
+            scatter(engine, e, m, emptied(engine, e, m, da_operand, part=half), part=half)
 
-        def emptied(engine, e, m, da_operand, held=None, part=ALL_SLOTS):
+        def emptied(engine, e, m, da_operand, held=None, part=ALL_SLOTS, late=False):
             name = "vector" if engine is nc.vector else "scalar"
-            if e == 0 and m in (0, 1, 4, 5):
+            if late or (e == 0 and m in (0, 1, 4, 5)):
                 dx = psum_h.tile([P, C], F32, name="dh")
             else:
                 dx = psum_x.tile([P, C], F32, name="dx", tag=f"dx_{name}")
@@ -251,7 +250,7 @@ def tile_moe_bdx_mlp_silu_kernel(
                 waiting = (m, result)
             scatter(engine, e, *waiting)
 
-        slopes = {0: keep.tile([P, PACK, C], F32, name="slope0")}
+        slopes = {0: keep.tile([P, PACK, C], F32, name="slope0", tag="slope0", align_bytes=64)}
         silus = {0: pre[0]}
         sigmoid(slopes[0], 0, halves=(LOWER,))
         gather_last(0)
@@ -268,9 +267,7 @@ def tile_moe_bdx_mlp_silu_kernel(
         gather_last(3)
         silu(silus[3], 3)
         grouped_first = keep.tile([P, 2 * C], F32, name="grouped_first", tag="grouped", align_bytes=64)
-        share = 3 * C // 4
-        interleave(nc.scalar.copy, grouped_first[:].bitcast(BF16)[:, 0 : PACK * share], g_planes[0][:, :, 0:share])
-        interleave(nc.vector.tensor_copy, grouped_first[:].bitcast(BF16)[:, PACK * share :], g_planes[0][:, :, share:])
+        interleave(nc.scalar.copy, grouped_first[:].bitcast(BF16), g_planes[0])
         silu(silus[2], 2)
         silu(silus[1], 1)
         slopes[1] = keep.tile([P, PACK, C], F32, name="slope1")
@@ -281,20 +278,22 @@ def tile_moe_bdx_mlp_silu_kernel(
         interleave(nc.vector.tensor_copy, straddle.bitcast(BF16), g_planes[1])
         nc.vector.tensor_scalar(silus[0][:], silus[0][:], -1.0, 1.0, ALU.mult, ALU.add)
         nc.vector.tensor_tensor(slopes[0][:], slopes[0][:], silus[0][:], ALU.mult)
-        permute(0, "pre0")
         [g_operand] = quantize(grouped_first[:], "one")
-        permute(2, "grouped")
+        permuted = keep.tile([P, 12 * H], U8, name="permuted", tag="pre0", align_bytes=64)
+        permute(0, permuted[:, 0 : 6 * H])
+        permute(2, permuted[:, 6 * H : 12 * H])
         grouped_da = keep.tile([P, 2 * C], F32, name="grouped_da", tag="columns2", align_bytes=64)
         through_silu(hidden_gradient(0, g_operand), slopes[0], grouped_da[:])
         rest = keep.tile([P, PACK, C], F32, name="rest", tag="w2_raw", align_bytes=64)
         one_minus(rest[:], silus[1][:])
         [da_operand] = quantize(grouped_da[:], "one")
-        [g_operand] = quantize(straddle, "second", slot="columns2")
+        [g_operand] = quantize(straddle, "second", slot="slope0")
 
         project(nc.vector, 0, (0, 1), da_operand)
+        first_half, second_half = SLOT_HALVES
+        half_tile(nc.scalar, 0, 2, da_operand, 0)
         project(nc.scalar, 0, (4, 5, 3), da_operand)
         banks = hidden_gradient(1, g_operand)
-        nc.gpsimd.tensor_tensor(slope, slopes[1][:], rest[:], ALU.mult)
         nc.gpsimd.tensor_scalar(
             g_part.bitcast(BF16).rearrange("p (c t) -> p c t", t=PACK),
             g_planes[2].rearrange("p t c -> p c t"),
@@ -303,19 +302,20 @@ def tile_moe_bdx_mlp_silu_kernel(
             ALU.mult,
             ALU.add,
         )
+        nc.gpsimd.tensor_tensor(slope, slopes[1][:], rest[:], ALU.mult)
         for planes in (LOWER, UPPER):
             one_minus(rest[:, planes, :], silus[2][:, planes, :])
         through_silu(banks, slope, da_part)
         before = da_operand
         g_operand, da_operand = quantize(both_parts, "both", operands=2)
-        scatter(nc.vector, 0, 2, emptied(nc.vector, 0, 2, before, held=da_part[:, 0:C]))
+        scatter(nc.vector, 0, 2, emptied(nc.vector, 0, 2, before, part=second_half, late=True), part=second_half)
 
-        project(nc.vector, 1, (0,), da_operand)
-        project(nc.scalar, 1, (4, 5, 3, 2), da_operand)
-        half_tile(nc.vector, 1, 1, da_operand, 0)
+        project(nc.vector, 1, (0, 1), da_operand)
+        project(nc.scalar, 1, (4, 5, 3), da_operand)
         banks = hidden_gradient(2, g_operand)
-        nc.gpsimd.tensor_tensor(slope, slopes[2][:], rest[:], ALU.mult)
         for half in SLOT_HALVES:
+            if half.start > 0:
+                nc.gpsimd.tensor_tensor(slope, slopes[2][:], rest[:], ALU.mult)
             nc.gpsimd.tensor_tensor(
                 g_part.bitcast(BF16).rearrange("p (c t) -> p c t", t=PACK)[:, half, :],
                 ungated[:, :, half].rearrange("p t c -> p c t"),
@@ -326,12 +326,12 @@ def tile_moe_bdx_mlp_silu_kernel(
         through_silu(banks, slope, da_part)
         before = da_operand
         g_operand, da_operand = quantize(both_parts, "both", operands=2)
-        half_tile(nc.vector, 1, 1, before, 1, held=da_part[:, 0:C])
+        scatter(nc.vector, 1, 2, emptied(nc.vector, 1, 2, before, part=first_half, late=True), part=first_half)
+        earlier = before
 
         project(nc.vector, 2, (0,), da_operand)
-        project(nc.scalar, 2, (4, 5), da_operand)
+        project(nc.scalar, 2, (4, 5, 3), da_operand)
         half_tile(nc.vector, 2, 1, da_operand, 0)
-        half_tile(nc.scalar, 2, 3, da_operand, 0)
         banks = hidden_gradient(3, g_operand)
         rest_upper = g_part.rearrange("p (t c) -> p t c", t=2)
         nc.gpsimd.tensor_tensor(slope[:, LOWER, :], slopes[3][:, LOWER, :], ungated[:, LOWER, :], ALU.mult)
@@ -340,18 +340,19 @@ def tile_moe_bdx_mlp_silu_kernel(
         through_silu(banks, slope, da_part)
         before = da_operand
         [da_operand] = quantize(da_part, "one")
-        half_tile(nc.vector, 2, 1, before, 1, held=da_part[:, 0:C])
-        for engine, name, first, second, third, left in (
-            (nc.vector, "vector", 0, 1, 2, ALL_SLOTS),
-            (nc.scalar, "scalar", 4, 5, 3, SLOT_HALVES[1]),
-        ):
-            turn = keep.tile([P, C], F32, name="turn", tag=f"turn_{name}")
-            emptied(engine, 3, first, da_operand, held=turn[:])
-            result = emptied(engine, 3, second, da_operand)
-            scatter(engine, 3, first, turn[:])
-            turn = keep.tile([P, C], F32, name="turn", tag=f"turn_{name}")
-            emptied(engine, 2, third, before, held=turn[:], part=left)
-            scatter(engine, 3, second, result)
-            result = emptied(engine, 3, third, da_operand)
-            scatter(engine, 2, third, turn[:], part=left)
-            scatter(engine, 3, third, result)
+        scatter(nc.vector, 2, 1, emptied(nc.vector, 2, 1, before, part=second_half, late=True), part=second_half)
+        results = [emptied(nc.vector, 3, m, da_operand) for m in (0, 1)]
+        scatter(nc.vector, 3, 0, results[0])
+        joint = shared[:, 11 * C // 2 : 17 * C // 2]
+        emptied(nc.vector, 1, 2, earlier, held=joint[:, 0:C], part=second_half)
+        emptied(nc.vector, 2, 2, before, held=joint[:, C : 2 * C])
+        emptied(nc.vector, 3, 2, da_operand, held=joint[:, 2 * C : 3 * C])
+        scatter(nc.vector, 3, 1, results[1])
+        nc.vector.tensor_copy(window[2][:].indirect(slots(1, slice(C // 2, 3 * C))), joint[:, C // 2 :])
+        nc.sync.dma_start(out=out[2 * P : 3 * P, :], in_=window[2][:])
+        turn = keep.tile([P, C], F32, name="turn", tag="grouped", align_bytes=64)
+        results = [emptied(nc.scalar, 3, 4, da_operand, held=turn[:]), emptied(nc.scalar, 3, 5, da_operand)]
+        scatter(nc.scalar, 3, 4, results[0])
+        emptied(nc.scalar, 3, 3, da_operand, held=turn[:])
+        scatter(nc.scalar, 3, 5, results[1])
+        scatter(nc.scalar, 3, 3, turn[:])

@@ -6,15 +6,15 @@ from concourse.masks import make_identity
 K, T, E, C, H, N = 768, 2048, 4, 512, 512, 512
 P = 128
 PACK = 4
-K_TILES = K // P
+LAST = E - 1
 LIST_ROWS = 16
 QUADRANTS, QUADRANT_ROWS, SCALE_ROWS = 4, 32, 4
+RUN = 4
 PAIR = 2
 LAP = 32
-RUN = 4
 LOWER, UPPER = slice(0, 2), slice(2, 4)
 ALL_SLOTS = slice(0, C)
-SLOT_HALVES = (slice(0, C // 2), slice(C // 2, C))
+FIRST_HALF, SECOND_HALF = slice(0, C // 2), slice(C // 2, C)
 
 F32 = mybir.dt.float32
 BF16 = mybir.dt.bfloat16
@@ -45,12 +45,15 @@ def tile_moe_bdx_mlp_silu_kernel(
         dy = [keep.tile([P, T], F32, name=f"dy{t}", tag=f"columns{t}", align_bytes=64) for t in range(PACK)]
         pre = [keep.tile([P, PACK, C], F32, name=f"pre{e}", tag=f"pre{e}", align_bytes=64) for e in range(E)]
         w2_raw = keep.tile([P, E, 2 * H], U8, name="w2_raw", tag="w2_raw", align_bytes=64)
-        w2_sraw = keep.tile([P, E, H], U8, name="w2_sraw", align_bytes=64)
+        w2_sraw = keep.tile([P, 1, H], U8, name="w2_sraw", align_bytes=64)
+        w2_s_late = keep.tile([P, LAST, H], U8, name="w2_s_late", align_bytes=64)
         w1 = keep.tile([P, E, 2 * K], U8, name="w1", align_bytes=64)
         w1_s = keep.tile([P, E, K], U8, name="w1_s", align_bytes=64)
-        gates_early = keep.tile([P, (E - 1) * C], F32, name="gates_early", align_bytes=64)
+        gates_row = keep.tile([P, 6 * C], F32, name="gates_row", align_bytes=64)
+        gates_early = gates_row[:, 3 * C : 6 * C]
+        rest_first = gates_row[:, 0 : 4 * C].rearrange("p (t c) -> p t c", t=PACK)
         gates_last = keep.tile([P, C], F32, name="gates_last", align_bytes=64)
-        gates = [gates_early[:, e * C : (e + 1) * C] for e in range(E - 1)] + [gates_last[:]]
+        gates = [gates_early[:, e * C : (e + 1) * C] for e in range(LAST)] + [gates_last[:]]
         shared = keep.tile([P, 12 * C], F32, name="shared", align_bytes=64)
         ungated = shared[:, 0 : 4 * C].rearrange("p (t c) -> p t c", t=PACK)
         g_part, da_part = [shared[:, j * C : (j + 2) * C] for j in (4, 6)]
@@ -59,22 +62,16 @@ def tile_moe_bdx_mlp_silu_kernel(
 
         nc.vector.memset(w2_sraw[:].bitcast(I32), 0)
         nc.vector.memset(w1_s[:].bitcast(I32), 0)
+        nc.vector.memset(w2_s_late[:].bitcast(I32), 0)
 
         dy_rows = dyT.rearrange("(p t) j -> p t j", t=PACK)
         a_rows = a.rearrange("(p t) j -> p t j", t=PACK)
 
-        def load_scales(rows, scales):
-            for q in range(QUADRANTS):
-                nc.sync.dma_start(
-                    out=rows[QUADRANT_ROWS * q : QUADRANT_ROWS * q + SCALE_ROWS].bitcast(I32),
-                    in_=scales[:, 0, SCALE_ROWS * q : SCALE_ROWS * (q + 1), :].rearrange("e f n -> f e n").bitcast(I32),
-                )
+        def load_words(target, source):
+            nc.sync.dma_start(out=target[:].bitcast(I32), in_=source.rearrange("e o p n -> p (e o) n").bitcast(I32))
 
-        def load_words(words, source):
-            nc.sync.dma_start(out=words[:].bitcast(I32), in_=source.rearrange("e o p n -> p (e o) n").bitcast(I32))
-
-        def load_dy(t):
-            nc.sync.dma_start(out=dy[t][:], in_=dy_rows[:, t, :])
+        def load_dy(t, tokens=slice(0, T)):
+            nc.sync.dma_start(out=dy[t][:, tokens], in_=dy_rows[:, t, tokens])
 
         def load_pre(e, planes=slice(0, PACK)):
             nc.sync.dma_start(out=pre[e][:, planes, :], in_=a_rows[:, planes, e * C : (e + 1) * C])
@@ -90,67 +87,70 @@ def tile_moe_bdx_mlp_silu_kernel(
         turned = psum_h.tile([P, C], F32, name="dh")
         nc.tensor.transpose(turned[:, 0:P], gate_rows[:], identity[:])
         nc.vector.tensor_copy(gate_columns[:], turned[:, 0:blocks])
-        for e in range(E - 1):
-            spread = psum_x.tile([P, C], F32, name="spread", tag=("dx_vector", "dx_scalar")[e % 2])
+
+        def spread(e):
+            bank = psum_x.tile([P, C], F32, name="spread", tag=("dx_vector", "dx_scalar")[e % 2])
             for j in range(C // P):
                 b = e * C // P + j
                 column = gate_columns[:, b : b + 1].to_broadcast([P, P])
-                nc.tensor.transpose(spread[:, j * P : (j + 1) * P], column, identity[:])
-            nc.vector.tensor_copy(gates[e], spread[:])
+                nc.tensor.transpose(bank[:, j * P : (j + 1) * P], column, identity[:])
+            return bank[:]
+
+        for e in range(LAST):
+            nc.vector.tensor_copy(gates[e], spread(e))
 
         load_pre(0, LOWER)
-        for half in (slice(0, T // 2), slice(T // 2, T)):
-            nc.sync.dma_start(out=dy[0][:, half], in_=dy_rows[:, 0, half])
+        load_dy(0, slice(0, T // 2))
+        load_dy(0, slice(T // 2, T))
         load_pre(0, UPPER)
         load_dy(1)
         load_dy(2)
-        load_dy(3)
         load_pre(3)
+        load_dy(3)
         load_pre(2)
         load_pre(1)
         load_words(w2_raw, w2_words)
-        load_scales(w2_sraw, w2_scales)
-        load_scales(w1_s, w1_scales)
+        for q in range(QUADRANTS):
+            nc.sync.dma_start(
+                out=w2_sraw[QUADRANT_ROWS * q : QUADRANT_ROWS * q + E * SCALE_ROWS, 0, :].bitcast(I32),
+                in_=w2_scales[:, 0, SCALE_ROWS * q : SCALE_ROWS * (q + 1), :].bitcast(I32),
+            )
+        for q in range(QUADRANTS):
+            nc.sync.dma_start(
+                out=w1_s[QUADRANT_ROWS * q : QUADRANT_ROWS * q + SCALE_ROWS].bitcast(I32),
+                in_=w1_scales[:, 0, SCALE_ROWS * q : SCALE_ROWS * (q + 1), :].rearrange("e f n -> f e n").bitcast(I32),
+            )
         load_words(w1, w1_words)
-        nc.sync.dma_start(out=gates[E - 1], in_=gate[0:P, (E - 1) * C : E * C])
 
-        w1_of = [w1[:, e, :] for e in range(E)]
-        w1_s_of = [w1_s[:, e, :] for e in range(E)]
-        w2, w2_s = {}, {}
-
-        def permute(first, both):
-            words = both[:, 0 : 4 * H].rearrange("p (e n) -> p e n", e=2)
-            scales = both[:, 4 * H : 6 * H].rearrange("p (e n) -> p e n", e=2)
-            pair = slice(first, first + 2)
-            for target, source in (
-                (scales, w2_sraw[:, pair, :]),
-                (words.bitcast(U16), w2_raw[:, pair, :].bitcast(U16)),
-            ):
-                nc.vector.tensor_copy(
-                    out=target.rearrange("p e (t m) -> p e t m", t=PACK),
-                    in_=source.rearrange("p e (m t) -> p e t m", t=PACK),
-                )
-            for j in range(2):
-                w2[first + j], w2_s[first + j] = words[:, j, :], scales[:, j, :]
+        def permute(target, source):
+            nc.vector.tensor_copy(
+                out=target.rearrange("p e (t m) -> p e t m", t=PACK),
+                in_=source.rearrange("p e (m t) -> p e t m", t=PACK),
+            )
 
         def slots(e, part=ALL_SLOTS):
             return offsets[:, (e * C + part.start) // LIST_ROWS : (e * C + part.stop) // LIST_ROWS]
 
-        g_early = keep.tile([P, PACK, (E - 1) * C], F32, name="g_early")
-        g_planes = [g_early[:, :, e * C : (e + 1) * C] for e in range(E - 1)]
+        g_early = keep.tile([P, PACK, LAST * C], F32, name="g_early")
+        g_planes = [g_early[:, :, e * C : (e + 1) * C] for e in range(LAST)]
 
         def gather(first, count, t):
             run = slice(first * C, (first + count) * C)
             nc.vector.tensor_tensor(g_early[:, t, run], dy[t][:].indirect(slots(0, run)), gates_early[:, run], ALU.mult)
 
         def gather_last(t):
-            nc.scalar.activation(ungated[:, t, :], dy[t][:].indirect(slots(E - 1)), ACT.Copy)
+            nc.scalar.activation(ungated[:, t, :], dy[t][:].indirect(slots(LAST)), ACT.Copy)
 
         def interleave(copy, grouped, planes):
             copy(
-                out=grouped.rearrange("p (c i t) -> p c t i", i=RUN, t=PACK),
+                out=grouped.bitcast(BF16).rearrange("p (c i t) -> p c t i", i=RUN, t=PACK),
                 in_=planes.rearrange("p t (c i) -> p c t i", i=RUN),
             )
+
+        def by_slot(planes):
+            return planes.rearrange("p t c -> p c t")
+
+        g_by_slot = g_part.bitcast(BF16).rearrange("p (c t) -> p c t", t=PACK)
 
         def quantize(grouped, kind, operands=1, slot=None):
             if slot is None:
@@ -161,11 +161,11 @@ def tile_moe_bdx_mlp_silu_kernel(
             nc.vector.quantize_mx(out=codes[:].bitcast(FP8X4), scales=scales[:], in_=grouped.bitcast(BF16))
             return [(codes[:, j * C : (j + 1) * C], scales[:, j * C : (j + 1) * C]) for j in range(operands)]
 
-        def product(target, words, scales, tile, operand, part):
+        def product(target, weight_words, weight_scales, tile, operand, part):
             nc.tensor.matmul_mx(
                 out=target,
-                lhsT=words[:, 2 * P * tile : 2 * P * (tile + 1)].bitcast(FP4X4),
-                lhsT_scale=scales[:, P * tile : P * (tile + 1)],
+                lhsT=weight_words[:, 2 * P * tile : 2 * P * (tile + 1)].bitcast(FP4X4),
+                lhsT_scale=weight_scales[:, P * tile : P * (tile + 1)],
                 rhs=operand[0][:, part].bitcast(FP8X4),
                 rhs_scale=operand[1][:, part],
                 start=True,
@@ -181,47 +181,33 @@ def tile_moe_bdx_mlp_silu_kernel(
                 banks.append(bank)
             return banks
 
-        def through_silu(banks, slope, grouped):
+        def through_silu(banks, factor, grouped):
             for j, bank in enumerate(banks):
                 nc.vector.tensor_tensor(
                     grouped.bitcast(BF16)[:, j * C : (j + 1) * C].rearrange("p (c i t) -> p c t i", i=PAIR, t=PACK),
                     bank[:].rearrange("p (t c i) -> p c t i", i=PAIR, t=PACK),
-                    slope[:, :, j * P : (j + 1) * P].rearrange("p t (c i) -> p c t i", i=PAIR),
+                    factor[:, :, j * P : (j + 1) * P].rearrange("p t (c i) -> p c t i", i=PAIR),
                     ALU.mult,
                 )
 
-        def sigmoid(target, e, halves=(LOWER, UPPER)):
-            for planes in halves:
-                nc.scalar.activation(target[:, planes, :], pre[e][:, planes, :], ACT.Sigmoid)
+        def sigmoid(e, planes):
+            nc.scalar.activation(sigmoids[e][:, planes, :], pre[e][:, planes, :], ACT.Sigmoid)
 
-        def silu(target, e):
-            for planes in (LOWER, UPPER) if e == 0 else (slice(0, PACK),):
-                nc.scalar.activation(target[:, planes, :], pre[e][:, planes, :], ACT.Silu, scale=-1.0)
+        def silu(e):
+            nc.scalar.activation(silus[e][:], pre[e][:], ACT.Silu, scale=-1.0)
 
-        def slope_on_gpsimd(e):
-            rest = g_part.rearrange("p (t c) -> p t c", t=2)
-            for planes in (LOWER, UPPER):
-                nc.gpsimd.tensor_scalar(rest, silus[e][:, planes, :], -1.0, 1.0, ALU.mult, ALU.add)
-                nc.gpsimd.tensor_tensor(slopes[e][:, planes, :], slopes[e][:, planes, :], rest, ALU.mult)
+        def one_minus(engine, target, source):
+            engine.tensor_scalar(target, source, -1.0, 1.0, ALU.mult, ALU.add)
 
-        def one_minus(target, source):
-            nc.gpsimd.tensor_scalar(target, source, -1.0, 1.0, ALU.mult, ALU.add)
-
-        window = {}
-
-        def half_tile(engine, e, m, da_operand, nth):
-            half = SLOT_HALVES[nth]
-            scatter(engine, e, m, emptied(engine, e, m, da_operand, part=half), part=half)
-
-        def emptied(engine, e, m, da_operand, held=None, part=ALL_SLOTS, late=False):
+        def emptied(engine, e, m, da_operand, part=ALL_SLOTS, into=None, bank_of_dh=False):
             name = "vector" if engine is nc.vector else "scalar"
-            if late or (e == 0 and m in (0, 1, 4, 5)):
+            if bank_of_dh:
                 dx = psum_h.tile([P, C], F32, name="dh")
             else:
                 dx = psum_x.tile([P, C], F32, name="dx", tag=f"dx_{name}")
-            product(dx[:, part], w1_of[e], w1_s_of[e], m, da_operand, part)
-            result = held
-            if held is None:
+            product(dx[:, part], w1[:, e, :], w1_s[:, e, :], m, da_operand, part)
+            result = into
+            if into is None:
                 result = ring.tile([P, C], F32, name="result", tag=f"result_{name}", bufs=3)[:]
             if engine is nc.vector:
                 nc.vector.tensor_copy(result[:, part], dx[:, part])
@@ -229,130 +215,159 @@ def tile_moe_bdx_mlp_silu_kernel(
                 nc.scalar.copy(out=result[:, part], in_=dx[:, part])
             return result
 
+        window = {}
+
         def scatter(engine, e, m, result, part=ALL_SLOTS):
             if m not in window:
                 window[m] = keep.tile([P, T], F32, name=f"window{m}", tag=f"columns{m}", align_bytes=64)
             if engine is nc.vector:
                 nc.vector.tensor_copy(window[m][:].indirect(slots(e, part)), result[:, part])
             else:
-                for half in SLOT_HALVES if part == ALL_SLOTS else (part,):
-                    nc.scalar.activation(window[m][:].indirect(slots(e, half)), result[:, half], ACT.Copy)
-            if e == E - 1:
-                queue = nc.sync if engine is nc.vector else nc.scalar
-                queue.dma_start(out=out[m * P : (m + 1) * P, :], in_=window[m][:])
+                for piece in (FIRST_HALF, SECOND_HALF) if part == ALL_SLOTS else (part,):
+                    nc.scalar.activation(window[m][:].indirect(slots(e, piece)), result[:, piece], ACT.Copy)
 
-        def project(engine, e, tiles, da_operand):
+        def store(engine, m):
+            queue = nc.sync if engine is nc.vector else nc.scalar
+            queue.dma_start(out=out[m * P : (m + 1) * P, :], in_=window[m][:])
+
+        def project(engine, e, tiles, da_operand, in_banks_of_dh=()):
             waiting = None
             for m in tiles:
-                result = emptied(engine, e, m, da_operand)
+                result = emptied(engine, e, m, da_operand, bank_of_dh=m in in_banks_of_dh)
                 if waiting is not None:
                     scatter(engine, e, *waiting)
                 waiting = (m, result)
             scatter(engine, e, *waiting)
 
-        slopes = {0: keep.tile([P, PACK, C], F32, name="slope0", tag="slope0", align_bytes=64)}
+        def held_back(e, m, da_operand, part):
+            scatter(nc.vector, e, m, emptied(nc.vector, e, m, da_operand, part, bank_of_dh=True), part)
+
+        sigmoids = {0: keep.tile([P, PACK, C], F32, name="sigmoid0", tag="sigmoid0", align_bytes=64)}
         silus = {0: pre[0]}
-        sigmoid(slopes[0], 0, halves=(LOWER,))
+        sigmoid(0, LOWER)
+        nc.scalar.copy(out=gates[LAST], in_=spread(LAST))
         gather_last(0)
-        sigmoid(slopes[0], 0, halves=(UPPER,))
-        silu(silus[0], 0)
+        sigmoid(0, UPPER)
+        silu(0)
         gather_last(1)
         gather_last(2)
         for t in range(PACK - 1):
-            gather(0, E - 1, t)
+            gather(0, LAST, t)
         gather(0, 1, PACK - 1)
         gather(1, 2, PACK - 1)
         for e in (3, 2, 1):
             silus[e] = keep.tile([P, PACK, C], F32, name=f"silu{e}")
+        silu(3)
         gather_last(3)
-        silu(silus[3], 3)
         grouped_first = keep.tile([P, 2 * C], F32, name="grouped_first", tag="grouped", align_bytes=64)
-        interleave(nc.scalar.copy, grouped_first[:].bitcast(BF16), g_planes[0])
-        silu(silus[2], 2)
-        silu(silus[1], 1)
-        slopes[1] = keep.tile([P, PACK, C], F32, name="slope1")
-        slopes[2], slopes[3] = pre[1], pre[2]
+        interleave(nc.scalar.copy, grouped_first[:], g_planes[0])
+        silu(2)
+        silu(1)
+        sigmoids[1] = keep.tile([P, PACK, C], F32, name="sigmoid1")
+        sigmoids[2], sigmoids[3] = pre[1], pre[2]
         for e in (1, 2, 3):
-            sigmoid(slopes[e], e)
-        straddle = shared[:, 6 * C - LAP // 2 : 8 * C - LAP // 2]
-        interleave(nc.vector.tensor_copy, straddle.bitcast(BF16), g_planes[1])
-        nc.vector.tensor_scalar(silus[0][:], silus[0][:], -1.0, 1.0, ALU.mult, ALU.add)
-        nc.vector.tensor_tensor(slopes[0][:], slopes[0][:], silus[0][:], ALU.mult)
-        [g_operand] = quantize(grouped_first[:], "one")
-        permuted = keep.tile([P, 12 * H], U8, name="permuted", tag="pre0", align_bytes=64)
-        permute(0, permuted[:, 0 : 6 * H])
-        permute(2, permuted[:, 6 * H : 12 * H])
-        grouped_da = keep.tile([P, 2 * C], F32, name="grouped_da", tag="columns2", align_bytes=64)
-        through_silu(hidden_gradient(0, g_operand), slopes[0], grouped_da[:])
-        rest = keep.tile([P, PACK, C], F32, name="rest", tag="w2_raw", align_bytes=64)
-        one_minus(rest[:], silus[1][:])
-        [da_operand] = quantize(grouped_da[:], "one")
-        [g_operand] = quantize(straddle, "second", slot="slope0")
+            sigmoid(e, LOWER)
+            sigmoid(e, UPPER)
 
-        project(nc.vector, 0, (0, 1), da_operand)
-        first_half, second_half = SLOT_HALVES
-        half_tile(nc.scalar, 0, 2, da_operand, 0)
-        project(nc.scalar, 0, (4, 5, 3), da_operand)
+        grouped_second = shared[:, 6 * C - LAP // 2 : 8 * C - LAP // 2]
+        one_minus(nc.vector, rest_first, silus[0][:])
+        interleave(nc.vector.tensor_copy, grouped_second, g_planes[1])
+        nc.vector.tensor_tensor(sigmoids[0][:], sigmoids[0][:], rest_first, ALU.mult)
+        [g_operand] = quantize(grouped_first[:], "one")
+        permuted = keep.tile([P, (2 * E + 1) * H], U8, name="permuted", tag="grouped", align_bytes=64)
+        words = permuted[:, 0 : 2 * E * H].rearrange("p (e n) -> p e n", e=E)
+        packed = permuted[:, 2 * E * H :]
+        permute(packed.rearrange("p (e n) -> p e n", e=1), w2_sraw[:])
+        for experts in (slice(0, 1), slice(1, 2), slice(2, E)):
+            permute(words[:, experts, :].bitcast(U16), w2_raw[:, experts, :].bitcast(U16))
+        w2 = [words[:, e, :] for e in range(E)]
+        w2_s = [packed] + [w2_s_late[:, e - 1, :] for e in range(1, E)]
+        for e in range(1, E):
+            for q in range(QUADRANTS):
+                row = QUADRANT_ROWS * q
+                nc.sync.dma_start(
+                    out=w2_s[e][row : row + SCALE_ROWS].bitcast(I32),
+                    in_=packed[row + SCALE_ROWS * e : row + SCALE_ROWS * (e + 1)].bitcast(I32),
+                )
+        grouped_da = keep.tile([P, 2 * C], F32, name="grouped_da", tag="columns2", align_bytes=64)
+        through_silu(hidden_gradient(0, g_operand), sigmoids[0], grouped_da[:])
+        rest = keep.tile([P, PACK, C], F32, name="rest", tag="w2_raw", align_bytes=64)
+        one_minus(nc.gpsimd, rest[:], silus[1][:])
+        [da_operand] = quantize(grouped_da[:], "one")
+        [g_operand] = quantize(grouped_second, "second", slot="sigmoid0")
+
+        project(nc.vector, 0, (0, 1), da_operand, in_banks_of_dh=(0, 1))
+        scatter(nc.scalar, 0, 2, emptied(nc.scalar, 0, 2, da_operand, FIRST_HALF), FIRST_HALF)
+        project(nc.scalar, 0, (4, 5, 3), da_operand, in_banks_of_dh=(4, 5))
         banks = hidden_gradient(1, g_operand)
-        nc.gpsimd.tensor_scalar(
-            g_part.bitcast(BF16).rearrange("p (c t) -> p c t", t=PACK),
-            g_planes[2].rearrange("p t c -> p c t"),
-            1.0,
-            0.0,
-            ALU.mult,
-            ALU.add,
-        )
-        nc.gpsimd.tensor_tensor(slope, slopes[1][:], rest[:], ALU.mult)
+        nc.gpsimd.tensor_scalar(g_by_slot, by_slot(g_planes[2]), 1.0, 0.0, ALU.mult, ALU.add)
+        nc.gpsimd.tensor_tensor(slope, sigmoids[1][:], rest[:], ALU.mult)
         for planes in (LOWER, UPPER):
-            one_minus(rest[:, planes, :], silus[2][:, planes, :])
+            one_minus(nc.gpsimd, rest[:, planes, :], silus[2][:, planes, :])
         through_silu(banks, slope, da_part)
-        before = da_operand
+        da_before = da_operand
         g_operand, da_operand = quantize(both_parts, "both", operands=2)
-        scatter(nc.vector, 0, 2, emptied(nc.vector, 0, 2, before, part=second_half, late=True), part=second_half)
+        held_back(0, 2, da_before, SECOND_HALF)
 
         project(nc.vector, 1, (0, 1), da_operand)
         project(nc.scalar, 1, (4, 5, 3), da_operand)
         banks = hidden_gradient(2, g_operand)
-        for half in SLOT_HALVES:
-            if half.start > 0:
-                nc.gpsimd.tensor_tensor(slope, slopes[2][:], rest[:], ALU.mult)
+
+        def gate_last(half):
             nc.gpsimd.tensor_tensor(
-                g_part.bitcast(BF16).rearrange("p (c t) -> p c t", t=PACK)[:, half, :],
-                ungated[:, :, half].rearrange("p t c -> p c t"),
-                gates[E - 1][:, half].unsqueeze(2).to_broadcast([P, C // 2, PACK]),
+                g_by_slot[:, half, :],
+                by_slot(ungated[:, :, half]),
+                gates[LAST][:, half].unsqueeze(2).to_broadcast([P, C // 2, PACK]),
                 ALU.mult,
             )
-        one_minus(ungated[:, LOWER, :], silus[3][:, LOWER, :])
+
+        gate_last(FIRST_HALF)
+        nc.gpsimd.tensor_tensor(slope, sigmoids[2][:], rest[:], ALU.mult)
+        gate_last(SECOND_HALF)
+        rest_lower = ungated[:, LOWER, :]
+        one_minus(nc.gpsimd, rest_lower, silus[3][:, LOWER, :])
         through_silu(banks, slope, da_part)
-        before = da_operand
+        da_before = da_operand
         g_operand, da_operand = quantize(both_parts, "both", operands=2)
-        scatter(nc.vector, 1, 2, emptied(nc.vector, 1, 2, before, part=first_half, late=True), part=first_half)
-        earlier = before
+        held_back(1, 2, da_before, FIRST_HALF)
+        left_of_2 = keep.tile([P, 3 * C], F32, name="left_of_2", tag="pre0", align_bytes=64)
+        emptied(nc.scalar, 1, 2, da_before, SECOND_HALF, into=left_of_2[:, 0:C])
 
         project(nc.vector, 2, (0,), da_operand)
-        project(nc.scalar, 2, (4, 5, 3), da_operand)
-        half_tile(nc.vector, 2, 1, da_operand, 0)
+        scatter(nc.vector, 2, 1, emptied(nc.vector, 2, 1, da_operand, FIRST_HALF), FIRST_HALF)
+        result_4 = emptied(nc.scalar, 2, 4, da_operand)
         banks = hidden_gradient(3, g_operand)
+        result_5 = emptied(nc.scalar, 2, 5, da_operand)
+        scatter(nc.scalar, 2, 4, result_4)
+        scatter(nc.scalar, 2, 5, result_5)
+        emptied(nc.scalar, 2, 2, da_operand, into=left_of_2[:, C : 2 * C])
+        left_of_3 = keep.tile([P, 2 * C], F32, name="left_of_3", tag="sigmoid0", align_bytes=64)
+        emptied(nc.scalar, 2, 3, da_operand, into=left_of_3[:, 0:C])
+        scatter(nc.scalar, 2, 3, left_of_3[:, 0:C], FIRST_HALF)
         rest_upper = g_part.rearrange("p (t c) -> p t c", t=2)
-        nc.gpsimd.tensor_tensor(slope[:, LOWER, :], slopes[3][:, LOWER, :], ungated[:, LOWER, :], ALU.mult)
-        one_minus(rest_upper, silus[3][:, UPPER, :])
-        nc.gpsimd.tensor_tensor(slope[:, UPPER, :], slopes[3][:, UPPER, :], rest_upper, ALU.mult)
+        nc.gpsimd.tensor_tensor(slope[:, LOWER, :], sigmoids[3][:, LOWER, :], rest_lower, ALU.mult)
+        one_minus(nc.gpsimd, rest_upper, silus[3][:, UPPER, :])
+        nc.gpsimd.tensor_tensor(slope[:, UPPER, :], sigmoids[3][:, UPPER, :], rest_upper, ALU.mult)
         through_silu(banks, slope, da_part)
-        before = da_operand
+        da_before = da_operand
         [da_operand] = quantize(da_part, "one")
-        scatter(nc.vector, 2, 1, emptied(nc.vector, 2, 1, before, part=second_half, late=True), part=second_half)
-        results = [emptied(nc.vector, 3, m, da_operand) for m in (0, 1)]
-        scatter(nc.vector, 3, 0, results[0])
-        joint = shared[:, 11 * C // 2 : 17 * C // 2]
-        emptied(nc.vector, 1, 2, earlier, held=joint[:, 0:C], part=second_half)
-        emptied(nc.vector, 2, 2, before, held=joint[:, C : 2 * C])
-        emptied(nc.vector, 3, 2, da_operand, held=joint[:, 2 * C : 3 * C])
-        scatter(nc.vector, 3, 1, results[1])
-        nc.vector.tensor_copy(window[2][:].indirect(slots(1, slice(C // 2, 3 * C))), joint[:, C // 2 :])
-        nc.sync.dma_start(out=out[2 * P : 3 * P, :], in_=window[2][:])
-        turn = keep.tile([P, C], F32, name="turn", tag="grouped", align_bytes=64)
-        results = [emptied(nc.scalar, 3, 4, da_operand, held=turn[:]), emptied(nc.scalar, 3, 5, da_operand)]
-        scatter(nc.scalar, 3, 4, results[0])
-        emptied(nc.scalar, 3, 3, da_operand, held=turn[:])
-        scatter(nc.scalar, 3, 5, results[1])
-        scatter(nc.scalar, 3, 3, turn[:])
+        held_back(2, 1, da_before, SECOND_HALF)
+
+        result_4 = emptied(nc.scalar, 3, 4, da_operand, into=left_of_3[:, C : 2 * C])
+        result_0, result_1 = [emptied(nc.vector, 3, m, da_operand) for m in (0, 1)]
+        scatter(nc.vector, 3, 0, result_0)
+        store(nc.vector, 0)
+        emptied(nc.vector, 3, 2, da_operand, into=left_of_2[:, 2 * C : 3 * C])
+        scatter(nc.vector, 3, 1, result_1)
+        store(nc.vector, 1)
+        scatter(nc.vector, 1, 2, left_of_2[:], slice(C // 2, 3 * C))
+        store(nc.vector, 2)
+        result_5 = emptied(nc.scalar, 3, 5, da_operand)
+        scatter(nc.scalar, 3, 4, result_4)
+        store(nc.scalar, 4)
+        emptied(nc.scalar, 3, 3, da_operand, into=left_of_3[:, C : 2 * C])
+        scatter(nc.scalar, 3, 5, result_5)
+        store(nc.scalar, 5)
+        for piece in (slice(C // 2, 5 * C // 4), slice(5 * C // 4, 2 * C)):
+            scatter(nc.scalar, 2, 3, left_of_3[:], piece)
+        store(nc.scalar, 3)

@@ -37,30 +37,35 @@ def tile_moe_bdx_mlp_silu_kernel(
     nc = tc.nc
     with ExitStack() as ctx:
         keep = ctx.enter_context(tc.tile_pool(name="keep", bufs=1))
+        head = ctx.enter_context(tc.tile_pool(name="head", bufs=1))
         ring = ctx.enter_context(tc.tile_pool(name="ring", bufs=2))
         psum_h = ctx.enter_context(tc.psum_pool(name="psum_h", bufs=4))
         psum_x = ctx.enter_context(tc.psum_pool(name="psum_x", bufs=2))
 
+        def floats(name, width, tag=""):
+            return keep.tile([P, width], F32, name=name, tag=tag, align_bytes=64)
+
+        def planes(region):
+            return region.rearrange("p (t c) -> p t c", t=PACK)
+
         offsets = keep.tile([P, E * C // LIST_ROWS], U16, name="offsets")
-        dy = [keep.tile([P, T], F32, name=f"dy{t}", tag=f"columns{t}", align_bytes=64) for t in range(PACK)]
-        pre = [keep.tile([P, PACK, C], F32, name=f"pre{e}", tag=f"pre{e}", align_bytes=64) for e in range(E)]
-        w2_raw = keep.tile([P, E, 2 * H], U8, name="w2_raw", tag="w2_raw", align_bytes=64)
+        dy = [floats(f"dy{t}", T, tag=f"columns{t}") for t in range(PACK)]
+        pre_first = [floats(f"pre_first{j}", 2 * C, tag=f"pre_first{j}") for j in range(2)]
+        pre_later = floats("pre_later", 12 * C)
+        pre = {1: pre_later[:, 0 : 4 * C], 3: pre_later[:, 4 * C : 8 * C], 2: pre_later[:, 8 * C : 12 * C]}
+        sigmoids = [floats(f"sigmoid{e}", 4 * C, tag=f"sigmoid{e}") for e in range(E)]
+        w2_raw = keep.tile([P, E, 2 * H], U8, name="w2_raw", align_bytes=64)
         w2_sraw = keep.tile([P, 1, H], U8, name="w2_sraw", align_bytes=64)
         w2_s_late = keep.tile([P, LAST, H], U8, name="w2_s_late", align_bytes=64)
         w1 = keep.tile([P, E, 2 * K], U8, name="w1", align_bytes=64)
         w1_s = keep.tile([P, E, K], U8, name="w1_s", align_bytes=64)
-        gates_row = keep.tile([P, 6 * C], F32, name="gates_row", align_bytes=64)
-        gates_early = gates_row[:, 3 * C : 6 * C]
-        rest_first = gates_row[:, 0 : 4 * C].rearrange("p (t c) -> p t c", t=PACK)
-        gates_last = keep.tile([P, C], F32, name="gates_last", align_bytes=64)
-        gates = [gates_early[:, e * C : (e + 1) * C] for e in range(LAST)] + [gates_last[:]]
-        shared = keep.tile([P, 12 * C], F32, name="shared", align_bytes=64)
-        ungated = shared[:, 0 : 4 * C].rearrange("p (t c) -> p t c", t=PACK)
-        g_part, da_part = [shared[:, j * C : (j + 2) * C] for j in (4, 6)]
-        both_parts = shared[:, 4 * C : 8 * C]
-        slope = shared[:, 8 * C - LAP : 12 * C - LAP].rearrange("p (t c) -> p t c", t=PACK)
+        row = floats("row", 11 * C)
+        rest, shared = row[:, 0 : 4 * C], row[:, 3 * C : 11 * C]
+        g_part, da_part, both_parts = shared[:, 0 : 2 * C], shared[:, 2 * C : 4 * C], shared[:, 0 : 4 * C]
+        g_first = shared[:, C - LAP : 3 * C - LAP]
+        slope_flat = shared[:, 4 * C - LAP : 8 * C - LAP]
+        slope = planes(slope_flat)
 
-        nc.vector.memset(w2_sraw[:].bitcast(I32), 0)
         nc.vector.memset(w1_s[:].bitcast(I32), 0)
         nc.vector.memset(w2_s_late[:].bitcast(I32), 0)
 
@@ -70,17 +75,22 @@ def tile_moe_bdx_mlp_silu_kernel(
         def load_words(target, source):
             nc.sync.dma_start(out=target[:].bitcast(I32), in_=source.rearrange("e o p n -> p (e o) n").bitcast(I32))
 
-        def load_dy(t, tokens=slice(0, T)):
-            nc.sync.dma_start(out=dy[t][:, tokens], in_=dy_rows[:, t, tokens])
+        def load_dy(t):
+            nc.sync.dma_start(out=dy[t][:], in_=dy_rows[:, t, :])
 
-        def load_pre(e, planes=slice(0, PACK)):
-            nc.sync.dma_start(out=pre[e][:, planes, :], in_=a_rows[:, planes, e * C : (e + 1) * C])
+        def load_pre(e):
+            nc.sync.dma_start(out=planes(pre[e]), in_=a_rows[:, :, e * C : (e + 1) * C])
+
+        def load_pre_first(j):
+            target = pre_first[j][:].rearrange("p (t c) -> p t c", t=2)
+            nc.sync.dma_start(out=target, in_=a_rows[:, 2 * j : 2 * j + 2, 0:C])
 
         blocks = E * C // P
         gate_rows = keep.tile([P, P], F32, name="gate_rows")
-        gate_columns = keep.tile([P, blocks], F32, name="gate_columns")
+        gate_columns = keep.tile([P, blocks], F32, name="gate_columns", tag="gathered0", align_bytes=64)
         identity = keep.tile([P, P], F32, name="identity")
         nc.gpsimd.memset(gate_rows[:], 0.0)
+        nc.gpsimd.memset(w2_sraw[:].bitcast(I32), 0)
         nc.sync.dma_start(out=offsets[:], in_=offs)
         nc.sync.dma_start(out=gate_rows[0:blocks, :], in_=gate[0, :].rearrange("(b c) -> b c", c=P))
         make_identity(nc, identity[:])
@@ -96,25 +106,28 @@ def tile_moe_bdx_mlp_silu_kernel(
                 nc.tensor.transpose(bank[:, j * P : (j + 1) * P], column, identity[:])
             return bank[:]
 
-        for e in range(LAST):
-            nc.vector.tensor_copy(gates[e], spread(e))
+        gates = {e: floats(f"gates{e}", C, tag=f"gates{e}") for e in (2, 3)}
+        for e in (2, 3):
+            nc.vector.tensor_copy(gates[e][:], spread(e))
+        gate_banks = [spread(e) for e in (0, 1)]
+        gates_second = floats("gates_second", C // 2, tag="gates_second")
+        nc.vector.tensor_copy(gates_second[:], gate_banks[1][:, SECOND_HALF])
 
-        load_pre(0, LOWER)
-        load_dy(0, slice(0, T // 2))
-        load_dy(0, slice(T // 2, T))
-        load_pre(0, UPPER)
-        load_dy(1)
-        load_dy(2)
-        load_pre(3)
-        load_dy(3)
-        load_pre(2)
-        load_pre(1)
+        gathered = [keep.tile([P, PACK, 2 * C], F32, name=f"gathered{j}", tag=f"gathered{j}", align_bytes=64) for j in range(2)]
+        ungated = [gathered[e // 2][:, :, (e % 2) * C : (e % 2 + 1) * C] for e in range(E)]
+
+        load_pre_first(0)
+        load_pre_first(1)
+        for t in range(PACK):
+            load_dy(t)
         load_words(w2_raw, w2_words)
         for q in range(QUADRANTS):
             nc.sync.dma_start(
                 out=w2_sraw[QUADRANT_ROWS * q : QUADRANT_ROWS * q + E * SCALE_ROWS, 0, :].bitcast(I32),
                 in_=w2_scales[:, 0, SCALE_ROWS * q : SCALE_ROWS * (q + 1), :].bitcast(I32),
             )
+        for e in (1, 2, 3):
+            load_pre(e)
         for q in range(QUADRANTS):
             nc.sync.dma_start(
                 out=w1_s[QUADRANT_ROWS * q : QUADRANT_ROWS * q + SCALE_ROWS].bitcast(I32),
@@ -122,8 +135,8 @@ def tile_moe_bdx_mlp_silu_kernel(
             )
         load_words(w1, w1_words)
 
-        def permute(target, source):
-            nc.vector.tensor_copy(
+        def permute(copy, target, source):
+            copy(
                 out=target.rearrange("p e (t m) -> p e t m", t=PACK),
                 in_=source.rearrange("p e (m t) -> p e t m", t=PACK),
             )
@@ -131,32 +144,40 @@ def tile_moe_bdx_mlp_silu_kernel(
         def slots(e, part=ALL_SLOTS):
             return offsets[:, (e * C + part.start) // LIST_ROWS : (e * C + part.stop) // LIST_ROWS]
 
-        g_early = keep.tile([P, PACK, LAST * C], F32, name="g_early")
-        g_planes = [g_early[:, :, e * C : (e + 1) * C] for e in range(LAST)]
+        def gather(engine, t, e, count):
+            first = (e % 2) * C
+            target = gathered[e // 2][:, t, first : first + count * C]
+            window = dy[t][:].indirect(slots(e, slice(0, count * C)))
+            if engine is nc.vector:
+                nc.vector.tensor_copy(target, window)
+            else:
+                nc.scalar.activation(target, window, ACT.Copy)
 
-        def gather(first, count, t):
-            run = slice(first * C, (first + count) * C)
-            nc.vector.tensor_tensor(g_early[:, t, run], dy[t][:].indirect(slots(0, run)), gates_early[:, run], ALU.mult)
+        def by_slot(source):
+            return source.rearrange("p t c -> p c t")
 
-        def gather_last(t):
-            nc.scalar.activation(ungated[:, t, :], dy[t][:].indirect(slots(LAST)), ACT.Copy)
-
-        def interleave(copy, grouped, planes):
-            copy(
-                out=grouped.bitcast(BF16).rearrange("p (c i t) -> p c t i", i=RUN, t=PACK),
-                in_=planes.rearrange("p t (c i) -> p c t i", i=RUN),
+        def gate_on_vector(target, source, bank):
+            width = bank.shape[1]
+            nc.vector.tensor_tensor(
+                target.bitcast(BF16).rearrange("p (c i t) -> p c t i", i=PAIR, t=PACK),
+                source.rearrange("p t (c i) -> p c t i", i=PAIR),
+                bank.rearrange("p (c i) -> p c i", i=PAIR).unsqueeze(2).to_broadcast([P, width // PAIR, PACK, PAIR]),
+                ALU.mult,
             )
 
-        def by_slot(planes):
-            return planes.rearrange("p t c -> p c t")
+        def gate_on_gpsimd(target, source, row):
+            nc.gpsimd.tensor_tensor(
+                target.bitcast(BF16).rearrange("p (c t) -> p c t", t=PACK),
+                by_slot(source),
+                row.unsqueeze(2).to_broadcast([P, row.shape[1], PACK]),
+                ALU.mult,
+            )
 
-        g_by_slot = g_part.bitcast(BF16).rearrange("p (c t) -> p c t", t=PACK)
-
-        def quantize(grouped, kind, operands=1, slot=None):
-            if slot is None:
+        def quantize(grouped, kind, operands=1, offset=None):
+            if offset is None:
                 codes = ring.tile([P, operands * C], U32, name=f"codes_{kind}", align_bytes=64)
             else:
-                codes = keep.tile([P, operands * C], U32, name=f"codes_{kind}", tag=slot, align_bytes=64)
+                codes = head.tile([P, operands * C], U32, name=f"codes_{kind}", offset=offset, align_bytes=64)
             scales = ring.tile([P, operands * C], U8, name=f"scales_{kind}", align_bytes=64)
             nc.vector.quantize_mx(out=codes[:].bitcast(FP8X4), scales=scales[:], in_=grouped.bitcast(BF16))
             return [(codes[:, j * C : (j + 1) * C], scales[:, j * C : (j + 1) * C]) for j in range(operands)]
@@ -190,14 +211,14 @@ def tile_moe_bdx_mlp_silu_kernel(
                     ALU.mult,
                 )
 
-        def sigmoid(e, planes):
-            nc.scalar.activation(sigmoids[e][:, planes, :], pre[e][:, planes, :], ACT.Sigmoid)
+        def sigmoid(target, source):
+            nc.scalar.activation(target, source, ACT.Sigmoid)
 
-        def silu(e):
-            nc.scalar.activation(silus[e][:], pre[e][:], ACT.Silu, scale=-1.0)
+        def silu(part):
+            nc.scalar.activation(pre_later[:, part], pre_later[:, part], ACT.Silu, scale=-1.0)
 
-        def one_minus(engine, target, source):
-            engine.tensor_scalar(target, source, -1.0, 1.0, ALU.mult, ALU.add)
+        def one_minus(target, source):
+            nc.gpsimd.tensor_scalar(target, source, -1.0, 1.0, ALU.mult, ALU.add)
 
         def emptied(engine, e, m, da_operand, part=ALL_SLOTS, into=None, bank_of_dh=False):
             name = "vector" if engine is nc.vector else "scalar"
@@ -242,132 +263,120 @@ def tile_moe_bdx_mlp_silu_kernel(
         def held_back(e, m, da_operand, part):
             scatter(nc.vector, e, m, emptied(nc.vector, e, m, da_operand, part, bank_of_dh=True), part)
 
-        sigmoids = {0: keep.tile([P, PACK, C], F32, name="sigmoid0", tag="sigmoid0", align_bytes=64)}
-        silus = {0: pre[0]}
-        sigmoid(0, LOWER)
-        nc.scalar.copy(out=gates[LAST], in_=spread(LAST))
-        gather_last(0)
-        sigmoid(0, UPPER)
-        silu(0)
-        gather_last(1)
-        gather_last(2)
+        halves = (slice(0, 2 * C), slice(2 * C, 4 * C))
+        for j, half in enumerate(halves):
+            sigmoid(sigmoids[0][:, half], pre_first[j][:])
         for t in range(PACK - 1):
-            gather(0, LAST, t)
-        gather(0, 1, PACK - 1)
-        gather(1, 2, PACK - 1)
-        for e in (3, 2, 1):
-            silus[e] = keep.tile([P, PACK, C], F32, name=f"silu{e}")
-        silu(3)
-        gather_last(3)
-        grouped_first = keep.tile([P, 2 * C], F32, name="grouped_first", tag="grouped", align_bytes=64)
-        interleave(nc.scalar.copy, grouped_first[:], g_planes[0])
-        silu(2)
-        silu(1)
-        sigmoids[1] = keep.tile([P, PACK, C], F32, name="sigmoid1")
-        sigmoids[2], sigmoids[3] = pre[1], pre[2]
+            gather(nc.vector, t, 0, 2)
+            gather(nc.scalar, t, 2, 2)
+        gather(nc.vector, PACK - 1, 0, 1)
+        gather(nc.scalar, PACK - 1, 1, 1)
+        gather(nc.scalar, PACK - 1, 2, 2)
         for e in (1, 2, 3):
-            sigmoid(e, LOWER)
-            sigmoid(e, UPPER)
+            sigmoid(sigmoids[e][:], pre[e])
+        silu(slice(0, 4 * C + LAP))
+        silu(slice(8 * C - LAP, 12 * C))
+        silu(slice(4 * C + LAP, 8 * C - LAP))
 
-        grouped_second = shared[:, 6 * C - LAP // 2 : 8 * C - LAP // 2]
-        one_minus(nc.vector, rest_first, silus[0][:])
-        interleave(nc.vector.tensor_copy, grouped_second, g_planes[1])
-        nc.vector.tensor_tensor(sigmoids[0][:], sigmoids[0][:], rest_first, ALU.mult)
-        [g_operand] = quantize(grouped_first[:], "one")
-        permuted = keep.tile([P, (2 * E + 1) * H], U8, name="permuted", tag="grouped", align_bytes=64)
-        words = permuted[:, 0 : 2 * E * H].rearrange("p (e n) -> p e n", e=E)
-        packed = permuted[:, 2 * E * H :]
-        permute(packed.rearrange("p (e n) -> p e n", e=1), w2_sraw[:])
-        for experts in (slice(0, 1), slice(1, 2), slice(2, E)):
-            permute(words[:, experts, :].bitcast(U16), w2_raw[:, experts, :].bitcast(U16))
-        w2 = [words[:, e, :] for e in range(E)]
+        work = head.tile([P, 4 * C], F32, name="work", offset=0, align_bytes=64)
+        lower, upper = halves
+        one_minus(work[:, lower], sigmoids[0][:, lower])
+        nc.gpsimd.tensor_tensor(work[:, lower], work[:, lower], pre_first[0][:], ALU.mult)
+        nc.gpsimd.tensor_scalar(work[:, lower], work[:, lower], 1.0, 1.0, ALU.mult, ALU.add)
+        nc.gpsimd.tensor_tensor(slope_flat[:, lower], work[:, lower], sigmoids[0][:, lower], ALU.mult)
+        one_minus(work[:, upper], sigmoids[0][:, upper])
+        nc.gpsimd.tensor_tensor(slope_flat[:, upper], work[:, upper], pre_first[1][:], ALU.mult)
+
+        gate_on_vector(g_first, ungated[0], gate_banks[0])
+        nc.vector.scalar_tensor_tensor(
+            slope_flat[:, upper], slope_flat[:, upper], 1.0, sigmoids[0][:, upper], ALU.add, ALU.mult
+        )
+        permuted = head.tile([P, 5 * H], U8, name="permuted", offset=0, align_bytes=64)
+        words = permuted[:, 0 : 4 * H].rearrange("p (e n) -> p e n", e=2)
+        packed = permuted[:, 4 * H : 5 * H]
+        permute(nc.vector.tensor_copy, packed.rearrange("p (e n) -> p e n", e=1), w2_sraw[:])
+        permute(nc.vector.tensor_copy, words.bitcast(U16), w2_raw[:, 0:2, :].bitcast(U16))
+        [g_operand] = quantize(g_first, "first", offset=8 * C)
+        words_late = keep.tile([P, 2, 2 * H], U8, name="words_late", tag="gates_second", align_bytes=64)
+        w2 = [words[:, 0, :], words[:, 1, :], words_late[:, 0, :], words_late[:, 1, :]]
         w2_s = [packed] + [w2_s_late[:, e - 1, :] for e in range(1, E)]
         for e in range(1, E):
             for q in range(QUADRANTS):
-                row = QUADRANT_ROWS * q
+                top = QUADRANT_ROWS * q
                 nc.sync.dma_start(
-                    out=w2_s[e][row : row + SCALE_ROWS].bitcast(I32),
-                    in_=packed[row + SCALE_ROWS * e : row + SCALE_ROWS * (e + 1)].bitcast(I32),
+                    out=w2_s[e][top : top + SCALE_ROWS].bitcast(I32),
+                    in_=packed[top + SCALE_ROWS * e : top + SCALE_ROWS * (e + 1)].bitcast(I32),
                 )
-        grouped_da = keep.tile([P, 2 * C], F32, name="grouped_da", tag="columns2", align_bytes=64)
-        through_silu(hidden_gradient(0, g_operand), sigmoids[0], grouped_da[:])
-        rest = keep.tile([P, PACK, C], F32, name="rest", tag="w2_raw", align_bytes=64)
-        one_minus(nc.gpsimd, rest[:], silus[1][:])
-        [da_operand] = quantize(grouped_da[:], "one")
-        [g_operand] = quantize(grouped_second, "second", slot="sigmoid0")
+        gate_on_gpsimd(g_part[:, C : 2 * C], ungated[1][:, :, SECOND_HALF], gates_second[:])
+        through_silu(hidden_gradient(0, g_operand), slope, da_part)
+        gate_on_vector(g_part[:, 0:C], ungated[1][:, :, FIRST_HALF], gate_banks[1][:, FIRST_HALF])
+        permute(nc.vector.tensor_copy, words_late[:].bitcast(U16), w2_raw[:, 2:E, :].bitcast(U16))
+        [da_operand] = quantize(da_part, "one")
+        [g_operand] = quantize(g_part, "second")
 
+        def behind_quantisation(e, m, operand, part):
+            scatter(nc.vector, e, m, emptied(nc.vector, e, m, operand, part, into=da_part[:, 0:C]), part)
+
+        def half_result(engine, e, m, operand, part):
+            scatter(engine, e, m, emptied(engine, e, m, operand, part), part)
+
+        def make_slope(e):
+            one_minus(rest, pre[e])
+            nc.gpsimd.tensor_tensor(slope, planes(sigmoids[e][:]), planes(rest), ALU.mult)
+
+        half_result(nc.vector, 0, 3, da_operand, FIRST_HALF)
         project(nc.vector, 0, (0, 1), da_operand, in_banks_of_dh=(0, 1))
-        scatter(nc.scalar, 0, 2, emptied(nc.scalar, 0, 2, da_operand, FIRST_HALF), FIRST_HALF)
-        project(nc.scalar, 0, (4, 5, 3), da_operand, in_banks_of_dh=(4, 5))
+        half_result(nc.scalar, 0, 2, da_operand, FIRST_HALF)
+        project(nc.scalar, 0, (4, 5), da_operand)
+        half_result(nc.scalar, 0, 3, da_operand, SECOND_HALF)
         banks = hidden_gradient(1, g_operand)
-        nc.gpsimd.tensor_scalar(g_by_slot, by_slot(g_planes[2]), 1.0, 0.0, ALU.mult, ALU.add)
-        nc.gpsimd.tensor_tensor(slope, sigmoids[1][:], rest[:], ALU.mult)
-        for planes in (LOWER, UPPER):
-            one_minus(nc.gpsimd, rest[:, planes, :], silus[2][:, planes, :])
+        gate_on_gpsimd(g_part[:, C : 2 * C], ungated[2][:, :, SECOND_HALF], gates[2][:, SECOND_HALF])
+        make_slope(1)
+        gate_on_gpsimd(g_part[:, 0:C], ungated[2][:, :, FIRST_HALF], gates[2][:, FIRST_HALF])
         through_silu(banks, slope, da_part)
         da_before = da_operand
         g_operand, da_operand = quantize(both_parts, "both", operands=2)
-        held_back(0, 2, da_before, SECOND_HALF)
+        behind_quantisation(0, 2, da_before, SECOND_HALF)
 
+        half_result(nc.scalar, 1, 2, da_operand, FIRST_HALF)
         project(nc.vector, 1, (0, 1), da_operand)
         project(nc.scalar, 1, (4, 5, 3), da_operand)
         banks = hidden_gradient(2, g_operand)
-
-        def gate_last(half):
-            nc.gpsimd.tensor_tensor(
-                g_by_slot[:, half, :],
-                by_slot(ungated[:, :, half]),
-                gates[LAST][:, half].unsqueeze(2).to_broadcast([P, C // 2, PACK]),
-                ALU.mult,
-            )
-
-        gate_last(FIRST_HALF)
-        nc.gpsimd.tensor_tensor(slope, sigmoids[2][:], rest[:], ALU.mult)
-        gate_last(SECOND_HALF)
-        rest_lower = ungated[:, LOWER, :]
-        one_minus(nc.gpsimd, rest_lower, silus[3][:, LOWER, :])
+        make_slope(2)
+        gate_on_gpsimd(g_part, ungated[3], gates[3][:])
         through_silu(banks, slope, da_part)
         da_before = da_operand
         g_operand, da_operand = quantize(both_parts, "both", operands=2)
-        held_back(1, 2, da_before, FIRST_HALF)
-        left_of_2 = keep.tile([P, 3 * C], F32, name="left_of_2", tag="pre0", align_bytes=64)
-        emptied(nc.scalar, 1, 2, da_before, SECOND_HALF, into=left_of_2[:, 0:C])
+        behind_quantisation(1, 2, da_before, SECOND_HALF)
 
-        project(nc.vector, 2, (0,), da_operand)
-        scatter(nc.vector, 2, 1, emptied(nc.vector, 2, 1, da_operand, FIRST_HALF), FIRST_HALF)
         result_4 = emptied(nc.scalar, 2, 4, da_operand)
+        project(nc.vector, 2, (0,), da_operand)
+        half_result(nc.vector, 2, 1, da_operand, FIRST_HALF)
         banks = hidden_gradient(3, g_operand)
-        result_5 = emptied(nc.scalar, 2, 5, da_operand)
         scatter(nc.scalar, 2, 4, result_4)
-        scatter(nc.scalar, 2, 5, result_5)
-        emptied(nc.scalar, 2, 2, da_operand, into=left_of_2[:, C : 2 * C])
-        left_of_3 = keep.tile([P, 2 * C], F32, name="left_of_3", tag="sigmoid0", align_bytes=64)
-        emptied(nc.scalar, 2, 3, da_operand, into=left_of_3[:, 0:C])
-        scatter(nc.scalar, 2, 3, left_of_3[:, 0:C], FIRST_HALF)
-        rest_upper = g_part.rearrange("p (t c) -> p t c", t=2)
-        nc.gpsimd.tensor_tensor(slope[:, LOWER, :], sigmoids[3][:, LOWER, :], rest_lower, ALU.mult)
-        one_minus(nc.gpsimd, rest_upper, silus[3][:, UPPER, :])
-        nc.gpsimd.tensor_tensor(slope[:, UPPER, :], sigmoids[3][:, UPPER, :], rest_upper, ALU.mult)
+        project(nc.scalar, 2, (5, 3), da_operand)
+        left_of_2 = floats("left_of_2", 2 * C)
+        emptied(nc.scalar, 2, 2, da_operand, into=left_of_2[:, 0:C])
+        make_slope(3)
         through_silu(banks, slope, da_part)
         da_before = da_operand
         [da_operand] = quantize(da_part, "one")
-        held_back(2, 1, da_before, SECOND_HALF)
+        behind_quantisation(2, 1, da_before, SECOND_HALF)
 
-        result_4 = emptied(nc.scalar, 3, 4, da_operand, into=left_of_3[:, C : 2 * C])
+        result_4 = emptied(nc.scalar, 3, 4, da_operand)
         result_0, result_1 = [emptied(nc.vector, 3, m, da_operand) for m in (0, 1)]
         scatter(nc.vector, 3, 0, result_0)
         store(nc.vector, 0)
-        emptied(nc.vector, 3, 2, da_operand, into=left_of_2[:, 2 * C : 3 * C])
+        emptied(nc.vector, 3, 2, da_operand, into=left_of_2[:, C : 2 * C])
         scatter(nc.vector, 3, 1, result_1)
         store(nc.vector, 1)
-        scatter(nc.vector, 1, 2, left_of_2[:], slice(C // 2, 3 * C))
+        scatter(nc.vector, 2, 2, left_of_2[:], slice(0, 2 * C))
         store(nc.vector, 2)
         result_5 = emptied(nc.scalar, 3, 5, da_operand)
         scatter(nc.scalar, 3, 4, result_4)
         store(nc.scalar, 4)
-        emptied(nc.scalar, 3, 3, da_operand, into=left_of_3[:, C : 2 * C])
+        result_3 = emptied(nc.scalar, 3, 3, da_operand)
         scatter(nc.scalar, 3, 5, result_5)
         store(nc.scalar, 5)
-        for piece in (slice(C // 2, 5 * C // 4), slice(5 * C // 4, 2 * C)):
-            scatter(nc.scalar, 2, 3, left_of_3[:], piece)
+        scatter(nc.scalar, 3, 3, result_3)
         store(nc.scalar, 3)

@@ -59,8 +59,7 @@ def tile_moe_bdx_mlp_silu_kernel(
         w2_s_late = keep.tile([P, LAST, H], U8, name="w2_s_late", align_bytes=64)
         w1 = keep.tile([P, E, 2 * K], U8, name="w1", align_bytes=64)
         w1_s = keep.tile([P, E, K], U8, name="w1_s", align_bytes=64)
-        row = floats("row", 11 * C)
-        rest, shared = row[:, 0 : 4 * C], row[:, 3 * C : 11 * C]
+        shared = floats("shared", 8 * C)
         g_part, da_part, both_parts = shared[:, 0 : 2 * C], shared[:, 2 * C : 4 * C], shared[:, 0 : 4 * C]
         g_first = shared[:, C - LAP : 3 * C - LAP]
         slope_flat = shared[:, 4 * C - LAP : 8 * C - LAP]
@@ -96,7 +95,7 @@ def tile_moe_bdx_mlp_silu_kernel(
         make_identity(nc, identity[:])
         turned = psum_h.tile([P, C], F32, name="dh")
         nc.tensor.transpose(turned[:, 0:P], gate_rows[:], identity[:])
-        nc.vector.tensor_copy(gate_columns[:], turned[:, 0:blocks])
+        nc.vector.tensor_scalar(gate_columns[:], turned[:, 0:blocks], -1.0, None, ALU.mult)
 
         def spread(e):
             bank = psum_x.tile([P, C], F32, name="spread", tag=("dx_vector", "dx_scalar")[e % 2])
@@ -144,10 +143,10 @@ def tile_moe_bdx_mlp_silu_kernel(
         def slots(e, part=ALL_SLOTS):
             return offsets[:, (e * C + part.start) // LIST_ROWS : (e * C + part.stop) // LIST_ROWS]
 
-        def gather(engine, t, e, count):
+        def gather(engine, t, e, part):
             first = (e % 2) * C
-            target = gathered[e // 2][:, t, first : first + count * C]
-            window = dy[t][:].indirect(slots(e, slice(0, count * C)))
+            target = gathered[e // 2][:, t, first + part.start : first + part.stop]
+            window = dy[t][:].indirect(slots(e, part))
             if engine is nc.vector:
                 nc.vector.tensor_copy(target, window)
             else:
@@ -217,8 +216,11 @@ def tile_moe_bdx_mlp_silu_kernel(
         def silu(part):
             nc.scalar.activation(pre_later[:, part], pre_later[:, part], ACT.Silu, scale=-1.0)
 
-        def one_minus(target, source):
-            nc.gpsimd.tensor_scalar(target, source, -1.0, 1.0, ALU.mult, ALU.add)
+        def minus_one(target, source):
+            nc.gpsimd.tensor_scalar(target, source, 1.0, -1.0, ALU.mult, ALU.add)
+
+        def less_one_times(target, first, second):
+            nc.vector.scalar_tensor_tensor(target, first, 1.0, second, ALU.subtract, ALU.mult)
 
         def emptied(engine, e, m, da_operand, part=ALL_SLOTS, into=None, bank_of_dh=False):
             name = "vector" if engine is nc.vector else "scalar"
@@ -229,7 +231,7 @@ def tile_moe_bdx_mlp_silu_kernel(
             product(dx[:, part], w1[:, e, :], w1_s[:, e, :], m, da_operand, part)
             result = into
             if into is None:
-                result = ring.tile([P, C], F32, name="result", tag=f"result_{name}", bufs=3)[:]
+                result = ring.tile([P, C], F32, name="result", tag=f"result_{name}", bufs=4)[:]
             if engine is nc.vector:
                 nc.vector.tensor_copy(result[:, part], dx[:, part])
             else:
@@ -260,6 +262,11 @@ def tile_moe_bdx_mlp_silu_kernel(
                 waiting = (m, result)
             scatter(engine, e, *waiting)
 
+        def in_turns(e, results):
+            for half in (FIRST_HALF, SECOND_HALF):
+                for m, result in results.items():
+                    scatter(nc.scalar, e, m, result, half)
+
         def held_back(e, m, da_operand, part):
             scatter(nc.vector, e, m, emptied(nc.vector, e, m, da_operand, part, bank_of_dh=True), part)
 
@@ -267,11 +274,12 @@ def tile_moe_bdx_mlp_silu_kernel(
         for j, half in enumerate(halves):
             sigmoid(sigmoids[0][:, half], pre_first[j][:])
         for t in range(PACK - 1):
-            gather(nc.vector, t, 0, 2)
-            gather(nc.scalar, t, 2, 2)
-        gather(nc.vector, PACK - 1, 0, 1)
-        gather(nc.scalar, PACK - 1, 1, 1)
-        gather(nc.scalar, PACK - 1, 2, 2)
+            gather(nc.vector, t, 0, slice(0, 2 * C))
+            gather(nc.scalar, t, 2, slice(0, 2 * C))
+        for half in (FIRST_HALF, SECOND_HALF):
+            gather(nc.vector, PACK - 1, 0, half)
+        gather(nc.scalar, PACK - 1, 1, ALL_SLOTS)
+        gather(nc.scalar, PACK - 1, 2, slice(0, 2 * C))
         for e in (1, 2, 3):
             sigmoid(sigmoids[e][:], pre[e])
         silu(slice(0, 4 * C + LAP))
@@ -280,17 +288,16 @@ def tile_moe_bdx_mlp_silu_kernel(
 
         work = head.tile([P, 4 * C], F32, name="work", offset=0, align_bytes=64)
         lower, upper = halves
-        one_minus(work[:, lower], sigmoids[0][:, lower])
+        minus_one(work[:, lower], sigmoids[0][:, lower])
         nc.gpsimd.tensor_tensor(work[:, lower], work[:, lower], pre_first[0][:], ALU.mult)
-        nc.gpsimd.tensor_scalar(work[:, lower], work[:, lower], 1.0, 1.0, ALU.mult, ALU.add)
+        minus_one(work[:, lower], work[:, lower])
         nc.gpsimd.tensor_tensor(slope_flat[:, lower], work[:, lower], sigmoids[0][:, lower], ALU.mult)
-        one_minus(work[:, upper], sigmoids[0][:, upper])
+        minus_one(work[:, upper], sigmoids[0][:, upper])
         nc.gpsimd.tensor_tensor(slope_flat[:, upper], work[:, upper], pre_first[1][:], ALU.mult)
 
-        gate_on_vector(g_first, ungated[0], gate_banks[0])
-        nc.vector.scalar_tensor_tensor(
-            slope_flat[:, upper], slope_flat[:, upper], 1.0, sigmoids[0][:, upper], ALU.add, ALU.mult
-        )
+        for j, half in enumerate((FIRST_HALF, SECOND_HALF)):
+            gate_on_vector(g_first[:, j * C : (j + 1) * C], ungated[0][:, :, half], gate_banks[0][:, half])
+        less_one_times(slope_flat[:, upper], slope_flat[:, upper], sigmoids[0][:, upper])
         permuted = head.tile([P, 5 * H], U8, name="permuted", offset=0, align_bytes=64)
         words = permuted[:, 0 : 4 * H].rearrange("p (e n) -> p e n", e=2)
         packed = permuted[:, 4 * H : 5 * H]
@@ -314,69 +321,91 @@ def tile_moe_bdx_mlp_silu_kernel(
         [da_operand] = quantize(da_part, "one")
         [g_operand] = quantize(g_part, "second")
 
-        def behind_quantisation(e, m, operand, part):
-            scatter(nc.vector, e, m, emptied(nc.vector, e, m, operand, part, into=da_part[:, 0:C]), part)
+        def beside_quantisation(e, m, operand, part, into):
+            scatter(nc.vector, e, m, emptied(nc.vector, e, m, operand, part, into=into), part)
 
         def half_result(engine, e, m, operand, part):
             scatter(engine, e, m, emptied(engine, e, m, operand, part), part)
 
-        def make_slope(e):
-            one_minus(rest, pre[e])
-            nc.gpsimd.tensor_tensor(slope, planes(sigmoids[e][:]), planes(rest), ALU.mult)
+        def times_dh(e, operand, part=ALL_SLOTS):
+            width = part.stop - part.start
+            group = C // width
+            for first in range(0, PACK, group):
+                bank = psum_h.tile([P, C], F32, name="dh")
+                for t in range(group):
+                    product(bank[:, t * width : (t + 1) * width], w2[e], w2_s[e], first + t, operand, part)
+                values = planes(pre[e])[:, first : first + group, part]
+                less_one_times(values, values, bank[:].rearrange("p (t c) -> p t c", t=group))
 
-        half_result(nc.vector, 0, 3, da_operand, FIRST_HALF)
-        project(nc.vector, 0, (0, 1), da_operand, in_banks_of_dh=(0, 1))
-        half_result(nc.scalar, 0, 2, da_operand, FIRST_HALF)
-        project(nc.scalar, 0, (4, 5), da_operand)
-        half_result(nc.scalar, 0, 3, da_operand, SECOND_HALF)
-        banks = hidden_gradient(1, g_operand)
-        gate_on_gpsimd(g_part[:, C : 2 * C], ungated[2][:, :, SECOND_HALF], gates[2][:, SECOND_HALF])
-        make_slope(1)
-        gate_on_gpsimd(g_part[:, 0:C], ungated[2][:, :, FIRST_HALF], gates[2][:, FIRST_HALF])
-        through_silu(banks, slope, da_part)
+        def times_sigmoid(e, part=ALL_SLOTS):
+            nc.gpsimd.tensor_tensor(
+                da_part.bitcast(BF16).rearrange("p (c t) -> p c t", t=PACK)[:, part, :],
+                by_slot(planes(pre[e])[:, :, part]),
+                by_slot(planes(sigmoids[e][:])[:, :, part]),
+                ALU.mult,
+            )
+
+        project(nc.vector, 0, (0,), da_operand, in_banks_of_dh=(0,))
+        results = {m: emptied(nc.scalar, 0, m, da_operand) for m in (4, 5)}
+        times_dh(1, g_operand)
+        project(nc.vector, 0, (1,), da_operand, in_banks_of_dh=(1,))
+        scatter(nc.vector, 0, 2, emptied(nc.vector, 0, 2, da_operand, FIRST_HALF, bank_of_dh=True), FIRST_HALF)
+        results[3] = emptied(nc.vector, 0, 3, da_operand, bank_of_dh=True)
+        in_turns(0, results)
+        gate_on_gpsimd(g_part, ungated[2], gates[2][:])
+        times_sigmoid(1)
         da_before = da_operand
         g_operand, da_operand = quantize(both_parts, "both", operands=2)
-        behind_quantisation(0, 2, da_before, SECOND_HALF)
+        beside_quantisation(0, 2, da_before, SECOND_HALF, sigmoids[1][:, 0:C])
 
-        half_result(nc.scalar, 1, 2, da_operand, FIRST_HALF)
-        project(nc.vector, 1, (0, 1), da_operand)
-        project(nc.scalar, 1, (4, 5, 3), da_operand)
-        banks = hidden_gradient(2, g_operand)
-        make_slope(2)
+        times_dh(2, g_operand)
+        results = {m: emptied(nc.scalar, 1, m, da_operand) for m in (4, 5)}
+        result_0, result_1 = [emptied(nc.vector, 1, m, da_operand) for m in (0, 1)]
+        scatter(nc.vector, 1, 0, result_0)
+        scatter(nc.vector, 1, 1, result_1)
+        results[3] = emptied(nc.scalar, 1, 3, da_operand)
+        in_turns(1, results)
+        left_of_2 = floats("left_of_2", 3 * C)
+        emptied(nc.scalar, 1, 2, da_operand, SECOND_HALF, into=left_of_2[:, 0:C])
         gate_on_gpsimd(g_part, ungated[3], gates[3][:])
-        through_silu(banks, slope, da_part)
+        times_sigmoid(2)
         da_before = da_operand
         g_operand, da_operand = quantize(both_parts, "both", operands=2)
-        behind_quantisation(1, 2, da_before, SECOND_HALF)
+        beside_quantisation(1, 2, da_before, FIRST_HALF, sigmoids[2][:, 0:C])
 
-        result_4 = emptied(nc.scalar, 2, 4, da_operand)
+        times_dh(3, g_operand, FIRST_HALF)
+        times_sigmoid(3, FIRST_HALF)
+        results = {m: emptied(nc.scalar, 2, m, da_operand) for m in (4, 5)}
+        times_dh(3, g_operand, SECOND_HALF)
+        times_sigmoid(3, SECOND_HALF)
         project(nc.vector, 2, (0,), da_operand)
         half_result(nc.vector, 2, 1, da_operand, FIRST_HALF)
-        banks = hidden_gradient(3, g_operand)
-        scatter(nc.scalar, 2, 4, result_4)
-        project(nc.scalar, 2, (5, 3), da_operand)
-        left_of_2 = floats("left_of_2", 2 * C)
-        emptied(nc.scalar, 2, 2, da_operand, into=left_of_2[:, 0:C])
-        make_slope(3)
-        through_silu(banks, slope, da_part)
+        in_turns(2, results)
+        left_of_3 = floats("left_of_3", 2 * C, tag="sigmoid0")
+        emptied(nc.scalar, 2, 3, da_operand, into=left_of_3[:, 0:C])
+        emptied(nc.scalar, 2, 2, da_operand, into=left_of_2[:, C : 2 * C])
+        scatter(nc.scalar, 2, 3, left_of_3[:, 0:C], FIRST_HALF)
         da_before = da_operand
         [da_operand] = quantize(da_part, "one")
-        behind_quantisation(2, 1, da_before, SECOND_HALF)
+        beside_quantisation(2, 1, da_before, SECOND_HALF, sigmoids[3][:, 0:C])
 
-        result_4 = emptied(nc.scalar, 3, 4, da_operand)
         result_0, result_1 = [emptied(nc.vector, 3, m, da_operand) for m in (0, 1)]
         scatter(nc.vector, 3, 0, result_0)
         store(nc.vector, 0)
-        emptied(nc.vector, 3, 2, da_operand, into=left_of_2[:, C : 2 * C])
+        emptied(nc.vector, 3, 2, da_operand, into=left_of_2[:, 2 * C : 3 * C], bank_of_dh=True)
         scatter(nc.vector, 3, 1, result_1)
         store(nc.vector, 1)
-        scatter(nc.vector, 2, 2, left_of_2[:], slice(0, 2 * C))
+        scatter(nc.vector, 1, 2, left_of_2[:], slice(C // 2, 3 * C))
         store(nc.vector, 2)
-        result_5 = emptied(nc.scalar, 3, 5, da_operand)
-        scatter(nc.scalar, 3, 4, result_4)
+        results = {4: emptied(nc.scalar, 3, 4, da_operand, into=left_of_3[:, C : 2 * C])}
+        results[5] = emptied(nc.scalar, 3, 5, da_operand)
+        scatter(nc.scalar, 3, 4, results[4], FIRST_HALF)
+        scatter(nc.scalar, 3, 5, results[5], FIRST_HALF)
+        scatter(nc.scalar, 3, 4, results[4], SECOND_HALF)
         store(nc.scalar, 4)
-        result_3 = emptied(nc.scalar, 3, 3, da_operand)
-        scatter(nc.scalar, 3, 5, result_5)
+        emptied(nc.scalar, 3, 3, da_operand, into=left_of_3[:, C : 2 * C])
+        scatter(nc.scalar, 3, 5, results[5], SECOND_HALF)
         store(nc.scalar, 5)
-        scatter(nc.scalar, 3, 3, result_3)
+        for piece in (slice(C // 2, 5 * C // 4), slice(5 * C // 4, 2 * C)):
+            scatter(nc.scalar, 2, 3, left_of_3[:], piece)
         store(nc.scalar, 3)

@@ -152,9 +152,6 @@ def tile_moe_bdx_mlp_silu_kernel(
             else:
                 nc.scalar.activation(target, window, ACT.Copy)
 
-        def by_slot(source):
-            return source.rearrange("p t c -> p c t")
-
         def gate_on_vector(target, source, bank):
             width = bank.shape[1]
             nc.vector.tensor_tensor(
@@ -165,10 +162,11 @@ def tile_moe_bdx_mlp_silu_kernel(
             )
 
         def gate_on_gpsimd(target, source, row):
+            width = row.shape[1]
             nc.gpsimd.tensor_tensor(
-                target.bitcast(BF16).rearrange("p (c t) -> p c t", t=PACK),
-                by_slot(source),
-                row.unsqueeze(2).to_broadcast([P, row.shape[1], PACK]),
+                target.bitcast(BF16).rearrange("p (c i t) -> p c t i", i=RUN, t=PACK),
+                source.rearrange("p t (c i) -> p c t i", i=RUN),
+                row.rearrange("p (c i) -> p c i", i=RUN).unsqueeze(2).to_broadcast([P, width // RUN, PACK, RUN]),
                 ALU.mult,
             )
 
@@ -339,9 +337,9 @@ def tile_moe_bdx_mlp_silu_kernel(
 
         def times_sigmoid(e, part=ALL_SLOTS):
             nc.gpsimd.tensor_tensor(
-                da_part.bitcast(BF16).rearrange("p (c t) -> p c t", t=PACK)[:, part, :],
-                by_slot(planes(pre[e])[:, :, part]),
-                by_slot(planes(sigmoids[e][:])[:, :, part]),
+                da_part[:, 2 * part.start : 2 * part.stop].bitcast(BF16).rearrange("p (c i t) -> p c t i", i=RUN, t=PACK),
+                planes(pre[e])[:, :, part].rearrange("p t (c i) -> p c t i", i=RUN),
+                planes(sigmoids[e][:])[:, :, part].rearrange("p t (c i) -> p c t i", i=RUN),
                 ALU.mult,
             )
 

@@ -10,7 +10,7 @@ LAST = E - 1
 LIST_ROWS = 16
 QUADRANTS, QUADRANT_ROWS, SCALE_ROWS = 4, 32, 4
 RUN = 4
-PAIR = 2
+PAIR = 4
 LAP = 32
 LOWER, UPPER = slice(0, 2), slice(2, 4)
 ALL_SLOTS = slice(0, C)

@@ -39,8 +39,10 @@ def tile_moe_bdx_mlp_silu_kernel(
         keep = ctx.enter_context(tc.tile_pool(name="keep", bufs=1))
         head = ctx.enter_context(tc.tile_pool(name="head", bufs=1))
         ring = ctx.enter_context(tc.tile_pool(name="ring", bufs=2))
-        psum_h = ctx.enter_context(tc.psum_pool(name="psum_h", bufs=4))
-        psum_x = ctx.enter_context(tc.psum_pool(name="psum_x", bufs=2))
+        psum = ctx.enter_context(tc.psum_pool(name="psum", bufs=1))
+
+        def bank_tile(bank):
+            return psum.tile([P, C], F32, name="bank", tag=bank)
 
         def floats(name, width, tag=""):
             return keep.tile([P, width], F32, name=name, tag=tag, align_bytes=64)
@@ -93,12 +95,12 @@ def tile_moe_bdx_mlp_silu_kernel(
         nc.sync.dma_start(out=offsets[:], in_=offs)
         nc.sync.dma_start(out=gate_rows[0:blocks, :], in_=gate[0, :].rearrange("(b c) -> b c", c=P))
         make_identity(nc, identity[:])
-        turned = psum_h.tile([P, C], F32, name="dh")
+        turned = bank_tile("v0")
         nc.tensor.transpose(turned[:, 0:P], gate_rows[:], identity[:])
         nc.vector.tensor_scalar(gate_columns[:], turned[:, 0:blocks], -1.0, None, ALU.mult)
 
         def spread(e):
-            bank = psum_x.tile([P, C], F32, name="spread", tag=("dx_vector", "dx_scalar")[e % 2])
+            bank = bank_tile(("s2", "s0", "s0", "s1")[e])
             for j in range(C // P):
                 b = e * C // P + j
                 column = gate_columns[:, b : b + 1].to_broadcast([P, P])
@@ -170,13 +172,17 @@ def tile_moe_bdx_mlp_silu_kernel(
                 ALU.mult,
             )
 
-        def quantize(grouped, kind, operands=1, offset=None):
+        def quantize(grouped, kind, operands=1, offset=None, calls=1):
             if offset is None:
                 codes = ring.tile([P, operands * C], U32, name=f"codes_{kind}", align_bytes=64)
             else:
                 codes = head.tile([P, operands * C], U32, name=f"codes_{kind}", offset=offset, align_bytes=64)
             scales = ring.tile([P, operands * C], U8, name=f"scales_{kind}", align_bytes=64)
-            nc.vector.quantize_mx(out=codes[:].bitcast(FP8X4), scales=scales[:], in_=grouped.bitcast(BF16))
+            width = operands * C // calls
+            for j in range(calls):
+                part = slice(j * width, (j + 1) * width)
+                values = grouped.bitcast(BF16)[:, PACK * part.start : PACK * part.stop]
+                nc.vector.quantize_mx(out=codes[:, part].bitcast(FP8X4), scales=scales[:, part], in_=values)
             return [(codes[:, j * C : (j + 1) * C], scales[:, j * C : (j + 1) * C]) for j in range(operands)]
 
         def product(target, weight_words, weight_scales, tile, operand, part):
@@ -193,7 +199,7 @@ def tile_moe_bdx_mlp_silu_kernel(
         def hidden_gradient(e, g_operand):
             banks = []
             for j in range(C // P):
-                bank = psum_h.tile([P, C], F32, name="dh")
+                bank = bank_tile(f"v{j + 1}")
                 for t in range(PACK):
                     product(bank[:, t * P : (t + 1) * P], w2[e], w2_s[e], t, g_operand, slice(j * P, (j + 1) * P))
                 banks.append(bank)
@@ -220,12 +226,9 @@ def tile_moe_bdx_mlp_silu_kernel(
         def less_one_times(target, first, second):
             nc.vector.scalar_tensor_tensor(target, first, 1.0, second, ALU.subtract, ALU.mult)
 
-        def emptied(engine, e, m, da_operand, part=ALL_SLOTS, into=None, bank_of_dh=False):
+        def emptied(engine, e, m, da_operand, bank, part=ALL_SLOTS, into=None):
             name = "vector" if engine is nc.vector else "scalar"
-            if bank_of_dh:
-                dx = psum_h.tile([P, C], F32, name="dh")
-            else:
-                dx = psum_x.tile([P, C], F32, name="dx", tag=f"dx_{name}")
+            dx = bank_tile(bank)
             product(dx[:, part], w1[:, e, :], w1_s[:, e, :], m, da_operand, part)
             result = into
             if into is None:
@@ -247,26 +250,13 @@ def tile_moe_bdx_mlp_silu_kernel(
                 for piece in (FIRST_HALF, SECOND_HALF) if part == ALL_SLOTS else (part,):
                     nc.scalar.activation(window[m][:].indirect(slots(e, piece)), result[:, piece], ACT.Copy)
 
-        def store(engine, m):
-            queue = nc.sync if engine is nc.vector else nc.scalar
+        def store(queue, m):
             queue.dma_start(out=out[m * P : (m + 1) * P, :], in_=window[m][:])
-
-        def project(engine, e, tiles, da_operand, in_banks_of_dh=()):
-            waiting = None
-            for m in tiles:
-                result = emptied(engine, e, m, da_operand, bank_of_dh=m in in_banks_of_dh)
-                if waiting is not None:
-                    scatter(engine, e, *waiting)
-                waiting = (m, result)
-            scatter(engine, e, *waiting)
 
         def in_turns(e, results):
             for half in (FIRST_HALF, SECOND_HALF):
                 for m, result in results.items():
                     scatter(nc.scalar, e, m, result, half)
-
-        def held_back(e, m, da_operand, part):
-            scatter(nc.vector, e, m, emptied(nc.vector, e, m, da_operand, part, bank_of_dh=True), part)
 
         halves = (slice(0, 2 * C), slice(2 * C, 4 * C))
         for j, half in enumerate(halves):
@@ -315,21 +305,15 @@ def tile_moe_bdx_mlp_silu_kernel(
         gate_on_gpsimd(g_part[:, C : 2 * C], ungated[1][:, :, SECOND_HALF], gates_second[:])
         through_silu(hidden_gradient(0, g_operand), slope, da_part)
         gate_on_vector(g_part[:, 0:C], ungated[1][:, :, FIRST_HALF], gate_banks[1][:, FIRST_HALF])
+        [da_operand] = quantize(da_part, "one", calls=2)
         permute(nc.vector.tensor_copy, words_late[:].bitcast(U16), w2_raw[:, 2:E, :].bitcast(U16))
-        [da_operand] = quantize(da_part, "one")
         [g_operand] = quantize(g_part, "second")
 
-        def beside_quantisation(e, m, operand, part, into):
-            scatter(nc.vector, e, m, emptied(nc.vector, e, m, operand, part, into=into), part)
-
-        def half_result(engine, e, m, operand, part):
-            scatter(engine, e, m, emptied(engine, e, m, operand, part), part)
-
-        def times_dh(e, operand, part=ALL_SLOTS):
+        def times_dh(e, operand, banks, part=ALL_SLOTS):
             width = part.stop - part.start
             group = C // width
-            for first in range(0, PACK, group):
-                bank = psum_h.tile([P, C], F32, name="dh")
+            for first, name in zip(range(0, PACK, group), banks):
+                bank = bank_tile(name)
                 for t in range(group):
                     product(bank[:, t * width : (t + 1) * width], w2[e], w2_s[e], first + t, operand, part)
                 values = planes(pre[e])[:, first : first + group, part]
@@ -343,67 +327,73 @@ def tile_moe_bdx_mlp_silu_kernel(
                 ALU.mult,
             )
 
-        project(nc.vector, 0, (0,), da_operand, in_banks_of_dh=(0,))
-        results = {m: emptied(nc.scalar, 0, m, da_operand) for m in (4, 5)}
-        times_dh(1, g_operand)
-        project(nc.vector, 0, (1,), da_operand, in_banks_of_dh=(1,))
-        scatter(nc.vector, 0, 2, emptied(nc.vector, 0, 2, da_operand, FIRST_HALF, bank_of_dh=True), FIRST_HALF)
-        results[3] = emptied(nc.vector, 0, 3, da_operand, bank_of_dh=True)
-        in_turns(0, results)
-        gate_on_gpsimd(g_part, ungated[2], gates[2][:])
-        times_sigmoid(1)
-        da_before = da_operand
-        g_operand, da_operand = quantize(both_parts, "both", operands=2)
-        beside_quantisation(0, 2, da_before, SECOND_HALF, sigmoids[1][:, 0:C])
+        V, S = nc.vector, nc.scalar
 
-        times_dh(2, g_operand)
-        results = {m: emptied(nc.scalar, 1, m, da_operand) for m in (4, 5)}
-        result_0, result_1 = [emptied(nc.vector, 1, m, da_operand) for m in (0, 1)]
-        scatter(nc.vector, 1, 0, result_0)
-        scatter(nc.vector, 1, 1, result_1)
-        results[3] = emptied(nc.scalar, 1, 3, da_operand)
+        result_0 = emptied(V, 0, 0, da_operand, "v0")
+        result_3 = emptied(V, 0, 3, da_operand, "v1", into=floats("first_of_3", C)[:])
+        scatter(V, 0, 0, result_0)
+        results = {m: emptied(S, 0, m, da_operand, bank) for m, bank in ((4, "s1"), (5, "s2"))}
+        results[3] = result_3
+        gate_on_gpsimd(g_part, ungated[2], gates[2][:])
+        for half, banks in ((FIRST_HALF, ("v2", "v3")), (SECOND_HALF, ("v4", "v0"))):
+            times_dh(1, g_operand, banks, half)
+            times_sigmoid(1, half)
+        result_1 = emptied(V, 0, 1, da_operand, "v2")
+        result_2 = emptied(V, 0, 2, da_operand, "v3", FIRST_HALF)
+        scatter(V, 0, 1, result_1)
+        scatter(V, 0, 2, result_2, FIRST_HALF)
+        in_turns(0, results)
+        held = emptied(V, 0, 2, da_operand, "v4", SECOND_HALF, into=sigmoids[1][:, 0:C])
+        g_operand, da_operand = quantize(both_parts, "both", operands=2)
+        scatter(V, 0, 2, held, SECOND_HALF)
+
+        times_dh(2, g_operand, ("v0", "v1", "v2", "v3"))
+        result_0, result_1 = [emptied(V, 1, m, da_operand, bank) for m, bank in ((0, "v4"), (1, "v0"))]
+        results = {m: emptied(S, 1, m, da_operand, bank) for m, bank in ((4, "s0"), (5, "s1"), (3, "s2"))}
+        scatter(V, 1, 0, result_0)
+        scatter(V, 1, 1, result_1)
         in_turns(1, results)
-        left_of_2 = floats("left_of_2", 3 * C)
-        emptied(nc.scalar, 1, 2, da_operand, SECOND_HALF, into=left_of_2[:, 0:C])
         gate_on_gpsimd(g_part, ungated[3], gates[3][:])
         times_sigmoid(2)
-        da_before = da_operand
+        left_of_2 = sigmoids[2][:, 0 : 3 * C]
+        emptied(V, 1, 2, da_operand, "v1", into=left_of_2[:, 0:C])
         g_operand, da_operand = quantize(both_parts, "both", operands=2)
-        beside_quantisation(1, 2, da_before, FIRST_HALF, sigmoids[2][:, 0:C])
+        scatter(V, 1, 2, left_of_2, FIRST_HALF)
 
-        times_dh(3, g_operand, FIRST_HALF)
+        times_dh(3, g_operand, ("v2", "v3"), FIRST_HALF)
         times_sigmoid(3, FIRST_HALF)
-        results = {m: emptied(nc.scalar, 2, m, da_operand) for m in (4, 5)}
-        times_dh(3, g_operand, SECOND_HALF)
+        times_dh(3, g_operand, ("v4", "v0"), SECOND_HALF)
         times_sigmoid(3, SECOND_HALF)
-        project(nc.vector, 2, (0,), da_operand)
-        half_result(nc.vector, 2, 1, da_operand, FIRST_HALF)
-        in_turns(2, results)
+        results = {m: emptied(S, 2, m, da_operand, bank) for m, bank in ((4, "s0"), (5, "s1"))}
+        result_0 = emptied(V, 2, 0, da_operand, "v1")
+        result_1 = emptied(V, 2, 1, da_operand, "v2", FIRST_HALF)
         left_of_3 = floats("left_of_3", 2 * C, tag="sigmoid0")
-        emptied(nc.scalar, 2, 3, da_operand, into=left_of_3[:, 0:C])
-        emptied(nc.scalar, 2, 2, da_operand, into=left_of_2[:, C : 2 * C])
-        scatter(nc.scalar, 2, 3, left_of_3[:, 0:C], FIRST_HALF)
-        da_before = da_operand
+        emptied(S, 2, 3, da_operand, "s2", into=left_of_3[:, 0:C])
+        emptied(S, 2, 2, da_operand, "v3", into=left_of_2[:, C : 2 * C])
+        scatter(V, 2, 0, result_0)
+        scatter(V, 2, 1, result_1, FIRST_HALF)
+        in_turns(2, results)
+        held = emptied(V, 2, 1, da_operand, "v4", SECOND_HALF, into=sigmoids[3][:, 0:C])
         [da_operand] = quantize(da_part, "one")
-        beside_quantisation(2, 1, da_before, SECOND_HALF, sigmoids[3][:, 0:C])
+        scatter(V, 2, 1, held, SECOND_HALF)
 
-        result_0, result_1 = [emptied(nc.vector, 3, m, da_operand) for m in (0, 1)]
-        scatter(nc.vector, 3, 0, result_0)
-        store(nc.vector, 0)
-        emptied(nc.vector, 3, 2, da_operand, into=left_of_2[:, 2 * C : 3 * C], bank_of_dh=True)
-        scatter(nc.vector, 3, 1, result_1)
-        store(nc.vector, 1)
-        scatter(nc.vector, 1, 2, left_of_2[:], slice(C // 2, 3 * C))
-        store(nc.vector, 2)
-        results = {4: emptied(nc.scalar, 3, 4, da_operand, into=left_of_3[:, C : 2 * C])}
-        results[5] = emptied(nc.scalar, 3, 5, da_operand)
-        scatter(nc.scalar, 3, 4, results[4], FIRST_HALF)
-        scatter(nc.scalar, 3, 5, results[5], FIRST_HALF)
-        scatter(nc.scalar, 3, 4, results[4], SECOND_HALF)
+        result_0, result_1 = [emptied(V, 3, m, da_operand, bank) for m, bank in ((0, "v0"), (1, "v1"))]
+        results = {m: emptied(S, 3, m, da_operand, bank) for m, bank in ((4, "s0"), (5, "s1"))}
+        emptied(S, 3, 3, da_operand, "s2", into=left_of_3[:, C : 2 * C])
+        emptied(V, 3, 2, da_operand, "v2", into=left_of_2[:, 2 * C : 3 * C])
+        scatter(V, 3, 0, result_0)
+        store(nc.sync, 0)
+        scatter(V, 3, 1, result_1)
+        store(nc.sync, 1)
+        scatter(V, 1, 2, left_of_2, slice(C // 2, 3 * C))
+        store(nc.sync, 2)
+        scatter(S, 2, 3, left_of_3[:], FIRST_HALF)
+        scatter(S, 3, 4, results[4], FIRST_HALF)
+        scatter(S, 3, 5, results[5], FIRST_HALF)
+        scatter(S, 3, 4, results[4], SECOND_HALF)
         store(nc.scalar, 4)
-        emptied(nc.scalar, 3, 3, da_operand, into=left_of_3[:, C : 2 * C])
-        scatter(nc.scalar, 3, 5, results[5], SECOND_HALF)
+        scatter(S, 3, 5, results[5], SECOND_HALF)
         store(nc.scalar, 5)
         for piece in (slice(C // 2, 5 * C // 4), slice(5 * C // 4, 2 * C)):
-            scatter(nc.scalar, 2, 3, left_of_3[:], piece)
+            scatter(S, 2, 3, left_of_3[:], piece)
         store(nc.scalar, 3)

@@ -39,6 +39,7 @@ def tile_moe_bdx_mlp_silu_kernel(
         keep = ctx.enter_context(tc.tile_pool(name="keep", bufs=1))
         head = ctx.enter_context(tc.tile_pool(name="head", bufs=1))
         ring = ctx.enter_context(tc.tile_pool(name="ring", bufs=2))
+        after = ctx.enter_context(tc.tile_pool(name="after", bufs=1))
         psum = ctx.enter_context(tc.psum_pool(name="psum", bufs=1))
 
         def bank_tile(bank):
@@ -55,15 +56,16 @@ def tile_moe_bdx_mlp_silu_kernel(
         pre_first = [floats(f"pre_first{j}", 2 * C, tag=f"pre_first{j}") for j in range(2)]
         pre_later = floats("pre_later", 12 * C)
         pre = {1: pre_later[:, 0 : 4 * C], 3: pre_later[:, 4 * C : 8 * C], 2: pre_later[:, 8 * C : 12 * C]}
-        sigmoids = [floats(f"sigmoid{e}", 4 * C, tag=f"sigmoid{e}") for e in range(E)]
+        sigmoids = {e: floats(f"sigmoid{e}", 4 * C, tag=f"sigmoid{e}") for e in (0, 1, 3)}
+        sigmoids[2] = after.tile([P, 4 * C], F32, name="sigmoid2", offset=0, align_bytes=64)
         w2_raw = keep.tile([P, E, 2 * H], U8, name="w2_raw", align_bytes=64)
-        w2_sraw = keep.tile([P, 1, H], U8, name="w2_sraw", align_bytes=64)
+        w2_sraw = keep.tile([P, 1, H], U8, name="w2_sraw", tag="scale_rows", align_bytes=64)
         w2_s_late = keep.tile([P, LAST, H], U8, name="w2_s_late", align_bytes=64)
         w1 = keep.tile([P, E, 2 * K], U8, name="w1", align_bytes=64)
         w1_s = keep.tile([P, E, K], U8, name="w1_s", align_bytes=64)
         shared = floats("shared", 8 * C)
         g_part, da_part, both_parts = shared[:, 0 : 2 * C], shared[:, 2 * C : 4 * C], shared[:, 0 : 4 * C]
-        g_first = shared[:, C - LAP : 3 * C - LAP]
+        g_first = shared[:, C : 3 * C]
         slope_flat = shared[:, 4 * C - LAP : 8 * C - LAP]
         slope = planes(slope_flat)
 
@@ -172,18 +174,20 @@ def tile_moe_bdx_mlp_silu_kernel(
                 ALU.mult,
             )
 
-        def quantize(grouped, kind, operands=1, offset=None, calls=1):
-            if offset is None:
+        def operand_tiles(kind, operands=1, codes=None):
+            if codes is None:
                 codes = ring.tile([P, operands * C], U32, name=f"codes_{kind}", align_bytes=64)
-            else:
-                codes = head.tile([P, operands * C], U32, name=f"codes_{kind}", offset=offset, align_bytes=64)
-            scales = ring.tile([P, operands * C], U8, name=f"scales_{kind}", align_bytes=64)
-            width = operands * C // calls
-            for j in range(calls):
-                part = slice(j * width, (j + 1) * width)
-                values = grouped.bitcast(BF16)[:, PACK * part.start : PACK * part.stop]
-                nc.vector.quantize_mx(out=codes[:, part].bitcast(FP8X4), scales=scales[:, part], in_=values)
-            return [(codes[:, j * C : (j + 1) * C], scales[:, j * C : (j + 1) * C]) for j in range(operands)]
+            return codes, ring.tile([P, operands * C], U8, name=f"scales_{kind}", align_bytes=64)
+
+        def quantize(grouped, operand, part=slice(None)):
+            codes, scales = operand
+            values = grouped.bitcast(BF16).rearrange("p (c t) -> p c t", t=PACK)[:, part, :].rearrange("p c t -> p (c t)")
+            nc.vector.quantize_mx(out=codes[:, part].bitcast(FP8X4), scales=scales[:, part], in_=values)
+
+        def quantize_both():
+            codes, scales = operand_tiles("both", operands=2)
+            quantize(both_parts, (codes, scales))
+            return [(codes[:, j * C : (j + 1) * C], scales[:, j * C : (j + 1) * C]) for j in range(2)]
 
         def product(target, weight_words, weight_scales, tile, operand, part):
             nc.tensor.matmul_mx(
@@ -291,7 +295,8 @@ def tile_moe_bdx_mlp_silu_kernel(
         packed = permuted[:, 4 * H : 5 * H]
         permute(nc.vector.tensor_copy, packed.rearrange("p (e n) -> p e n", e=1), w2_sraw[:])
         permute(nc.vector.tensor_copy, words.bitcast(U16), w2_raw[:, 0:2, :].bitcast(U16))
-        [g_operand] = quantize(g_first, "first", offset=8 * C)
+        g_operand = operand_tiles("first", codes=head.tile([P, C], U32, name="codes_first", offset=8 * C, align_bytes=64))
+        quantize(g_first, g_operand)
         words_late = keep.tile([P, 2, 2 * H], U8, name="words_late", tag="gates_second", align_bytes=64)
         w2 = [words[:, 0, :], words[:, 1, :], words_late[:, 0, :], words_late[:, 1, :]]
         w2_s = [packed] + [w2_s_late[:, e - 1, :] for e in range(1, E)]
@@ -304,10 +309,15 @@ def tile_moe_bdx_mlp_silu_kernel(
                 )
         gate_on_gpsimd(g_part[:, C : 2 * C], ungated[1][:, :, SECOND_HALF], gates_second[:])
         through_silu(hidden_gradient(0, g_operand), slope, da_part)
-        gate_on_vector(g_part[:, 0:C], ungated[1][:, :, FIRST_HALF], gate_banks[1][:, FIRST_HALF])
-        [da_operand] = quantize(da_part, "one", calls=2)
+        g_second = floats("g_second", C, tag="scale_rows")[:]
+        gate_on_vector(g_second, ungated[1][:, :, FIRST_HALF], gate_banks[1][:, FIRST_HALF])
+        da_operand = operand_tiles("one")
+        for half in (FIRST_HALF, SECOND_HALF):
+            quantize(da_part, da_operand, half)
         permute(nc.vector.tensor_copy, words_late[:].bitcast(U16), w2_raw[:, 2:E, :].bitcast(U16))
-        [g_operand] = quantize(g_part, "second")
+        g_operand = operand_tiles("second", codes=keep.tile([P, C], U32, name="codes_second", tag="gathered0", align_bytes=64))
+        quantize(g_second, g_operand, FIRST_HALF)
+        quantize(g_part, g_operand, SECOND_HALF)
 
         def times_dh(e, operand, banks, part=ALL_SLOTS):
             width = part.stop - part.start
@@ -344,7 +354,7 @@ def tile_moe_bdx_mlp_silu_kernel(
         scatter(V, 0, 2, result_2, FIRST_HALF)
         in_turns(0, results)
         held = emptied(V, 0, 2, da_operand, "v4", SECOND_HALF, into=sigmoids[1][:, 0:C])
-        g_operand, da_operand = quantize(both_parts, "both", operands=2)
+        g_operand, da_operand = quantize_both()
         scatter(V, 0, 2, held, SECOND_HALF)
 
         times_dh(2, g_operand, ("v0", "v1", "v2", "v3"))
@@ -353,34 +363,45 @@ def tile_moe_bdx_mlp_silu_kernel(
         scatter(V, 1, 0, result_0)
         scatter(V, 1, 1, result_1)
         in_turns(1, results)
-        gate_on_gpsimd(g_part, ungated[3], gates[3][:])
+        g_last = shared[:, LAP : 2 * C + LAP]
+        early, late = slice(0, 3 * C // 4), slice(3 * C // 4, C)
+        gate_on_gpsimd(g_last[:, 0 : 3 * C // 2], ungated[3][:, :, early], gates[3][:, early])
         times_sigmoid(2)
-        left_of_2 = sigmoids[2][:, 0 : 3 * C]
-        emptied(V, 1, 2, da_operand, "v1", into=left_of_2[:, 0:C])
-        g_operand, da_operand = quantize(both_parts, "both", operands=2)
+        left_of_2 = after.tile([P, 3 * C], F32, name="left_of_2", offset=0, align_bytes=64)[:]
+        emptied(V, 1, 2, da_operand, "v1", FIRST_HALF, into=left_of_2[:, 0:C])
+        da_before = da_operand
+        g_operand = operand_tiles("last", codes=after.tile([P, C], U32, name="codes_last", offset=12 * C, align_bytes=64))
+        quantize(g_last, g_operand, FIRST_HALF)
+        da_operand = operand_tiles("one")
+        quantize(da_part, da_operand)
         scatter(V, 1, 2, left_of_2, FIRST_HALF)
 
+        gate_on_gpsimd(g_last[:, 3 * C // 2 : 2 * C], ungated[3][:, :, late], gates[3][:, late])
         times_dh(3, g_operand, ("v2", "v3"), FIRST_HALF)
+        result_1 = emptied(V, 2, 1, da_operand, "v0", FIRST_HALF)
+        quantize(g_last, g_operand, SECOND_HALF)
         times_sigmoid(3, FIRST_HALF)
-        times_dh(3, g_operand, ("v4", "v0"), SECOND_HALF)
-        times_sigmoid(3, SECOND_HALF)
         results = {m: emptied(S, 2, m, da_operand, bank) for m, bank in ((4, "s0"), (5, "s1"))}
-        result_0 = emptied(V, 2, 0, da_operand, "v1")
-        result_1 = emptied(V, 2, 1, da_operand, "v2", FIRST_HALF)
+        times_dh(3, g_operand, ("v2", "v3"), SECOND_HALF)
+        times_sigmoid(3, SECOND_HALF)
+        behind_codes = after.tile([P, C], F32, name="behind_codes", offset=12 * C, align_bytes=64)
+        result_0 = emptied(V, 2, 0, da_operand, "v1", into=behind_codes[:])
+        emptied(V, 1, 2, da_before, "v2", SECOND_HALF, into=left_of_2[:, 0:C])
         left_of_3 = floats("left_of_3", 2 * C, tag="sigmoid0")
         emptied(S, 2, 3, da_operand, "s2", into=left_of_3[:, 0:C])
-        emptied(S, 2, 2, da_operand, "v3", into=left_of_2[:, C : 2 * C])
+        emptied(S, 2, 2, da_operand, "s0", into=left_of_2[:, C : 2 * C])
         scatter(V, 2, 0, result_0)
         scatter(V, 2, 1, result_1, FIRST_HALF)
         in_turns(2, results)
         held = emptied(V, 2, 1, da_operand, "v4", SECOND_HALF, into=sigmoids[3][:, 0:C])
-        [da_operand] = quantize(da_part, "one")
+        da_operand = operand_tiles("one")
+        quantize(da_part, da_operand)
         scatter(V, 2, 1, held, SECOND_HALF)
 
         result_0, result_1 = [emptied(V, 3, m, da_operand, bank) for m, bank in ((0, "v0"), (1, "v1"))]
         results = {m: emptied(S, 3, m, da_operand, bank) for m, bank in ((4, "s0"), (5, "s1"))}
         emptied(S, 3, 3, da_operand, "s2", into=left_of_3[:, C : 2 * C])
-        emptied(V, 3, 2, da_operand, "v2", into=left_of_2[:, 2 * C : 3 * C])
+        emptied(V, 3, 2, da_operand, "v3", into=left_of_2[:, 2 * C : 3 * C])
         scatter(V, 3, 0, result_0)
         store(nc.sync, 0)
         scatter(V, 3, 1, result_1)

@@ -94,7 +94,7 @@ def tile_moe_bdx_mlp_silu_kernel(
         identity = keep.tile([P, P], F32, name="identity")
         nc.gpsimd.memset(gate_rows[:], 0.0)
         nc.gpsimd.memset(w2_sraw[:].bitcast(I32), 0)
-        nc.sync.dma_start(out=offsets[:], in_=offs)
+        load_pre_first(0)
         nc.sync.dma_start(out=gate_rows[0:blocks, :], in_=gate[0, :].rearrange("(b c) -> b c", c=P))
         make_identity(nc, identity[:])
         turned = bank_tile("v0")
@@ -102,7 +102,7 @@ def tile_moe_bdx_mlp_silu_kernel(
         nc.vector.tensor_scalar(gate_columns[:], turned[:, 0:blocks], -1.0, None, ALU.mult)
 
         def spread(e):
-            bank = bank_tile(("s2", "s0", "s0", "s1")[e])
+            bank = bank_tile(("s2", "v0", "s0", "s1")[e])
             for j in range(C // P):
                 b = e * C // P + j
                 column = gate_columns[:, b : b + 1].to_broadcast([P, P])
@@ -119,7 +119,7 @@ def tile_moe_bdx_mlp_silu_kernel(
         gathered = [keep.tile([P, PACK, 2 * C], F32, name=f"gathered{j}", tag=f"gathered{j}", align_bytes=64) for j in range(2)]
         ungated = [gathered[e // 2][:, :, (e % 2) * C : (e % 2 + 1) * C] for e in range(E)]
 
-        load_pre_first(0)
+        nc.sync.dma_start(out=offsets[:], in_=offs)
         load_pre_first(1)
         for t in range(PACK):
             load_dy(t)
@@ -131,12 +131,12 @@ def tile_moe_bdx_mlp_silu_kernel(
             )
         for e in (1, 2, 3):
             load_pre(e)
-        for q in range(QUADRANTS):
-            nc.sync.dma_start(
-                out=w1_s[QUADRANT_ROWS * q : QUADRANT_ROWS * q + SCALE_ROWS].bitcast(I32),
-                in_=w1_scales[:, 0, SCALE_ROWS * q : SCALE_ROWS * (q + 1), :].rearrange("e f n -> f e n").bitcast(I32),
-            )
-        load_words(w1, w1_words)
+        w1_scale_rows = w1_scales.bitcast(I32).rearrange("e o (q r) n -> r q (e o) n", r=SCALE_ROWS)
+        w1_rows = w1_words.bitcast(I32).rearrange("e o p n -> p (e o) n")
+        for experts in (slice(0, 1), slice(1, E)):
+            for r in range(SCALE_ROWS):
+                nc.sync.dma_start(out=w1_s[r:P:QUADRANT_ROWS].bitcast(I32)[:, experts, :], in_=w1_scale_rows[r][:, experts, :])
+            nc.sync.dma_start(out=w1[:].bitcast(I32)[:, experts, :], in_=w1_rows[:, experts, :])
 
         def permute(copy, target, source):
             copy(
@@ -378,7 +378,8 @@ def tile_moe_bdx_mlp_silu_kernel(
 
         gate_on_gpsimd(g_last[:, 3 * C // 2 : 2 * C], ungated[3][:, :, late], gates[3][:, late])
         times_dh(3, g_operand, ("v2", "v3"), FIRST_HALF)
-        result_1 = emptied(V, 2, 1, da_operand, "v0", FIRST_HALF)
+        over_late = gathered[1][:].rearrange("p t c -> p (t c)")[:, 3 * C // 2 : 5 * C // 2]
+        result_1 = emptied(V, 2, 1, da_operand, "v0", FIRST_HALF, into=over_late)
         quantize(g_last, g_operand, SECOND_HALF)
         times_sigmoid(3, FIRST_HALF)
         results = {m: emptied(S, 2, m, da_operand, bank) for m, bank in ((4, "s0"), (5, "s1"))}
@@ -388,31 +389,33 @@ def tile_moe_bdx_mlp_silu_kernel(
         result_0 = emptied(V, 2, 0, da_operand, "v1", into=behind_codes[:])
         emptied(V, 1, 2, da_before, "v2", SECOND_HALF, into=left_of_2[:, 0:C])
         left_of_3 = floats("left_of_3", 2 * C, tag="sigmoid0")
-        emptied(S, 2, 3, da_operand, "s2", into=left_of_3[:, 0:C])
-        emptied(S, 2, 2, da_operand, "s0", into=left_of_2[:, C : 2 * C])
+        emptied(S, 2, 3, da_operand, "s2", SECOND_HALF, into=left_of_3[:, 0:C])
+        emptied(S, 2, 2, da_operand, "v3", into=left_of_2[:, C : 2 * C])
         scatter(V, 2, 0, result_0)
         scatter(V, 2, 1, result_1, FIRST_HALF)
         in_turns(2, results)
         held = emptied(V, 2, 1, da_operand, "v4", SECOND_HALF, into=sigmoids[3][:, 0:C])
+        da_before = da_operand
         da_operand = operand_tiles("one")
         quantize(da_part, da_operand)
         scatter(V, 2, 1, held, SECOND_HALF)
 
+        results = {m: emptied(S, 3, m, da_operand, bank) for m, bank in ((4, "s1"), (5, "s2"))}
         result_0, result_1 = [emptied(V, 3, m, da_operand, bank) for m, bank in ((0, "v0"), (1, "v1"))]
-        results = {m: emptied(S, 3, m, da_operand, bank) for m, bank in ((4, "s0"), (5, "s1"))}
-        emptied(S, 3, 3, da_operand, "s2", into=left_of_3[:, C : 2 * C])
-        emptied(V, 3, 2, da_operand, "v3", into=left_of_2[:, 2 * C : 3 * C])
+        scatter(S, 3, 4, results[4], FIRST_HALF)
+        emptied(S, 3, 3, da_operand, "s0", into=left_of_3[:, C : 2 * C])
+        scatter(S, 3, 4, results[4], SECOND_HALF)
+        store(nc.scalar, 4)
         scatter(V, 3, 0, result_0)
         store(nc.sync, 0)
+        emptied(V, 3, 2, da_operand, "v4", into=left_of_2[:, 2 * C : 3 * C])
         scatter(V, 3, 1, result_1)
         store(nc.sync, 1)
         scatter(V, 1, 2, left_of_2, slice(C // 2, 3 * C))
         store(nc.sync, 2)
-        scatter(S, 2, 3, left_of_3[:], FIRST_HALF)
-        scatter(S, 3, 4, results[4], FIRST_HALF)
+        emptied(S, 2, 3, da_before, "s1", FIRST_HALF, into=left_of_3[:, 0:C])
         scatter(S, 3, 5, results[5], FIRST_HALF)
-        scatter(S, 3, 4, results[4], SECOND_HALF)
-        store(nc.scalar, 4)
+        scatter(S, 2, 3, left_of_3[:], FIRST_HALF)
         scatter(S, 3, 5, results[5], SECOND_HALF)
         store(nc.scalar, 5)
         for piece in (slice(C // 2, 5 * C // 4), slice(5 * C // 4, 2 * C)):

@@ -54,10 +54,11 @@ def tile_moe_bdx_mlp_silu_kernel(
         offsets = keep.tile([P, E * C // LIST_ROWS], U16, name="offsets")
         dy = [floats(f"dy{t}", T, tag=f"columns{t}") for t in range(PACK)]
         pre_first = [floats(f"pre_first{j}", 2 * C, tag=f"pre_first{j}") for j in range(2)]
-        pre_later = floats("pre_later", 12 * C)
-        pre = {1: pre_later[:, 0 : 4 * C], 3: pre_later[:, 4 * C : 8 * C], 2: pre_later[:, 8 * C : 12 * C]}
-        sigmoids = {e: floats(f"sigmoid{e}", 4 * C, tag=f"sigmoid{e}") for e in (0, 1, 3)}
-        sigmoids[2] = after.tile([P, 4 * C], F32, name="sigmoid2", offset=0, align_bytes=64)
+        pre_later = planes(floats("pre_later", PACK * LAST * C)[:])
+        pre = {e: pre_later[:, :, (e - 1) * C : e * C] for e in range(1, E)}
+        sigmoid_first = floats("sigmoid_first", 4 * C, tag="sigmoid0")
+        sigmoid_later = planes(floats("sigmoid_later", PACK * LAST * C)[:])
+        sigmoids = {e: sigmoid_later[:, :, (e - 1) * C : e * C] for e in range(1, E)}
         w2_raw = keep.tile([P, E, 2 * H], U8, name="w2_raw", align_bytes=64)
         w2_sraw = keep.tile([P, 1, H], U8, name="w2_sraw", tag="scale_rows", align_bytes=64)
         w2_s_late = keep.tile([P, LAST, H], U8, name="w2_s_late", align_bytes=64)
@@ -81,8 +82,8 @@ def tile_moe_bdx_mlp_silu_kernel(
         def load_dy(t):
             nc.sync.dma_start(out=dy[t][:], in_=dy_rows[:, t, :])
 
-        def load_pre(e):
-            nc.sync.dma_start(out=planes(pre[e]), in_=a_rows[:, :, e * C : (e + 1) * C])
+        def load_pre_later(t):
+            nc.sync.dma_start(out=pre_later[:, t, :], in_=a_rows[:, t, C : E * C])
 
         def load_pre_first(j):
             target = pre_first[j][:].rearrange("p (t c) -> p t c", t=2)
@@ -129,8 +130,8 @@ def tile_moe_bdx_mlp_silu_kernel(
                 out=w2_sraw[QUADRANT_ROWS * q : QUADRANT_ROWS * q + E * SCALE_ROWS, 0, :].bitcast(I32),
                 in_=w2_scales[:, 0, SCALE_ROWS * q : SCALE_ROWS * (q + 1), :].bitcast(I32),
             )
-        for e in (1, 2, 3):
-            load_pre(e)
+        for t in range(PACK):
+            load_pre_later(t)
         w1_scale_rows = w1_scales.bitcast(I32).rearrange("e o (q r) n -> r q (e o) n", r=SCALE_ROWS)
         w1_rows = w1_words.bitcast(I32).rearrange("e o p n -> p (e o) n")
         for experts in (slice(0, 1), slice(1, E)):
@@ -221,8 +222,8 @@ def tile_moe_bdx_mlp_silu_kernel(
         def sigmoid(target, source):
             nc.scalar.activation(target, source, ACT.Sigmoid)
 
-        def silu(part):
-            nc.scalar.activation(pre_later[:, part], pre_later[:, part], ACT.Silu, scale=-1.0)
+        def silu(e):
+            nc.scalar.activation(pre[e], pre[e], ACT.Silu, scale=-1.0)
 
         def minus_one(target, source):
             nc.gpsimd.tensor_scalar(target, source, 1.0, -1.0, ALU.mult, ALU.add)
@@ -264,7 +265,7 @@ def tile_moe_bdx_mlp_silu_kernel(
 
         halves = (slice(0, 2 * C), slice(2 * C, 4 * C))
         for j, half in enumerate(halves):
-            sigmoid(sigmoids[0][:, half], pre_first[j][:])
+            sigmoid(sigmoid_first[:, half], pre_first[j][:])
         for t in range(PACK - 1):
             gather(nc.vector, t, 0, slice(0, 2 * C))
             gather(nc.scalar, t, 2, slice(0, 2 * C))
@@ -272,24 +273,23 @@ def tile_moe_bdx_mlp_silu_kernel(
             gather(nc.vector, PACK - 1, 0, half)
         gather(nc.scalar, PACK - 1, 1, ALL_SLOTS)
         gather(nc.scalar, PACK - 1, 2, slice(0, 2 * C))
-        for e in (1, 2, 3):
-            sigmoid(sigmoids[e][:], pre[e])
-        silu(slice(0, 4 * C + LAP))
-        silu(slice(8 * C - LAP, 12 * C))
-        silu(slice(4 * C + LAP, 8 * C - LAP))
+        for t in range(PACK):
+            sigmoid(sigmoid_later[:, t, :], pre_later[:, t, :])
+        for e in range(1, E):
+            silu(e)
 
         work = head.tile([P, 4 * C], F32, name="work", offset=0, align_bytes=64)
         lower, upper = halves
-        minus_one(work[:, lower], sigmoids[0][:, lower])
+        minus_one(work[:, lower], sigmoid_first[:, lower])
         nc.gpsimd.tensor_tensor(work[:, lower], work[:, lower], pre_first[0][:], ALU.mult)
         minus_one(work[:, lower], work[:, lower])
-        nc.gpsimd.tensor_tensor(slope_flat[:, lower], work[:, lower], sigmoids[0][:, lower], ALU.mult)
-        minus_one(work[:, upper], sigmoids[0][:, upper])
+        nc.gpsimd.tensor_tensor(slope_flat[:, lower], work[:, lower], sigmoid_first[:, lower], ALU.mult)
+        minus_one(work[:, upper], sigmoid_first[:, upper])
         nc.gpsimd.tensor_tensor(slope_flat[:, upper], work[:, upper], pre_first[1][:], ALU.mult)
 
         for j, half in enumerate((FIRST_HALF, SECOND_HALF)):
             gate_on_vector(g_first[:, j * C : (j + 1) * C], ungated[0][:, :, half], gate_banks[0][:, half])
-        less_one_times(slope_flat[:, upper], slope_flat[:, upper], sigmoids[0][:, upper])
+        less_one_times(slope_flat[:, upper], slope_flat[:, upper], sigmoid_first[:, upper])
         permuted = head.tile([P, 5 * H], U8, name="permuted", offset=0, align_bytes=64)
         words = permuted[:, 0 : 4 * H].rearrange("p (e n) -> p e n", e=2)
         packed = permuted[:, 4 * H : 5 * H]
@@ -319,21 +319,23 @@ def tile_moe_bdx_mlp_silu_kernel(
         quantize(g_second, g_operand, FIRST_HALF)
         quantize(g_part, g_operand, SECOND_HALF)
 
-        def times_dh(e, operand, banks, part=ALL_SLOTS):
+        def times_dh(e, operand, banks, part=ALL_SLOTS, into=None):
             width = part.stop - part.start
             group = C // width
             for first, name in zip(range(0, PACK, group), banks):
                 bank = bank_tile(name)
                 for t in range(group):
                     product(bank[:, t * width : (t + 1) * width], w2[e], w2_s[e], first + t, operand, part)
-                values = planes(pre[e])[:, first : first + group, part]
-                less_one_times(values, values, bank[:].rearrange("p (t c) -> p t c", t=group))
+                values = pre[e][:, first : first + group, part]
+                target = values if into is None else into[:, first : first + group, part]
+                less_one_times(target, values, bank[:].rearrange("p (t c) -> p t c", t=group))
 
-        def times_sigmoid(e, part=ALL_SLOTS):
+        def times_sigmoid(e, part=ALL_SLOTS, source=None):
+            source = pre[e] if source is None else source
             nc.gpsimd.tensor_tensor(
                 da_part[:, 2 * part.start : 2 * part.stop].bitcast(BF16).rearrange("p (c i t) -> p c t i", i=RUN, t=PACK),
-                planes(pre[e])[:, :, part].rearrange("p t (c i) -> p c t i", i=RUN),
-                planes(sigmoids[e][:])[:, :, part].rearrange("p t (c i) -> p c t i", i=RUN),
+                source[:, :, part].rearrange("p t (c i) -> p c t i", i=RUN),
+                sigmoids[e][:, :, part].rearrange("p t (c i) -> p c t i", i=RUN),
                 ALU.mult,
             )
 
@@ -353,11 +355,12 @@ def tile_moe_bdx_mlp_silu_kernel(
         scatter(V, 0, 1, result_1)
         scatter(V, 0, 2, result_2, FIRST_HALF)
         in_turns(0, results)
-        held = emptied(V, 0, 2, da_operand, "v4", SECOND_HALF, into=sigmoids[1][:, 0:C])
+        held = emptied(V, 0, 2, da_operand, "v4", SECOND_HALF, into=sigmoids[1][:, 0, :])
         g_operand, da_operand = quantize_both()
         scatter(V, 0, 2, held, SECOND_HALF)
 
-        times_dh(2, g_operand, ("v0", "v1", "v2", "v3"))
+        apart = planes(after.tile([P, 4 * C], F32, name="apart", offset=0, align_bytes=64)[:])
+        times_dh(2, g_operand, ("v0", "v1", "v2", "v3"), into=apart)
         result_0, result_1 = [emptied(V, 1, m, da_operand, bank) for m, bank in ((0, "v4"), (1, "v0"))]
         results = {m: emptied(S, 1, m, da_operand, bank) for m, bank in ((4, "s0"), (5, "s1"), (3, "s2"))}
         scatter(V, 1, 0, result_0)
@@ -366,7 +369,7 @@ def tile_moe_bdx_mlp_silu_kernel(
         g_last = shared[:, LAP : 2 * C + LAP]
         early, late = slice(0, 3 * C // 4), slice(3 * C // 4, C)
         gate_on_gpsimd(g_last[:, 0 : 3 * C // 2], ungated[3][:, :, early], gates[3][:, early])
-        times_sigmoid(2)
+        times_sigmoid(2, source=apart)
         left_of_2 = after.tile([P, 3 * C], F32, name="left_of_2", offset=0, align_bytes=64)[:]
         emptied(V, 1, 2, da_operand, "v1", FIRST_HALF, into=left_of_2[:, 0:C])
         da_before = da_operand
@@ -394,7 +397,7 @@ def tile_moe_bdx_mlp_silu_kernel(
         scatter(V, 2, 0, result_0)
         scatter(V, 2, 1, result_1, FIRST_HALF)
         in_turns(2, results)
-        held = emptied(V, 2, 1, da_operand, "v4", SECOND_HALF, into=sigmoids[3][:, 0:C])
+        held = emptied(V, 2, 1, da_operand, "v4", SECOND_HALF, into=sigmoids[3][:, 0, :])
         da_before = da_operand
         da_operand = operand_tiles("one")
         quantize(da_part, da_operand)

@@ -392,35 +392,33 @@ def tile_moe_bdx_mlp_silu_kernel(
         result_0 = emptied(V, 2, 0, da_operand, "v1", into=behind_codes[:])
         emptied(V, 1, 2, da_before, "v2", SECOND_HALF, into=left_of_2[:, 0:C])
         left_of_3 = floats("left_of_3", 2 * C, tag="sigmoid0")
-        emptied(S, 2, 3, da_operand, "s2", SECOND_HALF, into=left_of_3[:, 0:C])
+        emptied(S, 2, 3, da_operand, "s2", into=left_of_3[:, 0:C])
         emptied(S, 2, 2, da_operand, "v3", into=left_of_2[:, C : 2 * C])
         scatter(V, 2, 0, result_0)
         scatter(V, 2, 1, result_1, FIRST_HALF)
         in_turns(2, results)
         held = emptied(V, 2, 1, da_operand, "v4", SECOND_HALF, into=sigmoids[3][:, 0, :])
-        da_before = da_operand
         da_operand = operand_tiles("one")
         quantize(da_part, da_operand)
         scatter(V, 2, 1, held, SECOND_HALF)
 
-        results = {m: emptied(S, 3, m, da_operand, bank) for m, bank in ((4, "s1"), (5, "s2"))}
+        scatter(S, 2, 3, left_of_3[:], slice(0, 3 * C // 4))
         result_0, result_1 = [emptied(V, 3, m, da_operand, bank) for m, bank in ((0, "v0"), (1, "v1"))]
+        results = {m: emptied(S, 3, m, da_operand, bank) for m, bank in ((4, "s1"), (5, "s2"))}
         scatter(S, 3, 4, results[4], FIRST_HALF)
-        emptied(S, 3, 3, da_operand, "s0", into=left_of_3[:, C : 2 * C])
+        scatter(S, 3, 5, results[5], FIRST_HALF)
+        emptied(S, 3, 2, da_operand, "v4", into=left_of_2[:, 2 * C : 3 * C])
         scatter(S, 3, 4, results[4], SECOND_HALF)
         store(nc.scalar, 4)
+        emptied(S, 3, 3, da_operand, "s0", into=left_of_3[:, C : 2 * C])
+        scatter(S, 3, 5, results[5], SECOND_HALF)
+        store(nc.scalar, 5)
+        for piece in (slice(3 * C // 4, 3 * C // 2), slice(3 * C // 2, 2 * C)):
+            scatter(S, 2, 3, left_of_3[:], piece)
+        store(nc.scalar, 3)
         scatter(V, 3, 0, result_0)
         store(nc.sync, 0)
-        emptied(V, 3, 2, da_operand, "v4", into=left_of_2[:, 2 * C : 3 * C])
         scatter(V, 3, 1, result_1)
         store(nc.sync, 1)
         scatter(V, 1, 2, left_of_2, slice(C // 2, 3 * C))
         store(nc.sync, 2)
-        emptied(S, 2, 3, da_before, "s1", FIRST_HALF, into=left_of_3[:, 0:C])
-        scatter(S, 3, 5, results[5], FIRST_HALF)
-        scatter(S, 2, 3, left_of_3[:], FIRST_HALF)
-        scatter(S, 3, 5, results[5], SECOND_HALF)
-        store(nc.scalar, 5)
-        for piece in (slice(C // 2, 5 * C // 4), slice(5 * C // 4, 2 * C)):
-            scatter(S, 2, 3, left_of_3[:], piece)
-        store(nc.scalar, 3)

@@ -9,7 +9,7 @@ PACK = 4
 LAST = E - 1
 LIST_ROWS = 16
 QUADRANTS, QUADRANT_ROWS, SCALE_ROWS = 4, 32, 4
-RUN = 4
+RUN = 8
 PAIR = 4
 LAP = 32
 LOWER, UPPER = slice(0, 2), slice(2, 4)

from contextlib import ExitStack

import concourse.mybir as mybir
from concourse.masks import make_identity

K, T, E, C, H, N = 768, 2048, 4, 512, 512, 512
P = 128
PACK = 4
LAST = E - 1
LIST_ROWS = 16
QUADRANTS, QUADRANT_ROWS, SCALE_ROWS = 4, 32, 4
RUN = 8
PAIR = 4
LAP = 32
LOWER, UPPER = slice(0, 2), slice(2, 4)
ALL_SLOTS = slice(0, C)
FIRST_HALF, SECOND_HALF = slice(0, C // 2), slice(C // 2, C)

F32 = mybir.dt.float32
BF16 = mybir.dt.bfloat16
I32 = mybir.dt.int32
U32 = mybir.dt.uint32
U16 = mybir.dt.uint16
U8 = mybir.dt.uint8
FP4X4 = mybir.dt.float4_e2m1fn_x4
FP8X4 = mybir.dt.float8_e5m2_x4
ACT = mybir.ActivationFunctionType
ALU = mybir.AluOpType

FLOPS = 2 * E * C * (N * H + H * K)
BYTES = 4 * (N * T + H * E * C + E * C + K * T) + 2 * E * C + E * (N * H + H * K) * 17 // 32


def tile_moe_bdx_mlp_silu_kernel(
    tc, dyT, a, w2_words, w2_scales, w1_words, w1_scales, gate, offs, out
):
    nc = tc.nc
    with ExitStack() as ctx:
        keep = ctx.enter_context(tc.tile_pool(name="keep", bufs=1))
        head = ctx.enter_context(tc.tile_pool(name="head", bufs=1))
        ring = ctx.enter_context(tc.tile_pool(name="ring", bufs=2))
        after = ctx.enter_context(tc.tile_pool(name="after", bufs=1))
        psum = ctx.enter_context(tc.psum_pool(name="psum", bufs=1))

        def bank_tile(bank):
            return psum.tile([P, C], F32, name="bank", tag=bank)

        def floats(name, width, tag=""):
            return keep.tile([P, width], F32, name=name, tag=tag, align_bytes=64)

        def planes(region):
            return region.rearrange("p (t c) -> p t c", t=PACK)

        offsets = keep.tile([P, E * C // LIST_ROWS], U16, name="offsets")
        dy = [floats(f"dy{t}", T, tag=f"columns{t}") for t in range(PACK)]
        pre_first = [floats(f"pre_first{j}", 2 * C, tag=f"pre_first{j}") for j in range(2)]
        pre_later = planes(floats("pre_later", PACK * LAST * C)[:])
        pre = {e: pre_later[:, :, (e - 1) * C : e * C] for e in range(1, E)}
        sigmoid_first = floats("sigmoid_first", 4 * C, tag="sigmoid0")
        sigmoid_later = planes(floats("sigmoid_later", PACK * LAST * C)[:])
        sigmoids = {e: sigmoid_later[:, :, (e - 1) * C : e * C] for e in range(1, E)}
        w2_raw = keep.tile([P, E, 2 * H], U8, name="w2_raw", align_bytes=64)
        w2_sraw = keep.tile([P, 1, H], U8, name="w2_sraw", tag="scale_rows", align_bytes=64)
        w2_s_late = keep.tile([P, LAST, H], U8, name="w2_s_late", align_bytes=64)
        w1 = keep.tile([P, E, 2 * K], U8, name="w1", align_bytes=64)
        w1_s = keep.tile([P, E, K], U8, name="w1_s", align_bytes=64)
        shared = floats("shared", 8 * C)
        g_part, da_part, both_parts = shared[:, 0 : 2 * C], shared[:, 2 * C : 4 * C], shared[:, 0 : 4 * C]
        g_first = shared[:, C : 3 * C]
        slope_flat = shared[:, 4 * C - LAP : 8 * C - LAP]
        slope = planes(slope_flat)

        nc.vector.memset(w1_s[:].bitcast(I32), 0)
        nc.vector.memset(w2_s_late[:].bitcast(I32), 0)

        dy_rows = dyT.rearrange("(p t) j -> p t j", t=PACK)
        a_rows = a.rearrange("(p t) j -> p t j", t=PACK)

        def load_words(target, source):
            nc.sync.dma_start(out=target[:].bitcast(I32), in_=source.rearrange("e o p n -> p (e o) n").bitcast(I32))

        def load_dy(t):
            nc.sync.dma_start(out=dy[t][:], in_=dy_rows[:, t, :])

        def load_pre_later(t):
            nc.sync.dma_start(out=pre_later[:, t, :], in_=a_rows[:, t, C : E * C])

        def load_pre_first(j):
            target = pre_first[j][:].rearrange("p (t c) -> p t c", t=2)
            nc.sync.dma_start(out=target, in_=a_rows[:, 2 * j : 2 * j + 2, 0:C])

        blocks = E * C // P
        gate_rows = keep.tile([P, P], F32, name="gate_rows")
        gate_columns = keep.tile([P, blocks], F32, name="gate_columns", tag="gathered0", align_bytes=64)
        identity = keep.tile([P, P], F32, name="identity")
        nc.gpsimd.memset(gate_rows[:], 0.0)
        nc.gpsimd.memset(w2_sraw[:].bitcast(I32), 0)
        load_pre_first(0)
        nc.sync.dma_start(out=gate_rows[0:blocks, :], in_=gate[0, :].rearrange("(b c) -> b c", c=P))
        make_identity(nc, identity[:])
        turned = bank_tile("v0")
        nc.tensor.transpose(turned[:, 0:P], gate_rows[:], identity[:])
        nc.vector.tensor_scalar(gate_columns[:], turned[:, 0:blocks], -1.0, None, ALU.mult)

        def spread(e):
            bank = bank_tile(("s2", "v0", "s0", "s1")[e])
            for j in range(C // P):
                b = e * C // P + j
                column = gate_columns[:, b : b + 1].to_broadcast([P, P])
                nc.tensor.transpose(bank[:, j * P : (j + 1) * P], column, identity[:])
            return bank[:]

        gates = {e: floats(f"gates{e}", C, tag=f"gates{e}") for e in (2, 3)}
        for e in (2, 3):
            nc.vector.tensor_copy(gates[e][:], spread(e))
        gate_banks = [spread(e) for e in (0, 1)]
        gates_second = floats("gates_second", C // 2, tag="gates_second")
        nc.vector.tensor_copy(gates_second[:], gate_banks[1][:, SECOND_HALF])

        gathered = [keep.tile([P, PACK, 2 * C], F32, name=f"gathered{j}", tag=f"gathered{j}", align_bytes=64) for j in range(2)]
        ungated = [gathered[e // 2][:, :, (e % 2) * C : (e % 2 + 1) * C] for e in range(E)]

        nc.sync.dma_start(out=offsets[:], in_=offs)
        load_pre_first(1)
        for t in range(PACK):
            load_dy(t)
        load_words(w2_raw, w2_words)
        for q in range(QUADRANTS):
            nc.sync.dma_start(
                out=w2_sraw[QUADRANT_ROWS * q : QUADRANT_ROWS * q + E * SCALE_ROWS, 0, :].bitcast(I32),
                in_=w2_scales[:, 0, SCALE_ROWS * q : SCALE_ROWS * (q + 1), :].bitcast(I32),
            )
        for t in range(PACK):
            load_pre_later(t)
        w1_scale_rows = w1_scales.bitcast(I32).rearrange("e o (q r) n -> r q (e o) n", r=SCALE_ROWS)
        w1_rows = w1_words.bitcast(I32).rearrange("e o p n -> p (e o) n")
        for experts in (slice(0, 1), slice(1, E)):
            for r in range(SCALE_ROWS):
                nc.sync.dma_start(out=w1_s[r:P:QUADRANT_ROWS].bitcast(I32)[:, experts, :], in_=w1_scale_rows[r][:, experts, :])
            nc.sync.dma_start(out=w1[:].bitcast(I32)[:, experts, :], in_=w1_rows[:, experts, :])

        def permute(copy, target, source):
            copy(
                out=target.rearrange("p e (t m) -> p e t m", t=PACK),
                in_=source.rearrange("p e (m t) -> p e t m", t=PACK),
            )

        def slots(e, part=ALL_SLOTS):
            return offsets[:, (e * C + part.start) // LIST_ROWS : (e * C + part.stop) // LIST_ROWS]

        def gather(engine, t, e, part):
            first = (e % 2) * C
            target = gathered[e // 2][:, t, first + part.start : first + part.stop]
            window = dy[t][:].indirect(slots(e, part))
            if engine is nc.vector:
                nc.vector.tensor_copy(target, window)
            else:
                nc.scalar.activation(target, window, ACT.Copy)

        def gate_on_vector(target, source, bank):
            width = bank.shape[1]
            nc.vector.tensor_tensor(
                target.bitcast(BF16).rearrange("p (c i t) -> p c t i", i=PAIR, t=PACK),
                source.rearrange("p t (c i) -> p c t i", i=PAIR),
                bank.rearrange("p (c i) -> p c i", i=PAIR).unsqueeze(2).to_broadcast([P, width // PAIR, PACK, PAIR]),
                ALU.mult,
            )

        def gate_on_gpsimd(target, source, row):
            width = row.shape[1]
            nc.gpsimd.tensor_tensor(
                target.bitcast(BF16).rearrange("p (c i t) -> p c t i", i=RUN, t=PACK),
                source.rearrange("p t (c i) -> p c t i", i=RUN),
                row.rearrange("p (c i) -> p c i", i=RUN).unsqueeze(2).to_broadcast([P, width // RUN, PACK, RUN]),
                ALU.mult,
            )

        def operand_tiles(kind, operands=1, codes=None):
            if codes is None:
                codes = ring.tile([P, operands * C], U32, name=f"codes_{kind}", align_bytes=64)
            return codes, ring.tile([P, operands * C], U8, name=f"scales_{kind}", align_bytes=64)

        def quantize(grouped, operand, part=slice(None)):
            codes, scales = operand
            values = grouped.bitcast(BF16).rearrange("p (c t) -> p c t", t=PACK)[:, part, :].rearrange("p c t -> p (c t)")
            nc.vector.quantize_mx(out=codes[:, part].bitcast(FP8X4), scales=scales[:, part], in_=values)

        def quantize_both():
            codes, scales = operand_tiles("both", operands=2)
            quantize(both_parts, (codes, scales))
            return [(codes[:, j * C : (j + 1) * C], scales[:, j * C : (j + 1) * C]) for j in range(2)]

        def product(target, weight_words, weight_scales, tile, operand, part):
            nc.tensor.matmul_mx(
                out=target,
                lhsT=weight_words[:, 2 * P * tile : 2 * P * (tile + 1)].bitcast(FP4X4),
                lhsT_scale=weight_scales[:, P * tile : P * (tile + 1)],
                rhs=operand[0][:, part].bitcast(FP8X4),
                rhs_scale=operand[1][:, part],
                start=True,
                stop=True,
            )

        def hidden_gradient(e, g_operand):
            banks = []
            for j in range(C // P):
                bank = bank_tile(f"v{j + 1}")
                for t in range(PACK):
                    product(bank[:, t * P : (t + 1) * P], w2[e], w2_s[e], t, g_operand, slice(j * P, (j + 1) * P))
                banks.append(bank)
            return banks

        def through_silu(banks, factor, grouped):
            for j, bank in enumerate(banks):
                nc.vector.tensor_tensor(
                    grouped.bitcast(BF16)[:, j * C : (j + 1) * C].rearrange("p (c i t) -> p c t i", i=PAIR, t=PACK),
                    bank[:].rearrange("p (t c i) -> p c t i", i=PAIR, t=PACK),
                    factor[:, :, j * P : (j + 1) * P].rearrange("p t (c i) -> p c t i", i=PAIR),
                    ALU.mult,
                )

        def sigmoid(target, source):
            nc.scalar.activation(target, source, ACT.Sigmoid)

        def silu(e):
            nc.scalar.activation(pre[e], pre[e], ACT.Silu, scale=-1.0)

        def minus_one(target, source):
            nc.gpsimd.tensor_scalar(target, source, 1.0, -1.0, ALU.mult, ALU.add)

        def less_one_times(target, first, second):
            nc.vector.scalar_tensor_tensor(target, first, 1.0, second, ALU.subtract, ALU.mult)

        def emptied(engine, e, m, da_operand, bank, part=ALL_SLOTS, into=None):
            name = "vector" if engine is nc.vector else "scalar"
            dx = bank_tile(bank)
            product(dx[:, part], w1[:, e, :], w1_s[:, e, :], m, da_operand, part)
            result = into
            if into is None:
                result = ring.tile([P, C], F32, name="result", tag=f"result_{name}", bufs=4)[:]
            if engine is nc.vector:
                nc.vector.tensor_copy(result[:, part], dx[:, part])
            else:
                nc.scalar.copy(out=result[:, part], in_=dx[:, part])
            return result

        window = {}

        def scatter(engine, e, m, result, part=ALL_SLOTS):
            if m not in window:
                window[m] = keep.tile([P, T], F32, name=f"window{m}", tag=f"columns{m}", align_bytes=64)
            if engine is nc.vector:
                nc.vector.tensor_copy(window[m][:].indirect(slots(e, part)), result[:, part])
            else:
                for piece in (FIRST_HALF, SECOND_HALF) if part == ALL_SLOTS else (part,):
                    nc.scalar.activation(window[m][:].indirect(slots(e, piece)), result[:, piece], ACT.Copy)

        def store(queue, m):
            queue.dma_start(out=out[m * P : (m + 1) * P, :], in_=window[m][:])

        def in_turns(e, results):
            for half in (FIRST_HALF, SECOND_HALF):
                for m, result in results.items():
                    scatter(nc.scalar, e, m, result, half)

        halves = (slice(0, 2 * C), slice(2 * C, 4 * C))
        for j, half in enumerate(halves):
            sigmoid(sigmoid_first[:, half], pre_first[j][:])
        for t in range(PACK - 1):
            gather(nc.vector, t, 0, slice(0, 2 * C))
            gather(nc.scalar, t, 2, slice(0, 2 * C))
        for half in (FIRST_HALF, SECOND_HALF):
            gather(nc.vector, PACK - 1, 0, half)
        gather(nc.scalar, PACK - 1, 1, ALL_SLOTS)
        gather(nc.scalar, PACK - 1, 2, slice(0, 2 * C))
        for t in range(PACK):
            sigmoid(sigmoid_later[:, t, :], pre_later[:, t, :])
        for e in range(1, E):
            silu(e)

        work = head.tile([P, 4 * C], F32, name="work", offset=0, align_bytes=64)
        lower, upper = halves
        minus_one(work[:, lower], sigmoid_first[:, lower])
        nc.gpsimd.tensor_tensor(work[:, lower], work[:, lower], pre_first[0][:], ALU.mult)
        minus_one(work[:, lower], work[:, lower])
        nc.gpsimd.tensor_tensor(slope_flat[:, lower], work[:, lower], sigmoid_first[:, lower], ALU.mult)
        minus_one(work[:, upper], sigmoid_first[:, upper])
        nc.gpsimd.tensor_tensor(slope_flat[:, upper], work[:, upper], pre_first[1][:], ALU.mult)

        for j, half in enumerate((FIRST_HALF, SECOND_HALF)):
            gate_on_vector(g_first[:, j * C : (j + 1) * C], ungated[0][:, :, half], gate_banks[0][:, half])
        less_one_times(slope_flat[:, upper], slope_flat[:, upper], sigmoid_first[:, upper])
        permuted = head.tile([P, 5 * H], U8, name="permuted", offset=0, align_bytes=64)
        words = permuted[:, 0 : 4 * H].rearrange("p (e n) -> p e n", e=2)
        packed = permuted[:, 4 * H : 5 * H]
        permute(nc.vector.tensor_copy, packed.rearrange("p (e n) -> p e n", e=1), w2_sraw[:])
        permute(nc.vector.tensor_copy, words.bitcast(U16), w2_raw[:, 0:2, :].bitcast(U16))
        g_operand = operand_tiles("first", codes=head.tile([P, C], U32, name="codes_first", offset=8 * C, align_bytes=64))
        quantize(g_first, g_operand)
        words_late = keep.tile([P, 2, 2 * H], U8, name="words_late", tag="gates_second", align_bytes=64)
        w2 = [words[:, 0, :], words[:, 1, :], words_late[:, 0, :], words_late[:, 1, :]]
        w2_s = [packed] + [w2_s_late[:, e - 1, :] for e in range(1, E)]
        for e in range(1, E):
            for q in range(QUADRANTS):
                top = QUADRANT_ROWS * q
                nc.sync.dma_start(
                    out=w2_s[e][top : top + SCALE_ROWS].bitcast(I32),
                    in_=packed[top + SCALE_ROWS * e : top + SCALE_ROWS * (e + 1)].bitcast(I32),
                )
        gate_on_gpsimd(g_part[:, C : 2 * C], ungated[1][:, :, SECOND_HALF], gates_second[:])
        through_silu(hidden_gradient(0, g_operand), slope, da_part)
        g_second = floats("g_second", C, tag="scale_rows")[:]
        gate_on_vector(g_second, ungated[1][:, :, FIRST_HALF], gate_banks[1][:, FIRST_HALF])
        da_operand = operand_tiles("one")
        for half in (FIRST_HALF, SECOND_HALF):
            quantize(da_part, da_operand, half)
        permute(nc.vector.tensor_copy, words_late[:].bitcast(U16), w2_raw[:, 2:E, :].bitcast(U16))
        g_operand = operand_tiles("second", codes=keep.tile([P, C], U32, name="codes_second", tag="gathered0", align_bytes=64))
        quantize(g_second, g_operand, FIRST_HALF)
        quantize(g_part, g_operand, SECOND_HALF)

        def times_dh(e, operand, banks, part=ALL_SLOTS, into=None):
            width = part.stop - part.start
            group = C // width
            for first, name in zip(range(0, PACK, group), banks):
                bank = bank_tile(name)
                for t in range(group):
                    product(bank[:, t * width : (t + 1) * width], w2[e], w2_s[e], first + t, operand, part)
                values = pre[e][:, first : first + group, part]
                target = values if into is None else into[:, first : first + group, part]
                less_one_times(target, values, bank[:].rearrange("p (t c) -> p t c", t=group))

        def times_sigmoid(e, part=ALL_SLOTS, source=None):
            source = pre[e] if source is None else source
            nc.gpsimd.tensor_tensor(
                da_part[:, 2 * part.start : 2 * part.stop].bitcast(BF16).rearrange("p (c i t) -> p c t i", i=RUN, t=PACK),
                source[:, :, part].rearrange("p t (c i) -> p c t i", i=RUN),
                sigmoids[e][:, :, part].rearrange("p t (c i) -> p c t i", i=RUN),
                ALU.mult,
            )

        V, S = nc.vector, nc.scalar

        result_0 = emptied(V, 0, 0, da_operand, "v0")
        result_3 = emptied(V, 0, 3, da_operand, "v1", into=floats("first_of_3", C)[:])
        scatter(V, 0, 0, result_0)
        results = {m: emptied(S, 0, m, da_operand, bank) for m, bank in ((4, "s1"), (5, "s2"))}
        results[3] = result_3
        gate_on_gpsimd(g_part, ungated[2], gates[2][:])
        for half, banks in ((FIRST_HALF, ("v2", "v3")), (SECOND_HALF, ("v4", "v0"))):
            times_dh(1, g_operand, banks, half)
            times_sigmoid(1, half)
        result_1 = emptied(V, 0, 1, da_operand, "v2")
        result_2 = emptied(V, 0, 2, da_operand, "v3", FIRST_HALF)
        scatter(V, 0, 1, result_1)
        scatter(V, 0, 2, result_2, FIRST_HALF)
        in_turns(0, results)
        held = emptied(V, 0, 2, da_operand, "v4", SECOND_HALF, into=sigmoids[1][:, 0, :])
        g_operand, da_operand = quantize_both()
        scatter(V, 0, 2, held, SECOND_HALF)

        apart = planes(after.tile([P, 4 * C], F32, name="apart", offset=0, align_bytes=64)[:])
        times_dh(2, g_operand, ("v0", "v1", "v2", "v3"), into=apart)
        result_0, result_1 = [emptied(V, 1, m, da_operand, bank) for m, bank in ((0, "v4"), (1, "v0"))]
        results = {m: emptied(S, 1, m, da_operand, bank) for m, bank in ((4, "s0"), (5, "s1"), (3, "s2"))}
        scatter(V, 1, 0, result_0)
        scatter(V, 1, 1, result_1)
        in_turns(1, results)
        g_last = shared[:, LAP : 2 * C + LAP]
        early, late = slice(0, 3 * C // 4), slice(3 * C // 4, C)
        gate_on_gpsimd(g_last[:, 0 : 3 * C // 2], ungated[3][:, :, early], gates[3][:, early])
        times_sigmoid(2, source=apart)
        left_of_2 = after.tile([P, 3 * C], F32, name="left_of_2", offset=0, align_bytes=64)[:]
        emptied(V, 1, 2, da_operand, "v1", FIRST_HALF, into=left_of_2[:, 0:C])
        da_before = da_operand
        g_operand = operand_tiles("last", codes=after.tile([P, C], U32, name="codes_last", offset=12 * C, align_bytes=64))
        quantize(g_last, g_operand, FIRST_HALF)
        da_operand = operand_tiles("one")
        quantize(da_part, da_operand)
        scatter(V, 1, 2, left_of_2, FIRST_HALF)

        gate_on_gpsimd(g_last[:, 3 * C // 2 : 2 * C], ungated[3][:, :, late], gates[3][:, late])
        times_dh(3, g_operand, ("v2", "v3"), FIRST_HALF)
        over_late = gathered[1][:].rearrange("p t c -> p (t c)")[:, 3 * C // 2 : 5 * C // 2]
        result_1 = emptied(V, 2, 1, da_operand, "v0", FIRST_HALF, into=over_late)
        quantize(g_last, g_operand, SECOND_HALF)
        times_sigmoid(3, FIRST_HALF)
        results = {m: emptied(S, 2, m, da_operand, bank) for m, bank in ((4, "s0"), (5, "s1"))}
        times_dh(3, g_operand, ("v2", "v3"), SECOND_HALF)
        times_sigmoid(3, SECOND_HALF)
        behind_codes = after.tile([P, C], F32, name="behind_codes", offset=12 * C, align_bytes=64)
        result_0 = emptied(V, 2, 0, da_operand, "v1", into=behind_codes[:])
        emptied(V, 1, 2, da_before, "v2", SECOND_HALF, into=left_of_2[:, 0:C])
        left_of_3 = floats("left_of_3", 2 * C, tag="sigmoid0")
        emptied(S, 2, 3, da_operand, "s2", into=left_of_3[:, 0:C])
        emptied(S, 2, 2, da_operand, "v3", into=left_of_2[:, C : 2 * C])
        scatter(V, 2, 0, result_0)
        scatter(V, 2, 1, result_1, FIRST_HALF)
        in_turns(2, results)
        held = emptied(V, 2, 1, da_operand, "v4", SECOND_HALF, into=sigmoids[3][:, 0, :])
        da_operand = operand_tiles("one")
        quantize(da_part, da_operand)
        scatter(V, 2, 1, held, SECOND_HALF)

        scatter(S, 2, 3, left_of_3[:], slice(0, 3 * C // 4))
        result_0, result_1 = [emptied(V, 3, m, da_operand, bank) for m, bank in ((0, "v0"), (1, "v1"))]
        results = {m: emptied(S, 3, m, da_operand, bank) for m, bank in ((4, "s1"), (5, "s2"))}
        scatter(S, 3, 4, results[4], FIRST_HALF)
        scatter(S, 3, 5, results[5], FIRST_HALF)
        emptied(S, 3, 2, da_operand, "v4", into=left_of_2[:, 2 * C : 3 * C])
        scatter(S, 3, 4, results[4], SECOND_HALF)
        store(nc.scalar, 4)
        emptied(S, 3, 3, da_operand, "s0", into=left_of_3[:, C : 2 * C])
        scatter(S, 3, 5, results[5], SECOND_HALF)
        store(nc.scalar, 5)
        for piece in (slice(3 * C // 4, 3 * C // 2), slice(3 * C // 2, 2 * C)):
            scatter(S, 2, 3, left_of_3[:], piece)
        store(nc.scalar, 3)
        scatter(V, 3, 0, result_0)
        store(nc.sync, 0)
        scatter(V, 3, 1, result_1)
        store(nc.sync, 1)
        scatter(V, 1, 2, left_of_2, slice(C // 2, 3 * C))
        store(nc.sync, 2)
